import numpy as np
import ml_dtypes


def mxq(x, axis, fmt="e4m3"):
    dtype, down = {"e4m3": (ml_dtypes.float8_e4m3fn, 7), "e5m2": (ml_dtypes.float8_e5m2, 14)}[fmt]
    v = np.moveaxis(np.asarray(x, np.float32).astype(ml_dtypes.bfloat16).astype(np.float64), axis, -1)
    blocks = v.reshape(v.shape[:-1] + (-1, 32))
    amax = np.abs(blocks).max(-1, keepdims=True)
    byte = np.maximum(np.where(amax > 0, np.frexp(amax)[1] - 1 + 127, 0) - down, 1)
    scale = np.exp2(byte - 127.0)
    codes = (blocks / scale).astype(np.float32).astype(dtype).astype(np.float64)
    return np.moveaxis((codes * scale).reshape(v.shape), -1, axis)


WIDE = False


def mx_kscale(k):
    if not WIDE:
        return np.ones(k)
    levels = np.array([10, -10, 5, -5, 0])
    if k % 512:
        return np.exp2(np.random.permutation(np.resize(levels, k // 32))).repeat(32)
    a = np.empty((k // 512, 16))
    for p in range(k // 512):
        a[p, :8] = np.random.permutation(np.resize(levels, 8))
        for g in range(8):
            far = levels[np.abs(levels - a[p, g]) >= 10]
            a[p, g + 8] = far[np.random.randint(len(far))]
    return np.exp2(a.ravel()).repeat(32)


def f64(x):
    return np.asarray(x).astype(np.float64)


def striped(idx):
    return np.tile(idx.reshape(-1, 16).T, (8, 1)).astype(np.uint16)


def unstriped(offs):
    return offs[:16].T.reshape(-1).astype(np.int64)


def silu(v):
    return v / (1.0 + np.exp(-np.maximum(v, -700.0)))


K, T, E, C, N = 1024, 1536, 12, 256, 128


def by_expert(wq, xq):
    return np.concatenate([wq[e].T @ xq[:, e * C:(e + 1) * C] for e in range(E)], axis=1)


def setup_inputs():
    n = np.random.standard_normal
    s = mx_kscale(K)[:, None]
    first = np.random.permutation(np.repeat(np.arange(E), T // E))
    second = (first + 1 + np.random.permutation(np.repeat(np.arange(E - 1), -(-T // (E - 1)))[:T])) % E
    while np.bincount(second, minlength=E).max() != T // E:
        load = np.bincount(second, minlength=E); hi, lo = int(load.argmax()), int(load.argmin())
        t = np.flatnonzero((second == hi) & (first != lo))[0]; second[t] = lo
    slot_token = np.empty(E * C, np.int64); pos = np.empty((2, T), np.int64); fill = np.zeros(E, np.int64)
    place = np.stack([np.random.permutation(C) for _ in range(E)])
    for r, deal in enumerate((first, second)):
        for t in np.random.permutation(T):
            e = deal[t]; j = e * C + place[e, fill[e]]; fill[e] += 1; slot_token[j] = t; pos[r, t] = j
    g = np.random.uniform(0.2, 0.8, T)
    w_slot = np.empty(E * C); w_slot[pos[0]] = g; w_slot[pos[1]] = 1.0 - g
    return {
        "xT": (n((K, T)) * s).astype(np.float32),
        "w": (n((E, K, N)) / np.sqrt(K) / s[None]).astype(np.float32),
        "b": (0.3 * n((N, E))).astype(np.float32),
        "gate": np.tile(w_slot, (K, 1)).astype(np.float32),
        "offs": striped(slot_token),
        "pos1": striped(pos[0]),
        "pos2": striped(pos[1]),
    }


def reference(xT, w, b, gate, offs, pos1, pos2):
    idx = unstriped(offs)
    xq = mxq(f64(gate) * f64(xT)[:, idx], 0, "e4m3")
    y = by_expert(mxq(f64(w), 1, "e4m3"), xq)
    y = silu(y + np.repeat(f64(b), C, axis=1))
    return y[:, unstriped(pos1)] + y[:, unstriped(pos2)]

@@ -1,0 +1,203 @@
+from contextlib import ExitStack
+
+import concourse.mybir as mybir
+
+K, T, E, C, N = 1024, 1536, 12, 256, 128
+S = E * C
+FLOPS = 2 * K * N * S
+BYTES = 4 * (K * T + E * K * N + N * E + S + N * T) + 2 * 128 * (S + 2 * T) // 16
+
+F32 = mybir.dt.float32
+BF16 = mybir.dt.bfloat16
+U32 = mybir.dt.uint32
+U16 = mybir.dt.uint16
+U8 = mybir.dt.uint8
+FP8X4 = mybir.dt.float8_e4m3fn_x4
+MULT = mybir.AluOpType.mult
+ADD = mybir.AluOpType.add
+SILU = mybir.ActivationFunctionType.Silu
+
+P = 128
+PACK = 4
+PASSES = K // (P * PACK)
+PER_COLUMN = 16
+PAIRS = E // 2
+
+CHUNKS = ((1024, 1024, 1024), (1024, 768, 512, 384, 256, 128))
+TOKEN_PIECES = (576, 576, 384)
+GATE_PIECE = 1024
+
+
+def spans(widths):
+    result, start = [], 0
+    for width in widths:
+        result.append((start, start + width))
+        start += width
+    return result
+
+
+def powers_of_two(lo, hi):
+    result = []
+    while lo < hi:
+        width = 1024
+        while width > hi - lo:
+            width //= 2
+        result.append((lo, lo + width))
+        lo += width
+    return result
+
+
+def tile_moe_pre_lin_silu_kernel(tc, xT, w, b, gate, offs, pos1, pos2, out):
+    nc = tc.nc
+    with ExitStack() as ctx:
+        keep = ctx.enter_context(tc.tile_pool(name="keep", bufs=1))
+        ring2 = ctx.enter_context(tc.tile_pool(name="ring2", bufs=2))
+        ring3 = ctx.enter_context(tc.tile_pool(name="ring3", bufs=3))
+        ring4 = ctx.enter_context(tc.tile_pool(name="ring4", bufs=4))
+        psum = ctx.enter_context(tc.psum_pool(name="psum", bufs=6))
+
+        offs_sb = keep.tile([P, S // PER_COLUMN], U16, name="offs_sb")
+        pos1_sb = keep.tile([P, T // PER_COLUMN], U16, name="pos1_sb")
+        pos2_sb = keep.tile([P, T // PER_COLUMN], U16, name="pos2_sb")
+        bias = keep.tile([P, E], F32, name="bias")
+        gate_sb = keep.tile([P, S], F32, name="gate_sb")
+        rows = [[keep.tile([P, T], F32, name="rows%d%d" % (g, j)) for j in range(PACK)] for g in range(PASSES)]
+        x_codes = [keep.tile([P, S], U32, name="x_codes%d" % g, align_bytes=64) for g in range(PASSES)]
+        x_scales = [keep.tile([P, S], U8, name="x_scales%d" % g, align_bytes=64) for g in range(PASSES)]
+        w_codes = keep.tile([P, E * PASSES * N], U32, name="w_codes", align_bytes=64)
+        w_scales = keep.tile([P, E * PASSES * N], U8, name="w_scales", align_bytes=64)
+        y = keep.tile([P, S], F32, name="y")
+
+        x_view = xT.rearrange("(g p j) t -> g j p t", g=PASSES, j=PACK)
+        w_view = w.rearrange("e (g p j) n -> p (e g) (j n)", g=PASSES, j=PACK)
+        w_raw = {}
+        w_grouped = {}
+        gathered = {}
+        grouped = {}
+
+        def load_rows(g, j):
+            nc.sync.dma_start(rows[g][j][:], x_view[g, j])
+
+        def load_gate(i):
+            cols = slice(i * GATE_PIECE, (i + 1) * GATE_PIECE)
+            nc.sync.dma_start(gate_sb[:, cols], gate[0:P, cols])
+
+        def load_w(pair):
+            w_raw[pair] = ring4.tile([P, 2 * PASSES, PACK * N], F32, name="w_raw")
+            nc.sync.dma_start(w_raw[pair][:], w_view[:, 2 * PASSES * pair : 2 * PASSES * (pair + 1), :])
+
+        def round_w(pair):
+            w_grouped[pair] = ring3.tile([P, 2 * PASSES, N * PACK], BF16, name="w_grouped", align_bytes=64)
+            for q in range(2 * PASSES):
+                nc.scalar.copy(
+                    w_grouped[pair][:, q, :].rearrange("p (c i j) -> p c j i", i=4, j=PACK),
+                    w_raw[pair][:, q, :].rearrange("p (j c i) -> p c j i", i=4, j=PACK),
+                )
+
+        def quantize_w(pair):
+            cols = slice(2 * PASSES * N * pair, 2 * PASSES * N * (pair + 1))
+            nc.vector.quantize_mx(
+                out=w_codes[:, cols].bitcast(FP8X4),
+                scales=w_scales[:, cols],
+                in_=w_grouped[pair][:].rearrange("p q c -> p (q c)"),
+            )
+
+        def gather(g, lo, hi):
+            gathered[g, lo] = ring2.tile([P, PACK, hi - lo], F32, name="gathered")
+            for j in range(PACK):
+                nc.vector.tensor_tensor(
+                    gathered[g, lo][:, j, :],
+                    rows[g][j][:].indirect(offs_sb[:, lo // PER_COLUMN : hi // PER_COLUMN]),
+                    gate_sb[:, lo:hi],
+                    MULT,
+                )
+
+        def round_x(g, lo, hi):
+            grouped[g, lo] = ring2.tile([P, (hi - lo) * PACK], BF16, name="grouped", align_bytes=64)
+            nc.scalar.copy(
+                grouped[g, lo][:].rearrange("p (c i j) -> p c j i", i=4, j=PACK),
+                gathered[g, lo][:].rearrange("p j (c i) -> p c j i", i=4),
+            )
+
+        def quantize_x(g, lo, hi):
+            for a, z in powers_of_two(lo, hi):
+                nc.vector.quantize_mx(
+                    out=x_codes[g][:, a:z].bitcast(FP8X4),
+                    scales=x_scales[g][:, a:z],
+                    in_=grouped[g, lo][:, (a - lo) * PACK : (z - lo) * PACK],
+                )
+
+        def experts(lo, hi):
+            a = lo
+            while a < hi:
+                e = a // C
+                z = min(hi, (e + 1) * C)
+                acc = psum.tile([P, z - a], F32, name="acc")
+                for g in range(PASSES):
+                    wc = slice((e * PASSES + g) * N, (e * PASSES + g + 1) * N)
+                    nc.tensor.matmul_mx(
+                        out=acc[:],
+                        lhsT=w_codes[:, wc].bitcast(FP8X4),
+                        lhsT_scale=w_scales[:, wc],
+                        rhs=x_codes[g][:, a:z].bitcast(FP8X4),
+                        rhs_scale=x_scales[g][:, a:z],
+                        start=(g == 0),
+                        stop=(g == PASSES - 1),
+                    )
+                nc.scalar.activation(y[:, a:z], acc[:], SILU, bias=bias[:, e : e + 1])
+                a = z
+
+        nc.sync.dma_start(offs_sb[:], offs)
+        load_rows(0, 0)
+        load_gate(0)
+        for j in range(1, PACK):
+            load_rows(0, j)
+        load_gate(1)
+        load_w(0)
+        load_w(1)
+        load_gate(2)
+        nc.sync.dma_start(bias[:], b)
+        nc.sync.dma_start(pos1_sb[:], pos1)
+        nc.sync.dma_start(pos2_sb[:], pos2)
+        load_w(2)
+        load_w(3)
+        for j in range(PACK):
+            load_rows(1, j)
+
+        steps = [(g, lo, hi) for g in range(PASSES) for lo, hi in spans(CHUNKS[g])]
+        round_pairs = {0: (0, 1), 1: (2, 3), 2: (4, 5)}
+        quantize_pairs = {1: (0,), 2: (1, 2), 3: (3, 4), 4: (5,)}
+        for i, step in enumerate(steps):
+            gather(*step)
+            round_x(*step)
+            if i > 0:
+                quantize_x(*steps[i - 1])
+            for pair in quantize_pairs.get(i, ()):
+                quantize_w(pair)
+            for pair in round_pairs.get(i, ()):
+                round_w(pair)
+                if pair + 4 < PAIRS:
+                    load_w(pair + 4)
+            if i > 0 and steps[i - 1][0] == PASSES - 1:
+                experts(*steps[i - 1][1:])
+        quantize_x(*steps[-1])
+        experts(*steps[-1][1:])
+
+        pieces = spans(TOKEN_PIECES)
+        first, second = {}, {}
+
+        def fetch(dest, name, positions, lo, hi):
+            dest[lo] = ring2.tile([P, hi - lo], F32, name=name)
+            nc.vector.tensor_copy(dest[lo][:], y[:].indirect(positions[:, lo // PER_COLUMN : hi // PER_COLUMN]))
+
+        def combine(lo, hi):
+            total = ring2.tile([P, hi - lo], F32, name="total")
+            nc.vector.tensor_tensor(total[:], first[lo][:], second[lo][:], ADD)
+            nc.sync.dma_start(out[:, lo:hi], total[:])
+
+        for i, piece in enumerate(pieces):
+            fetch(first, "first", pos1_sb, *piece)
+            if i > 0:
+                combine(*pieces[i - 1])
+            fetch(second, "second", pos2_sb, *piece)
+        combine(*pieces[-1])

@@ -25,7 +25,7 @@ PAIRS = E // 2
 
 CHUNKS = ((1024, 1024, 1024), (1024, 768, 512, 384, 256, 128))
 TOKEN_PIECES = (576, 576, 384)
-GATE_PIECE = 1024
+GATE_PIECES = (384, 640, 1024, 1024)
 
 
 def spans(widths):
@@ -54,7 +54,7 @@ def tile_moe_pre_lin_silu_kernel(tc, xT, w, b, gate, offs, pos1, pos2, out):
         ring2 = ctx.enter_context(tc.tile_pool(name="ring2", bufs=2))
         ring3 = ctx.enter_context(tc.tile_pool(name="ring3", bufs=3))
         ring4 = ctx.enter_context(tc.tile_pool(name="ring4", bufs=4))
-        psum = ctx.enter_context(tc.psum_pool(name="psum", bufs=6))
+        psum = ctx.enter_context(tc.psum_pool(name="psum", bufs=8))
 
         offs_sb = keep.tile([P, S // PER_COLUMN], U16, name="offs_sb")
         pos1_sb = keep.tile([P, T // PER_COLUMN], U16, name="pos1_sb")
@@ -79,7 +79,7 @@ def tile_moe_pre_lin_silu_kernel(tc, xT, w, b, gate, offs, pos1, pos2, out):
             nc.sync.dma_start(rows[g][j][:], x_view[g, j])
 
         def load_gate(i):
-            cols = slice(i * GATE_PIECE, (i + 1) * GATE_PIECE)
+            cols = slice(*spans(GATE_PIECES)[i])
             nc.sync.dma_start(gate_sb[:, cols], gate[0:P, cols])
 
         def load_w(pair):
@@ -94,23 +94,26 @@ def tile_moe_pre_lin_silu_kernel(tc, xT, w, b, gate, offs, pos1, pos2, out):
                     w_raw[pair][:, q, :].rearrange("p (j c i) -> p c j i", i=4, j=PACK),
                 )
 
-        def quantize_w(pair):
-            cols = slice(2 * PASSES * N * pair, 2 * PASSES * N * (pair + 1))
+        def quantize_w(e0, e1):
+            cols = slice(PASSES * N * e0, PASSES * N * e1)
+            pair = e0 // 2
             nc.vector.quantize_mx(
                 out=w_codes[:, cols].bitcast(FP8X4),
                 scales=w_scales[:, cols],
-                in_=w_grouped[pair][:].rearrange("p q c -> p (q c)"),
+                in_=w_grouped[pair][:, PASSES * (e0 - 2 * pair) : PASSES * (e1 - 2 * pair), :].rearrange("p q c -> p (q c)"),
             )
 
         def gather(g, lo, hi):
             gathered[g, lo] = ring2.tile([P, PACK, hi - lo], F32, name="gathered")
             for j in range(PACK):
-                nc.vector.tensor_tensor(
-                    gathered[g, lo][:, j, :],
-                    rows[g][j][:].indirect(offs_sb[:, lo // PER_COLUMN : hi // PER_COLUMN]),
-                    gate_sb[:, lo:hi],
-                    MULT,
-                )
+                cuts = spans(GATE_PIECES[:2]) if (g, lo, j) == (0, 0, 0) else [(lo, hi)]
+                for a, z in cuts:
+                    nc.vector.tensor_tensor(
+                        gathered[g, lo][:, j, a - lo : z - lo],
+                        rows[g][j][:].indirect(offs_sb[:, a // PER_COLUMN : z // PER_COLUMN]),
+                        gate_sb[:, a:z],
+                        MULT,
+                    )
 
         def round_x(g, lo, hi):
             grouped[g, lo] = ring2.tile([P, (hi - lo) * PACK], BF16, name="grouped", align_bytes=64)
@@ -147,15 +150,21 @@ def tile_moe_pre_lin_silu_kernel(tc, xT, w, b, gate, offs, pos1, pos2, out):
                 nc.scalar.activation(y[:, a:z], acc[:], SILU, bias=bias[:, e : e + 1])
                 a = z
 
-        nc.sync.dma_start(offs_sb[:], offs)
+        warm = keep.tile([P, 1], F32, name="warm")
+        warm_out = keep.tile([P, 1], F32, name="warm_out")
+        nc.vector.memset(warm[:], 0.0)
+        nc.scalar.activation(warm_out[:], warm[:], SILU)
+
         load_rows(0, 0)
+        nc.sync.dma_start(offs_sb[:], offs)
         load_gate(0)
+        load_gate(1)
         for j in range(1, PACK):
             load_rows(0, j)
-        load_gate(1)
+        load_gate(2)
         load_w(0)
         load_w(1)
-        load_gate(2)
+        load_gate(3)
         nc.sync.dma_start(bias[:], b)
         nc.sync.dma_start(pos1_sb[:], pos1)
         nc.sync.dma_start(pos2_sb[:], pos2)
@@ -166,14 +175,14 @@ def tile_moe_pre_lin_silu_kernel(tc, xT, w, b, gate, offs, pos1, pos2, out):
 
         steps = [(g, lo, hi) for g in range(PASSES) for lo, hi in spans(CHUNKS[g])]
         round_pairs = {0: (0, 1), 1: (2, 3), 2: (4, 5)}
-        quantize_pairs = {1: (0,), 2: (1, 2), 3: (3, 4), 4: (5,)}
+        quantize_experts = {1: ((0, 2),), 2: ((2, 4), (4, 6)), 3: ((6, 8), (8, 10)), 4: ((10, 11),), 8: ((11, 12),)}
         for i, step in enumerate(steps):
             gather(*step)
             round_x(*step)
             if i > 0:
                 quantize_x(*steps[i - 1])
-            for pair in quantize_pairs.get(i, ()):
-                quantize_w(pair)
+            for e0, e1 in quantize_experts.get(i, ()):
+                quantize_w(e0, e1)
             for pair in round_pairs.get(i, ()):
                 round_w(pair)
                 if pair + 4 < PAIRS:
@@ -191,13 +200,13 @@ def tile_moe_pre_lin_silu_kernel(tc, xT, w, b, gate, offs, pos1, pos2, out):
             nc.vector.tensor_copy(dest[lo][:], y[:].indirect(positions[:, lo // PER_COLUMN : hi // PER_COLUMN]))
 
         def combine(lo, hi):
-            total = ring2.tile([P, hi - lo], F32, name="total")
+            total = ring3.tile([P, hi - lo], F32, name="total")
             nc.vector.tensor_tensor(total[:], first[lo][:], second[lo][:], ADD)
             nc.sync.dma_start(out[:, lo:hi], total[:])
 
         for i, piece in enumerate(pieces):
             fetch(first, "first", pos1_sb, *piece)
+            fetch(second, "second", pos2_sb, *piece)
             if i > 0:
                 combine(*pieces[i - 1])
-            fetch(second, "second", pos2_sb, *piece)
         combine(*pieces[-1])

@@ -196,17 +196,16 @@ def tile_moe_pre_lin_silu_kernel(tc, xT, w, b, gate, offs, pos1, pos2, out):
         first, second = {}, {}
 
         def fetch(dest, name, positions, lo, hi):
-            dest[lo] = ring2.tile([P, hi - lo], F32, name=name)
+            dest[lo] = ring3.tile([P, hi - lo], F32, name=name)
             nc.vector.tensor_copy(dest[lo][:], y[:].indirect(positions[:, lo // PER_COLUMN : hi // PER_COLUMN]))
 
         def combine(lo, hi):
             total = ring3.tile([P, hi - lo], F32, name="total")
-            nc.vector.tensor_tensor(total[:], first[lo][:], second[lo][:], ADD)
+            engine = nc.vector if hi == T else nc.gpsimd
+            engine.tensor_tensor(total[:], first[lo][:], second[lo][:], ADD)
             nc.sync.dma_start(out[:, lo:hi], total[:])
 
         for i, piece in enumerate(pieces):
             fetch(first, "first", pos1_sb, *piece)
             fetch(second, "second", pos2_sb, *piece)
-            if i > 0:
-                combine(*pieces[i - 1])
-        combine(*pieces[-1])
+            combine(*piece)

@@ -23,9 +23,10 @@ PASSES = K // (P * PACK)
 PER_COLUMN = 16
 PAIRS = E // 2
 
-CHUNKS = ((1024, 1024, 1024), (1024, 768, 512, 384, 256, 128))
-TOKEN_PIECES = (576, 576, 384)
-GATE_PIECES = (384, 640, 1024, 1024)
+CHUNKS = ((1280, 1024, 768), (1024, 768, 512, 384, 256, 128))
+FIRST_PIECES = (768, 768)
+TOKEN_PIECES = (768, 384, 256, 128)
+GATE_PIECES = (128, 256, 896, 1024, 768)
 
 
 def spans(widths):
@@ -103,10 +104,11 @@ def tile_moe_pre_lin_silu_kernel(tc, xT, w, b, gate, offs, pos1, pos2, out):
                 in_=w_grouped[pair][:, PASSES * (e0 - 2 * pair) : PASSES * (e1 - 2 * pair), :].rearrange("p q c -> p (q c)"),
             )
 
-        def gather(g, lo, hi):
-            gathered[g, lo] = ring2.tile([P, PACK, hi - lo], F32, name="gathered")
-            for j in range(PACK):
-                cuts = spans(GATE_PIECES[:2]) if (g, lo, j) == (0, 0, 0) else [(lo, hi)]
+        def gather(g, lo, hi, planes):
+            if (g, lo) not in gathered:
+                gathered[g, lo] = ring2.tile([P, PACK, hi - lo], F32, name="gathered")
+            for j in planes:
+                cuts = spans(GATE_PIECES[:3]) if (g, lo, j) == (0, 0, 0) else [(lo, hi)]
                 for a, z in cuts:
                     nc.vector.tensor_tensor(
                         gathered[g, lo][:, j, a - lo : z - lo],
@@ -150,21 +152,16 @@ def tile_moe_pre_lin_silu_kernel(tc, xT, w, b, gate, offs, pos1, pos2, out):
                 nc.scalar.activation(y[:, a:z], acc[:], SILU, bias=bias[:, e : e + 1])
                 a = z
 
-        warm = keep.tile([P, 1], F32, name="warm")
-        warm_out = keep.tile([P, 1], F32, name="warm_out")
-        nc.vector.memset(warm[:], 0.0)
-        nc.scalar.activation(warm_out[:], warm[:], SILU)
-
         load_rows(0, 0)
         nc.sync.dma_start(offs_sb[:], offs)
-        load_gate(0)
-        load_gate(1)
+        for i in range(3):
+            load_gate(i)
         for j in range(1, PACK):
             load_rows(0, j)
-        load_gate(2)
+        load_gate(3)
         load_w(0)
         load_w(1)
-        load_gate(3)
+        load_gate(4)
         nc.sync.dma_start(bias[:], b)
         nc.sync.dma_start(pos1_sb[:], pos1)
         nc.sync.dma_start(pos2_sb[:], pos2)
@@ -177,7 +174,7 @@ def tile_moe_pre_lin_silu_kernel(tc, xT, w, b, gate, offs, pos1, pos2, out):
         round_pairs = {0: (0, 1), 1: (2, 3), 2: (4, 5)}
         quantize_experts = {1: ((0, 2),), 2: ((2, 4), (4, 6)), 3: ((6, 8), (8, 10)), 4: ((10, 11),), 8: ((11, 12),)}
         for i, step in enumerate(steps):
-            gather(*step)
+            gather(*step, range(PACK))
             round_x(*step)
             if i > 0:
                 quantize_x(*steps[i - 1])
@@ -192,20 +189,15 @@ def tile_moe_pre_lin_silu_kernel(tc, xT, w, b, gate, offs, pos1, pos2, out):
         quantize_x(*steps[-1])
         experts(*steps[-1][1:])
 
-        pieces = spans(TOKEN_PIECES)
-        first, second = {}, {}
-
-        def fetch(dest, name, positions, lo, hi):
-            dest[lo] = ring3.tile([P, hi - lo], F32, name=name)
-            nc.vector.tensor_copy(dest[lo][:], y[:].indirect(positions[:, lo // PER_COLUMN : hi // PER_COLUMN]))
-
-        def combine(lo, hi):
-            total = ring3.tile([P, hi - lo], F32, name="total")
-            engine = nc.vector if hi == T else nc.gpsimd
-            engine.tensor_tensor(total[:], first[lo][:], second[lo][:], ADD)
-            nc.sync.dma_start(out[:, lo:hi], total[:])
-
-        for i, piece in enumerate(pieces):
-            fetch(first, "first", pos1_sb, *piece)
-            fetch(second, "second", pos2_sb, *piece)
-            combine(*piece)
+        first = keep.tile([P, T], F32, name="first")
+        total = keep.tile([P, T], F32, name="total")
+        for lo, hi in spans(FIRST_PIECES):
+            nc.vector.tensor_copy(first[:, lo:hi], y[:].indirect(pos1_sb[:, lo // PER_COLUMN : hi // PER_COLUMN]))
+        for lo, hi in spans(TOKEN_PIECES):
+            nc.vector.tensor_tensor(
+                total[:, lo:hi],
+                y[:].indirect(pos2_sb[:, lo // PER_COLUMN : hi // PER_COLUMN]),
+                first[:, lo:hi],
+                ADD,
+            )
+            nc.sync.dma_start(out[:, lo:hi], total[:, lo:hi])

@@ -23,10 +23,11 @@ PASSES = K // (P * PACK)
 PER_COLUMN = 16
 PAIRS = E // 2
 
-CHUNKS = ((1280, 1024, 768), (1024, 768, 512, 384, 256, 128))
+CHUNKS = ((1536, 1536), (1408, 768, 512, 256, 128))
+SPARE = 16
 FIRST_PIECES = (768, 768)
-TOKEN_PIECES = (768, 384, 256, 128)
-GATE_PIECES = (128, 256, 896, 1024, 768)
+TOKEN_PIECES = (768, 512, 256)
+GATE_PIECES = (192, 448, 896, 1536)
 
 
 def spans(widths):
@@ -54,7 +55,6 @@ def tile_moe_pre_lin_silu_kernel(tc, xT, w, b, gate, offs, pos1, pos2, out):
         keep = ctx.enter_context(tc.tile_pool(name="keep", bufs=1))
         ring2 = ctx.enter_context(tc.tile_pool(name="ring2", bufs=2))
         ring3 = ctx.enter_context(tc.tile_pool(name="ring3", bufs=3))
-        ring4 = ctx.enter_context(tc.tile_pool(name="ring4", bufs=4))
         psum = ctx.enter_context(tc.psum_pool(name="psum", bufs=8))
 
         offs_sb = keep.tile([P, S // PER_COLUMN], U16, name="offs_sb")
@@ -62,7 +62,7 @@ def tile_moe_pre_lin_silu_kernel(tc, xT, w, b, gate, offs, pos1, pos2, out):
         pos2_sb = keep.tile([P, T // PER_COLUMN], U16, name="pos2_sb")
         bias = keep.tile([P, E], F32, name="bias")
         gate_sb = keep.tile([P, S], F32, name="gate_sb")
-        rows = [[keep.tile([P, T], F32, name="rows%d%d" % (g, j)) for j in range(PACK)] for g in range(PASSES)]
+        rows = [[keep.tile([P, T + (SPARE if g == 0 else 0)], F32, name="rows%d%d" % (g, j)) for j in range(PACK)] for g in range(PASSES)]
         x_codes = [keep.tile([P, S], U32, name="x_codes%d" % g, align_bytes=64) for g in range(PASSES)]
         x_scales = [keep.tile([P, S], U8, name="x_scales%d" % g, align_bytes=64) for g in range(PASSES)]
         w_codes = keep.tile([P, E * PASSES * N], U32, name="w_codes", align_bytes=64)
@@ -77,31 +77,32 @@ def tile_moe_pre_lin_silu_kernel(tc, xT, w, b, gate, offs, pos1, pos2, out):
         grouped = {}
 
         def load_rows(g, j):
-            nc.sync.dma_start(rows[g][j][:], x_view[g, j])
+            nc.sync.dma_start(rows[g][j][:, :T], x_view[g, j])
 
         def load_gate(i):
             cols = slice(*spans(GATE_PIECES)[i])
             nc.sync.dma_start(gate_sb[:, cols], gate[0:P, cols])
 
         def load_w(pair):
-            w_raw[pair] = ring4.tile([P, 2 * PASSES, PACK * N], F32, name="w_raw")
+            w_raw[pair] = ring3.tile([P, 2 * PASSES, PACK * N], F32, name="w_raw")
             nc.sync.dma_start(w_raw[pair][:], w_view[:, 2 * PASSES * pair : 2 * PASSES * (pair + 1), :])
 
         def round_w(pair):
-            w_grouped[pair] = ring3.tile([P, 2 * PASSES, N * PACK], BF16, name="w_grouped", align_bytes=64)
+            quad, half = divmod(pair, 2)
+            if half == 0:
+                w_grouped[quad] = ring2.tile([P, 4 * PASSES, N * PACK], BF16, name="w_grouped", align_bytes=64)
             for q in range(2 * PASSES):
                 nc.scalar.copy(
-                    w_grouped[pair][:, q, :].rearrange("p (c i j) -> p c j i", i=4, j=PACK),
+                    w_grouped[quad][:, 2 * PASSES * half + q, :].rearrange("p (c i j) -> p c j i", i=4, j=PACK),
                     w_raw[pair][:, q, :].rearrange("p (j c i) -> p c j i", i=4, j=PACK),
                 )
 
-        def quantize_w(e0, e1):
-            cols = slice(PASSES * N * e0, PASSES * N * e1)
-            pair = e0 // 2
+        def quantize_w(quad):
+            cols = slice(4 * PASSES * N * quad, 4 * PASSES * N * (quad + 1))
             nc.vector.quantize_mx(
                 out=w_codes[:, cols].bitcast(FP8X4),
                 scales=w_scales[:, cols],
-                in_=w_grouped[pair][:, PASSES * (e0 - 2 * pair) : PASSES * (e1 - 2 * pair), :].rearrange("p q c -> p (q c)"),
+                in_=w_grouped[quad][:].rearrange("p q c -> p (q c)"),
             )
 
         def gather(g, lo, hi, planes):
@@ -152,45 +153,50 @@ def tile_moe_pre_lin_silu_kernel(tc, xT, w, b, gate, offs, pos1, pos2, out):
                 nc.scalar.activation(y[:, a:z], acc[:], SILU, bias=bias[:, e : e + 1])
                 a = z
 
+        for j in range(PACK):
+            nc.gpsimd.memset(rows[0][j][:, T:], 0.0)
+
         load_rows(0, 0)
         nc.sync.dma_start(offs_sb[:], offs)
         for i in range(3):
             load_gate(i)
-        for j in range(1, PACK):
-            load_rows(0, j)
-        load_gate(3)
+        load_rows(0, 1)
+        load_rows(0, 2)
         load_w(0)
+        load_rows(0, 3)
+        load_gate(3)
         load_w(1)
-        load_gate(4)
+        load_w(2)
         nc.sync.dma_start(bias[:], b)
         nc.sync.dma_start(pos1_sb[:], pos1)
         nc.sync.dma_start(pos2_sb[:], pos2)
-        load_w(2)
-        load_w(3)
         for j in range(PACK):
             load_rows(1, j)
 
+        def round_pair(pair):
+            round_w(pair)
+            if pair + 3 < PAIRS:
+                load_w(pair + 3)
+            if pair % 2 == 1:
+                quantize_w(pair // 2)
+
         steps = [(g, lo, hi) for g in range(PASSES) for lo, hi in spans(CHUNKS[g])]
-        round_pairs = {0: (0, 1), 1: (2, 3), 2: (4, 5)}
-        quantize_experts = {1: ((0, 2),), 2: ((2, 4), (4, 6)), 3: ((6, 8), (8, 10)), 4: ((10, 11),), 8: ((11, 12),)}
+        round_pair(0)
+        round_pairs = {0: (1, 2), 1: (3, 4, 5)}
         for i, step in enumerate(steps):
             gather(*step, range(PACK))
             round_x(*step)
             if i > 0:
                 quantize_x(*steps[i - 1])
-            for e0, e1 in quantize_experts.get(i, ()):
-                quantize_w(e0, e1)
             for pair in round_pairs.get(i, ()):
-                round_w(pair)
-                if pair + 4 < PAIRS:
-                    load_w(pair + 4)
+                round_pair(pair)
             if i > 0 and steps[i - 1][0] == PASSES - 1:
                 experts(*steps[i - 1][1:])
         quantize_x(*steps[-1])
         experts(*steps[-1][1:])
 
-        first = keep.tile([P, T], F32, name="first")
-        total = keep.tile([P, T], F32, name="total")
+        first = keep.tile([P, T], F32, name="rows00")
+        total = keep.tile([P, T], F32, name="rows01")
         for lo, hi in spans(FIRST_PIECES):
             nc.vector.tensor_copy(first[:, lo:hi], y[:].indirect(pos1_sb[:, lo // PER_COLUMN : hi // PER_COLUMN]))
         for lo, hi in spans(TOKEN_PIECES):

@@ -21,12 +21,13 @@ P = 128
 PACK = 4
 PASSES = K // (P * PACK)
 PER_COLUMN = 16
-PAIRS = E // 2
+QUAD = 4
+W_BUFS = 6
 
-CHUNKS = ((1536, 1536), (1408, 768, 512, 256, 128))
+CHUNKS = ((1536, 1536), (1024, 768, 512, 384, 256, 128))
 SPARE = 16
 FIRST_PIECES = (768, 768)
-TOKEN_PIECES = (768, 512, 256)
+TOKEN_PIECES = (768, 384, 256, 128)
 GATE_PIECES = (192, 448, 896, 1536)
 
 
@@ -54,7 +55,7 @@ def tile_moe_pre_lin_silu_kernel(tc, xT, w, b, gate, offs, pos1, pos2, out):
     with ExitStack() as ctx:
         keep = ctx.enter_context(tc.tile_pool(name="keep", bufs=1))
         ring2 = ctx.enter_context(tc.tile_pool(name="ring2", bufs=2))
-        ring3 = ctx.enter_context(tc.tile_pool(name="ring3", bufs=3))
+        ring6 = ctx.enter_context(tc.tile_pool(name="ring6", bufs=6))
         psum = ctx.enter_context(tc.psum_pool(name="psum", bufs=8))
 
         offs_sb = keep.tile([P, S // PER_COLUMN], U16, name="offs_sb")
@@ -83,19 +84,23 @@ def tile_moe_pre_lin_silu_kernel(tc, xT, w, b, gate, offs, pos1, pos2, out):
             cols = slice(*spans(GATE_PIECES)[i])
             nc.sync.dma_start(gate_sb[:, cols], gate[0:P, cols])
 
-        def load_w(pair):
-            w_raw[pair] = ring3.tile([P, 2 * PASSES, PACK * N], F32, name="w_raw")
-            nc.sync.dma_start(w_raw[pair][:], w_view[:, 2 * PASSES * pair : 2 * PASSES * (pair + 1), :])
+        def load_w(e):
+            w_raw[e] = ring6.tile([P, PASSES, PACK * N], F32, name="w_raw")
+            nc.sync.dma_start(w_raw[e][:], w_view[:, PASSES * e : PASSES * (e + 1), :])
 
-        def round_w(pair):
-            quad, half = divmod(pair, 2)
-            if half == 0:
-                w_grouped[quad] = ring2.tile([P, 4 * PASSES, N * PACK], BF16, name="w_grouped", align_bytes=64)
-            for q in range(2 * PASSES):
+        def round_w(e):
+            quad, place = divmod(e, QUAD)
+            if place == 0:
+                w_grouped[quad] = ring2.tile([P, QUAD * PASSES, N * PACK], BF16, name="w_grouped", align_bytes=64)
+            for g in range(PASSES):
                 nc.scalar.copy(
-                    w_grouped[quad][:, 2 * PASSES * half + q, :].rearrange("p (c i j) -> p c j i", i=4, j=PACK),
-                    w_raw[pair][:, q, :].rearrange("p (j c i) -> p c j i", i=4, j=PACK),
+                    w_grouped[quad][:, PASSES * place + g, :].rearrange("p (c i j) -> p c j i", i=4, j=PACK),
+                    w_raw[e][:, g, :].rearrange("p (j c i) -> p c j i", i=4, j=PACK),
                 )
+            if e + W_BUFS < E:
+                load_w(e + W_BUFS)
+            if place == QUAD - 1:
+                quantize_w(quad)
 
         def quantize_w(quad):
             cols = slice(4 * PASSES * N * quad, 4 * PASSES * N * (quad + 1))
@@ -156,6 +161,11 @@ def tile_moe_pre_lin_silu_kernel(tc, xT, w, b, gate, offs, pos1, pos2, out):
         for j in range(PACK):
             nc.gpsimd.memset(rows[0][j][:, T:], 0.0)
 
+        warm = keep.tile([P, 1], F32, name="warm")
+        warm_out = keep.tile([P, 1], F32, name="warm_out")
+        nc.gpsimd.memset(warm[:], 0.0)
+        nc.scalar.activation(warm_out[:], warm[:], SILU)
+
         load_rows(0, 0)
         nc.sync.dma_start(offs_sb[:], offs)
         for i in range(3):
@@ -163,33 +173,30 @@ def tile_moe_pre_lin_silu_kernel(tc, xT, w, b, gate, offs, pos1, pos2, out):
         load_rows(0, 1)
         load_rows(0, 2)
         load_w(0)
-        load_rows(0, 3)
-        load_gate(3)
         load_w(1)
+        load_rows(0, 3)
         load_w(2)
+        load_w(3)
+        load_gate(3)
+        load_w(4)
+        load_w(5)
         nc.sync.dma_start(bias[:], b)
         nc.sync.dma_start(pos1_sb[:], pos1)
         nc.sync.dma_start(pos2_sb[:], pos2)
         for j in range(PACK):
             load_rows(1, j)
 
-        def round_pair(pair):
-            round_w(pair)
-            if pair + 3 < PAIRS:
-                load_w(pair + 3)
-            if pair % 2 == 1:
-                quantize_w(pair // 2)
-
         steps = [(g, lo, hi) for g in range(PASSES) for lo, hi in spans(CHUNKS[g])]
-        round_pair(0)
-        round_pairs = {0: (1, 2), 1: (3, 4, 5)}
+        for e in range(QUAD):
+            round_w(e)
+        round_experts = {0: range(4, 10), 1: range(10, 12)}
         for i, step in enumerate(steps):
             gather(*step, range(PACK))
             round_x(*step)
             if i > 0:
                 quantize_x(*steps[i - 1])
-            for pair in round_pairs.get(i, ()):
-                round_pair(pair)
+            for e in round_experts.get(i, ()):
+                round_w(e)
             if i > 0 and steps[i - 1][0] == PASSES - 1:
                 experts(*steps[i - 1][1:])
         quantize_x(*steps[-1])

@@ -23,6 +23,7 @@ PASSES = K // (P * PACK)
 PER_COLUMN = 16
 QUAD = 4
 W_BUFS = 6
+W_CALLS = {3: 0, 7: 4, 9: 8, 10: 10}
 
 CHUNKS = ((1536, 1536), (1024, 768, 512, 384, 256, 128))
 SPARE = 16
@@ -63,10 +64,11 @@ def tile_moe_pre_lin_silu_kernel(tc, xT, w, b, gate, offs, pos1, pos2, out):
         pos2_sb = keep.tile([P, T // PER_COLUMN], U16, name="pos2_sb")
         bias = keep.tile([P, E], F32, name="bias")
         gate_sb = keep.tile([P, S], F32, name="gate_sb")
-        rows = [[keep.tile([P, T + (SPARE if g == 0 else 0)], F32, name="rows%d%d" % (g, j)) for j in range(PACK)] for g in range(PASSES)]
+        rows = [[keep.tile([P, T + (SPARE if g == 0 else 0)], F32, name="rows%d%d" % (g, j), align_bytes=64) for j in range(PACK)] for g in range(PASSES)]
         x_codes = [keep.tile([P, S], U32, name="x_codes%d" % g, align_bytes=64) for g in range(PASSES)]
         x_scales = [keep.tile([P, S], U8, name="x_scales%d" % g, align_bytes=64) for g in range(PASSES)]
-        w_codes = keep.tile([P, E * PASSES * N], U32, name="w_codes", align_bytes=64)
+        w_codes = keep.tile([P, (E - 1) * PASSES * N], U32, name="w_codes", align_bytes=64)
+        last_codes = []
         w_scales = keep.tile([P, E * PASSES * N], U8, name="w_scales", align_bytes=64)
         y = keep.tile([P, S], F32, name="y")
 
@@ -99,15 +101,20 @@ def tile_moe_pre_lin_silu_kernel(tc, xT, w, b, gate, offs, pos1, pos2, out):
                 )
             if e + W_BUFS < E:
                 load_w(e + W_BUFS)
-            if place == QUAD - 1:
-                quantize_w(quad)
+            if e in W_CALLS:
+                quantize_w(W_CALLS[e], e + 1)
 
-        def quantize_w(quad):
-            cols = slice(4 * PASSES * N * quad, 4 * PASSES * N * (quad + 1))
+        def codes_of(e0, e1):
+            if e0 == E - 1:
+                return last_codes[0][:]
+            return w_codes[:, PASSES * N * e0 : PASSES * N * e1]
+
+        def quantize_w(e0, e1):
+            quad = e0 // QUAD
             nc.vector.quantize_mx(
-                out=w_codes[:, cols].bitcast(FP8X4),
-                scales=w_scales[:, cols],
-                in_=w_grouped[quad][:].rearrange("p q c -> p (q c)"),
+                out=codes_of(e0, e1).bitcast(FP8X4),
+                scales=w_scales[:, PASSES * N * e0 : PASSES * N * e1],
+                in_=w_grouped[quad][:, PASSES * (e0 - QUAD * quad) : PASSES * (e1 - QUAD * quad), :].rearrange("p q c -> p (q c)"),
             )
 
         def gather(g, lo, hi, planes):
@@ -148,7 +155,7 @@ def tile_moe_pre_lin_silu_kernel(tc, xT, w, b, gate, offs, pos1, pos2, out):
                     wc = slice((e * PASSES + g) * N, (e * PASSES + g + 1) * N)
                     nc.tensor.matmul_mx(
                         out=acc[:],
-                        lhsT=w_codes[:, wc].bitcast(FP8X4),
+                        lhsT=codes_of(e, e + 1)[:, g * N : (g + 1) * N].bitcast(FP8X4),
                         lhsT_scale=w_scales[:, wc],
                         rhs=x_codes[g][:, a:z].bitcast(FP8X4),
                         rhs_scale=x_scales[g][:, a:z],
@@ -160,11 +167,6 @@ def tile_moe_pre_lin_silu_kernel(tc, xT, w, b, gate, offs, pos1, pos2, out):
 
         for j in range(PACK):
             nc.gpsimd.memset(rows[0][j][:, T:], 0.0)
-
-        warm = keep.tile([P, 1], F32, name="warm")
-        warm_out = keep.tile([P, 1], F32, name="warm_out")
-        nc.gpsimd.memset(warm[:], 0.0)
-        nc.scalar.activation(warm_out[:], warm[:], SILU)
 
         load_rows(0, 0)
         nc.sync.dma_start(offs_sb[:], offs)
@@ -195,6 +197,9 @@ def tile_moe_pre_lin_silu_kernel(tc, xT, w, b, gate, offs, pos1, pos2, out):
             round_x(*step)
             if i > 0:
                 quantize_x(*steps[i - 1])
+            if i == len(steps) - 1:
+                last_codes.append(keep.tile([P, PASSES * N], U32, name="rows12", align_bytes=64))
+                quantize_w(E - 1, E)
             for e in round_experts.get(i, ()):
                 round_w(e)
             if i > 0 and steps[i - 1][0] == PASSES - 1:
@@ -202,8 +207,8 @@ def tile_moe_pre_lin_silu_kernel(tc, xT, w, b, gate, offs, pos1, pos2, out):
         quantize_x(*steps[-1])
         experts(*steps[-1][1:])
 
-        first = keep.tile([P, T], F32, name="rows00")
-        total = keep.tile([P, T], F32, name="rows01")
+        first = keep.tile([P, T], F32, name="rows00", align_bytes=64)
+        total = keep.tile([P, T], F32, name="rows01", align_bytes=64)
         for lo, hi in spans(FIRST_PIECES):
             nc.vector.tensor_copy(first[:, lo:hi], y[:].indirect(pos1_sb[:, lo // PER_COLUMN : hi // PER_COLUMN]))
         for lo, hi in spans(TOKEN_PIECES):

@@ -21,15 +21,19 @@ P = 128
 PACK = 4
 PASSES = K // (P * PACK)
 PER_COLUMN = 16
-QUAD = 4
-W_BUFS = 6
-W_CALLS = {3: 0, 7: 4, 9: 8, 10: 10}
+RUN = 4
+WIDEST = 1024
 
 CHUNKS = ((1536, 1536), (1024, 768, 512, 384, 256, 128))
 SPARE = 16
+GATE_PIECES = (192, 448, 896, 1536)
+HEAD_PIECES = 3
 FIRST_PIECES = (768, 768)
 TOKEN_PIECES = (768, 384, 256, 128)
-GATE_PIECES = (192, 448, 896, 1536)
+QUAD = 4
+W_BUFS = 6
+W_CALLS = {3: 0, 7: 4, 9: 8, 10: 10}
+ROUND_IN_STEP = {0: range(4, 10), 1: range(10, 12)}
 
 
 def spans(widths):
@@ -40,10 +44,14 @@ def spans(widths):
     return result
 
 
+def halves(lo, hi):
+    return [(lo, (lo + hi) // 2), ((lo + hi) // 2, hi)]
+
+
 def powers_of_two(lo, hi):
     result = []
     while lo < hi:
-        width = 1024
+        width = WIDEST
         while width > hi - lo:
             width //= 2
         result.append((lo, lo + width))
@@ -56,7 +64,7 @@ def tile_moe_pre_lin_silu_kernel(tc, xT, w, b, gate, offs, pos1, pos2, out):
     with ExitStack() as ctx:
         keep = ctx.enter_context(tc.tile_pool(name="keep", bufs=1))
         ring2 = ctx.enter_context(tc.tile_pool(name="ring2", bufs=2))
-        ring6 = ctx.enter_context(tc.tile_pool(name="ring6", bufs=6))
+        w_ring = ctx.enter_context(tc.tile_pool(name="w_ring", bufs=W_BUFS))
         psum = ctx.enter_context(tc.psum_pool(name="psum", bufs=8))
 
         offs_sb = keep.tile([P, S // PER_COLUMN], U16, name="offs_sb")
@@ -64,7 +72,13 @@ def tile_moe_pre_lin_silu_kernel(tc, xT, w, b, gate, offs, pos1, pos2, out):
         pos2_sb = keep.tile([P, T // PER_COLUMN], U16, name="pos2_sb")
         bias = keep.tile([P, E], F32, name="bias")
         gate_sb = keep.tile([P, S], F32, name="gate_sb")
-        rows = [[keep.tile([P, T + (SPARE if g == 0 else 0)], F32, name="rows%d%d" % (g, j), align_bytes=64) for j in range(PACK)] for g in range(PASSES)]
+        rows = [
+            [
+                keep.tile([P, T + (SPARE if g == 0 else 0)], F32, name="rows%d%d" % (g, j), align_bytes=64)
+                for j in range(PACK)
+            ]
+            for g in range(PASSES)
+        ]
         x_codes = [keep.tile([P, S], U32, name="x_codes%d" % g, align_bytes=64) for g in range(PASSES)]
         x_scales = [keep.tile([P, S], U8, name="x_scales%d" % g, align_bytes=64) for g in range(PASSES)]
         w_codes = keep.tile([P, (E - 1) * PASSES * N], U32, name="w_codes", align_bytes=64)
@@ -87,7 +101,7 @@ def tile_moe_pre_lin_silu_kernel(tc, xT, w, b, gate, offs, pos1, pos2, out):
             nc.sync.dma_start(gate_sb[:, cols], gate[0:P, cols])
 
         def load_w(e):
-            w_raw[e] = ring6.tile([P, PASSES, PACK * N], F32, name="w_raw")
+            w_raw[e] = w_ring.tile([P, PASSES, PACK * N], F32, name="w_raw")
             nc.sync.dma_start(w_raw[e][:], w_view[:, PASSES * e : PASSES * (e + 1), :])
 
         def round_w(e):
@@ -96,8 +110,8 @@ def tile_moe_pre_lin_silu_kernel(tc, xT, w, b, gate, offs, pos1, pos2, out):
                 w_grouped[quad] = ring2.tile([P, QUAD * PASSES, N * PACK], BF16, name="w_grouped", align_bytes=64)
             for g in range(PASSES):
                 nc.scalar.copy(
-                    w_grouped[quad][:, PASSES * place + g, :].rearrange("p (c i j) -> p c j i", i=4, j=PACK),
-                    w_raw[e][:, g, :].rearrange("p (j c i) -> p c j i", i=4, j=PACK),
+                    w_grouped[quad][:, PASSES * place + g, :].rearrange("p (c i j) -> p c j i", i=RUN, j=PACK),
+                    w_raw[e][:, g, :].rearrange("p (j c i) -> p c j i", i=RUN, j=PACK),
                 )
             if e + W_BUFS < E:
                 load_w(e + W_BUFS)
@@ -111,17 +125,21 @@ def tile_moe_pre_lin_silu_kernel(tc, xT, w, b, gate, offs, pos1, pos2, out):
 
         def quantize_w(e0, e1):
             quad = e0 // QUAD
+            rounded = w_grouped[quad][:, PASSES * (e0 - QUAD * quad) : PASSES * (e1 - QUAD * quad), :]
             nc.vector.quantize_mx(
                 out=codes_of(e0, e1).bitcast(FP8X4),
                 scales=w_scales[:, PASSES * N * e0 : PASSES * N * e1],
-                in_=w_grouped[quad][:, PASSES * (e0 - QUAD * quad) : PASSES * (e1 - QUAD * quad), :].rearrange("p q c -> p (q c)"),
+                in_=rounded.rearrange("p q c -> p (q c)"),
             )
 
-        def gather(g, lo, hi, planes):
-            if (g, lo) not in gathered:
-                gathered[g, lo] = ring2.tile([P, PACK, hi - lo], F32, name="gathered")
-            for j in planes:
-                cuts = spans(GATE_PIECES[:3]) if (g, lo, j) == (0, 0, 0) else [(lo, hi)]
+        def gather(g, lo, hi):
+            gathered[g, lo] = ring2.tile([P, PACK, hi - lo], F32, name="gathered")
+            for j in range(PACK):
+                cuts = [(lo, hi)]
+                if (g, lo, j) == (0, 0, 0):
+                    cuts = spans(GATE_PIECES[:HEAD_PIECES])
+                if (g, hi, j) == (PASSES - 1, S, PACK - 1):
+                    cuts = halves(lo, hi)
                 for a, z in cuts:
                     nc.vector.tensor_tensor(
                         gathered[g, lo][:, j, a - lo : z - lo],
@@ -132,10 +150,11 @@ def tile_moe_pre_lin_silu_kernel(tc, xT, w, b, gate, offs, pos1, pos2, out):
 
         def round_x(g, lo, hi):
             grouped[g, lo] = ring2.tile([P, (hi - lo) * PACK], BF16, name="grouped", align_bytes=64)
-            nc.scalar.copy(
-                grouped[g, lo][:].rearrange("p (c i j) -> p c j i", i=4, j=PACK),
-                gathered[g, lo][:].rearrange("p j (c i) -> p c j i", i=4),
-            )
+            for a, z in halves(lo, hi) if (g, hi) == (PASSES - 1, S) else [(lo, hi)]:
+                nc.scalar.copy(
+                    grouped[g, lo][:, (a - lo) * PACK : (z - lo) * PACK].rearrange("p (c i j) -> p c j i", i=RUN, j=PACK),
+                    gathered[g, lo][:, :, a - lo : z - lo].rearrange("p j (c i) -> p c j i", i=RUN),
+                )
 
         def quantize_x(g, lo, hi):
             for a, z in powers_of_two(lo, hi):
@@ -152,11 +171,10 @@ def tile_moe_pre_lin_silu_kernel(tc, xT, w, b, gate, offs, pos1, pos2, out):
                 z = min(hi, (e + 1) * C)
                 acc = psum.tile([P, z - a], F32, name="acc")
                 for g in range(PASSES):
-                    wc = slice((e * PASSES + g) * N, (e * PASSES + g + 1) * N)
                     nc.tensor.matmul_mx(
                         out=acc[:],
                         lhsT=codes_of(e, e + 1)[:, g * N : (g + 1) * N].bitcast(FP8X4),
-                        lhsT_scale=w_scales[:, wc],
+                        lhsT_scale=w_scales[:, (e * PASSES + g) * N : (e * PASSES + g + 1) * N],
                         rhs=x_codes[g][:, a:z].bitcast(FP8X4),
                         rhs_scale=x_scales[g][:, a:z],
                         start=(g == 0),
@@ -170,7 +188,7 @@ def tile_moe_pre_lin_silu_kernel(tc, xT, w, b, gate, offs, pos1, pos2, out):
 
         load_rows(0, 0)
         nc.sync.dma_start(offs_sb[:], offs)
-        for i in range(3):
+        for i in range(HEAD_PIECES):
             load_gate(i)
         load_rows(0, 1)
         load_rows(0, 2)
@@ -179,7 +197,7 @@ def tile_moe_pre_lin_silu_kernel(tc, xT, w, b, gate, offs, pos1, pos2, out):
         load_rows(0, 3)
         load_w(2)
         load_w(3)
-        load_gate(3)
+        load_gate(HEAD_PIECES)
         load_w(4)
         load_w(5)
         nc.sync.dma_start(bias[:], b)
@@ -191,16 +209,15 @@ def tile_moe_pre_lin_silu_kernel(tc, xT, w, b, gate, offs, pos1, pos2, out):
         steps = [(g, lo, hi) for g in range(PASSES) for lo, hi in spans(CHUNKS[g])]
         for e in range(QUAD):
             round_w(e)
-        round_experts = {0: range(4, 10), 1: range(10, 12)}
         for i, step in enumerate(steps):
-            gather(*step, range(PACK))
+            gather(*step)
             round_x(*step)
             if i > 0:
                 quantize_x(*steps[i - 1])
             if i == len(steps) - 1:
                 last_codes.append(keep.tile([P, PASSES * N], U32, name="rows12", align_bytes=64))
                 quantize_w(E - 1, E)
-            for e in round_experts.get(i, ()):
+            for e in ROUND_IN_STEP.get(i, ()):
                 round_w(e)
             if i > 0 and steps[i - 1][0] == PASSES - 1:
                 experts(*steps[i - 1][1:])

@@ -22,18 +22,14 @@ PACK = 4
 PASSES = K // (P * PACK)
 PER_COLUMN = 16
 RUN = 4
-WIDEST = 1024
-
-CHUNKS = ((1536, 1536), (1024, 768, 512, 384, 256, 128))
+W_WORDS = PASSES * N
 SPARE = 16
-GATE_PIECES = (192, 448, 896, 1536)
-HEAD_PIECES = 3
+A, B = 1536, 2560
+LAST = 2816
+GATE_PIECES = (192, 448, 896)
 FIRST_PIECES = (768, 768)
 TOKEN_PIECES = (768, 384, 256, 128)
-QUAD = 4
 W_BUFS = 6
-W_CALLS = {3: 0, 7: 4, 9: 8, 10: 10}
-ROUND_IN_STEP = {0: range(4, 10), 1: range(10, 12)}
 
 
 def spans(widths):
@@ -48,17 +44,6 @@ def halves(lo, hi):
     return [(lo, (lo + hi) // 2), ((lo + hi) // 2, hi)]
 
 
-def powers_of_two(lo, hi):
-    result = []
-    while lo < hi:
-        width = WIDEST
-        while width > hi - lo:
-            width //= 2
-        result.append((lo, lo + width))
-        lo += width
-    return result
-
-
 def tile_moe_pre_lin_silu_kernel(tc, xT, w, b, gate, offs, pos1, pos2, out):
     nc = tc.nc
     with ExitStack() as ctx:
@@ -71,65 +56,43 @@ def tile_moe_pre_lin_silu_kernel(tc, xT, w, b, gate, offs, pos1, pos2, out):
         pos1_sb = keep.tile([P, T // PER_COLUMN], U16, name="pos1_sb")
         pos2_sb = keep.tile([P, T // PER_COLUMN], U16, name="pos2_sb")
         bias = keep.tile([P, E], F32, name="bias")
-        gate_sb = keep.tile([P, S], F32, name="gate_sb")
+        gate_first = keep.tile([P, A], F32, name="gate_first", align_bytes=64)
+        gate_rest = keep.tile([P, S - A], F32, name="gate_rest")
         rows = [
-            [
-                keep.tile([P, T + (SPARE if g == 0 else 0)], F32, name="rows%d%d" % (g, j), align_bytes=64)
-                for j in range(PACK)
-            ]
+            [keep.tile([P, T + SPARE], F32, name="rows%d%d" % (g, j), align_bytes=64) for j in range(PACK)]
             for g in range(PASSES)
         ]
-        x_codes = [keep.tile([P, S], U32, name="x_codes%d" % g, align_bytes=64) for g in range(PASSES)]
-        x_scales = [keep.tile([P, S], U8, name="x_scales%d" % g, align_bytes=64) for g in range(PASSES)]
-        w_codes = keep.tile([P, (E - 1) * PASSES * N], U32, name="w_codes", align_bytes=64)
-        last_codes = []
-        w_scales = keep.tile([P, E * PASSES * N], U8, name="w_scales", align_bytes=64)
         y = keep.tile([P, S], F32, name="y")
 
         x_view = xT.rearrange("(g p j) t -> g j p t", g=PASSES, j=PACK)
         w_view = w.rearrange("e (g p j) n -> p (e g) (j n)", g=PASSES, j=PACK)
         w_raw = {}
-        w_grouped = {}
         gathered = {}
-        grouped = {}
+        x_ops = {}
+        w_ops = {}
+        sums = {}
 
         def load_rows(g, j):
             nc.sync.dma_start(rows[g][j][:, :T], x_view[g, j])
-
-        def load_gate(i):
-            cols = slice(*spans(GATE_PIECES)[i])
-            nc.sync.dma_start(gate_sb[:, cols], gate[0:P, cols])
 
         def load_w(e):
             w_raw[e] = w_ring.tile([P, PASSES, PACK * N], F32, name="w_raw")
             nc.sync.dma_start(w_raw[e][:], w_view[:, PASSES * e : PASSES * (e + 1), :])
 
-        def round_w(e):
-            quad, place = divmod(e, QUAD)
-            if place == 0:
-                w_grouped[quad] = ring2.tile([P, QUAD * PASSES, N * PACK], BF16, name="w_grouped", align_bytes=64)
-            for g in range(PASSES):
-                nc.scalar.copy(
-                    w_grouped[quad][:, PASSES * place + g, :].rearrange("p (c i j) -> p c j i", i=RUN, j=PACK),
-                    w_raw[e][:, g, :].rearrange("p (j c i) -> p c j i", i=RUN, j=PACK),
-                )
-            if e + W_BUFS < E:
-                load_w(e + W_BUFS)
-            if e in W_CALLS:
-                quantize_w(W_CALLS[e], e + 1)
+        def rounded_tile(pool, words, name):
+            return pool.tile([P, words * PACK], BF16, name=name, align_bytes=64)
 
-        def codes_of(e0, e1):
-            if e0 == E - 1:
-                return last_codes[0][:]
-            return w_codes[:, PASSES * N * e0 : PASSES * N * e1]
+        def operand_tiles(words, codes_name, scales_name):
+            codes = keep.tile([P, words], U32, name=codes_name, align_bytes=64)
+            scales = keep.tile([P, words], U8, name=scales_name, align_bytes=64)
+            return codes, scales
 
-        def quantize_w(e0, e1):
-            quad = e0 // QUAD
-            rounded = w_grouped[quad][:, PASSES * (e0 - QUAD * quad) : PASSES * (e1 - QUAD * quad), :]
-            nc.vector.quantize_mx(
-                out=codes_of(e0, e1).bitcast(FP8X4),
-                scales=w_scales[:, PASSES * N * e0 : PASSES * N * e1],
-                in_=rounded.rearrange("p q c -> p (q c)"),
+        def round_w(e, rounded, word):
+            nc.scalar.copy(
+                rounded[:, word * PACK : (word + W_WORDS) * PACK].rearrange(
+                    "p (g c i j) -> p g c j i", g=PASSES, i=RUN, j=PACK
+                ),
+                w_raw[e][:].rearrange("p g (j c i) -> p g c j i", i=RUN, j=PACK),
             )
 
         def gather(g, lo, hi):
@@ -137,92 +100,165 @@ def tile_moe_pre_lin_silu_kernel(tc, xT, w, b, gate, offs, pos1, pos2, out):
             for j in range(PACK):
                 cuts = [(lo, hi)]
                 if (g, lo, j) == (0, 0, 0):
-                    cuts = spans(GATE_PIECES[:HEAD_PIECES])
+                    cuts = spans(GATE_PIECES)
                 if (g, hi, j) == (PASSES - 1, S, PACK - 1):
                     cuts = halves(lo, hi)
                 for a, z in cuts:
                     nc.vector.tensor_tensor(
                         gathered[g, lo][:, j, a - lo : z - lo],
                         rows[g][j][:].indirect(offs_sb[:, a // PER_COLUMN : z // PER_COLUMN]),
-                        gate_sb[:, a:z],
+                        gate_first[:, a:z] if lo < A else gate_rest[:, a - A : z - A],
                         MULT,
                     )
 
-        def round_x(g, lo, hi):
-            grouped[g, lo] = ring2.tile([P, (hi - lo) * PACK], BF16, name="grouped", align_bytes=64)
+        def round_x(g, lo, hi, rounded):
             for a, z in halves(lo, hi) if (g, hi) == (PASSES - 1, S) else [(lo, hi)]:
                 nc.scalar.copy(
-                    grouped[g, lo][:, (a - lo) * PACK : (z - lo) * PACK].rearrange("p (c i j) -> p c j i", i=RUN, j=PACK),
+                    rounded[:, (a - lo) * PACK : (z - lo) * PACK].rearrange("p (c i j) -> p c j i", i=RUN, j=PACK),
                     gathered[g, lo][:, :, a - lo : z - lo].rearrange("p j (c i) -> p c j i", i=RUN),
                 )
 
-        def quantize_x(g, lo, hi):
-            for a, z in powers_of_two(lo, hi):
-                nc.vector.quantize_mx(
-                    out=x_codes[g][:, a:z].bitcast(FP8X4),
-                    scales=x_scales[g][:, a:z],
-                    in_=grouped[g, lo][:, (a - lo) * PACK : (z - lo) * PACK],
-                )
+        def quantize(rounded, a, z, operand, at):
+            codes, scales = operand
+            nc.vector.quantize_mx(
+                out=codes[:, at : at + z - a].bitcast(FP8X4),
+                scales=scales[:, at : at + z - a],
+                in_=rounded[:, a * PACK : z * PACK],
+            )
 
-        def experts(lo, hi):
-            a = lo
-            while a < hi:
-                e = a // C
-                z = min(hi, (e + 1) * C)
-                acc = psum.tile([P, z - a], F32, name="acc")
+        def name_x(g, lo, hi, operand):
+            for e in range(lo // C, hi // C):
+                x_ops[g, e] = [t[:, e * C - lo : (e + 1) * C - lo] for t in operand]
+
+        def name_w(e0, e1, operand, at):
+            for e in range(e0, e1):
+                a = at + (e - e0) * W_WORDS
+                w_ops[e] = [t[:, a : a + W_WORDS] for t in operand]
+
+        def multiply(g, e, lo, hi):
+            if g == 0:
+                sums[e, lo] = psum.tile([P, hi - lo], F32, name="acc")
+            nc.tensor.matmul_mx(
+                out=sums[e, lo][:],
+                lhsT=w_ops[e][0][:, g * N : (g + 1) * N].bitcast(FP8X4),
+                lhsT_scale=w_ops[e][1][:, g * N : (g + 1) * N],
+                rhs=x_ops[g, e][0][:, lo:hi].bitcast(FP8X4),
+                rhs_scale=x_ops[g, e][1][:, lo:hi],
+                start=(g == 0),
+                stop=(g == PASSES - 1),
+            )
+            if g == PASSES - 1:
+                nc.scalar.activation(y[:, e * C + lo : e * C + hi], sums[e, lo][:], SILU, bias=bias[:, e : e + 1])
+
+        def experts(e0, e1):
+            for e in range(e0, e1):
                 for g in range(PASSES):
-                    nc.tensor.matmul_mx(
-                        out=acc[:],
-                        lhsT=codes_of(e, e + 1)[:, g * N : (g + 1) * N].bitcast(FP8X4),
-                        lhsT_scale=w_scales[:, (e * PASSES + g) * N : (e * PASSES + g + 1) * N],
-                        rhs=x_codes[g][:, a:z].bitcast(FP8X4),
-                        rhs_scale=x_scales[g][:, a:z],
-                        start=(g == 0),
-                        stop=(g == PASSES - 1),
-                    )
-                nc.scalar.activation(y[:, a:z], acc[:], SILU, bias=bias[:, e : e + 1])
-                a = z
+                    multiply(g, e, 0, C)
 
-        for j in range(PACK):
-            nc.gpsimd.memset(rows[0][j][:, T:], 0.0)
+        for g in range(PASSES):
+            for j in range(PACK):
+                nc.gpsimd.memset(rows[g][j][:, T:], 0.0)
 
         load_rows(0, 0)
         nc.sync.dma_start(offs_sb[:], offs)
-        for i in range(HEAD_PIECES):
-            load_gate(i)
+        for a, z in spans(GATE_PIECES):
+            nc.sync.dma_start(gate_first[:, a:z], gate[0:P, a:z])
         load_rows(0, 1)
         load_rows(0, 2)
-        load_w(0)
-        load_w(1)
+        for e in range(3):
+            load_w(e)
         load_rows(0, 3)
-        load_w(2)
-        load_w(3)
-        load_gate(HEAD_PIECES)
-        load_w(4)
-        load_w(5)
+        for j in range(PACK - 1):
+            load_w(3 + j)
+            load_rows(1, j)
+
+        rounded_a0 = rounded_tile(ring2, A + 2 * W_WORDS, "rounded")
+        rounded_a1 = rounded_tile(ring2, A + 2 * W_WORDS, "rounded")
+        round_w(0, rounded_a0, A)
+        load_w(6)
+        load_rows(1, 3)
+        round_w(1, rounded_a0, A + W_WORDS)
+        load_w(7)
+        nc.sync.dma_start(gate_rest[:], gate[0:P, A:S])
         nc.sync.dma_start(bias[:], b)
         nc.sync.dma_start(pos1_sb[:], pos1)
         nc.sync.dma_start(pos2_sb[:], pos2)
-        for j in range(PACK):
-            load_rows(1, j)
+        round_w(2, rounded_a1, A)
+        load_w(8)
+        round_w(3, rounded_a1, A + W_WORDS)
+        load_w(9)
+        gather(0, 0, A)
+        round_x(0, 0, A, rounded_a0)
+        rounded_w4 = rounded_tile(keep, 4 * W_WORDS, "rounded_w4")
+        for e in range(4, 8):
+            round_w(e, rounded_w4, (e - 4) * W_WORDS)
+            if e + W_BUFS < E:
+                load_w(e + W_BUFS)
+        gather(1, 0, A)
+        round_x(1, 0, A, rounded_a1)
+        early = operand_tiles(A + 6 * W_WORDS, "gate_first", "scales_early")
+        quantize(rounded_a0, 0, 1024, early, 0)
+        quantize(rounded_a0, 1024, 2048, early, 1024)
+        quantize(rounded_w4, 0, 1024, early, 2048)
+        name_x(0, 0, A, early)
+        name_w(0, 2, early, A)
+        name_w(4, 8, early, 2048)
+        rounded_w8 = rounded_tile(keep, 2 * W_WORDS, "rounded_w8")
+        for e in range(8, 10):
+            round_w(e, rounded_w8, (e - 8) * W_WORDS)
 
-        steps = [(g, lo, hi) for g in range(PASSES) for lo, hi in spans(CHUNKS[g])]
-        for e in range(QUAD):
-            round_w(e)
-        for i, step in enumerate(steps):
-            gather(*step)
-            round_x(*step)
-            if i > 0:
-                quantize_x(*steps[i - 1])
-            if i == len(steps) - 1:
-                last_codes.append(keep.tile([P, PASSES * N], U32, name="rows12", align_bytes=64))
-                quantize_w(E - 1, E)
-            for e in ROUND_IN_STEP.get(i, ()):
-                round_w(e)
-            if i > 0 and steps[i - 1][0] == PASSES - 1:
-                experts(*steps[i - 1][1:])
-        quantize_x(*steps[-1])
-        experts(*steps[-1][1:])
+        gather(0, A, B)
+        rounded_b0 = rounded_tile(ring2, B - A, "rounded")
+        round_x(0, A, B, rounded_b0)
+        op_a1 = operand_tiles(2048, "codes_a1", "scales_a1")
+        quantize(rounded_a1, 0, 1024, op_a1, 0)
+        quantize(rounded_a1, 1024, 2048, op_a1, 1024)
+        name_x(1, 0, A, op_a1)
+        name_w(2, 4, op_a1, A)
+        experts(0, 6)
+        rounded_c0 = rounded_tile(keep, 2 * (W_WORDS + C), "rounded_c0")
+        round_w(E - 2, rounded_c0, 0)
+        round_w(E - 1, rounded_c0, W_WORDS + 2 * C)
+        gather(1, A, B)
+        rounded_b1 = rounded_tile(ring2, B - A, "rounded")
+        round_x(1, A, B, rounded_b1)
+        op_b0 = operand_tiles(B - A, "codes_b0", "scales_b0")
+        quantize(rounded_b0, 0, B - A, op_b0, 0)
+        name_x(0, A, B, op_b0)
+        op_w8 = operand_tiles(2 * W_WORDS, "codes_w8", "scales_w8")
+        quantize(rounded_w8, 0, 2 * W_WORDS, op_w8, 0)
+        name_w(8, 10, op_w8, 0)
+
+        gather(0, B, S)
+        round_x(0, B, S, rounded_c0[:, W_WORDS * PACK : (W_WORDS + 2 * C) * PACK])
+        op_b1 = operand_tiles(B - A, "codes_b1", "scales_b1")
+        quantize(rounded_b1, 0, B - A, op_b1, 0)
+        name_x(1, A, B, op_b1)
+        experts(6, 10)
+        gather(1, B, LAST)
+        rounded_c1 = rounded_tile(ring2, C, "rounded")
+        round_x(1, B, LAST, rounded_c1)
+        op_10 = operand_tiles(W_WORDS + C, "codes_10", "scales_10")
+        quantize(rounded_c0, 0, W_WORDS + C, op_10, 0)
+        name_w(E - 2, E - 1, op_10, 0)
+        x_ops[0, E - 2] = [t[:, W_WORDS:] for t in op_10]
+        multiply(0, E - 2, 0, C)
+        gather(1, LAST, S)
+        rounded_last = rounded_tile(ring2, C, "rounded")
+        round_x(1, LAST, S, rounded_last)
+        op_c1 = operand_tiles(S - B, "codes_c1", "scales_c1")
+        name_x(1, B, S, op_c1)
+        quantize(rounded_c1, 0, C, op_c1, 0)
+        multiply(1, E - 2, 0, C)
+        op_11 = operand_tiles(C + W_WORDS, "rows10", "scales_11")
+        quantize(rounded_c0, W_WORDS + C, 2 * (W_WORDS + C), op_11, 0)
+        x_ops[0, E - 1] = [t[:, :C] for t in op_11]
+        name_w(E - 1, E, op_11, C)
+        for lo, hi in halves(0, C):
+            multiply(0, E - 1, lo, hi)
+        for lo, hi in halves(0, C):
+            quantize(rounded_last, lo, hi, op_c1, C + lo)
+            multiply(1, E - 1, lo, hi)
 
         first = keep.tile([P, T], F32, name="rows00", align_bytes=64)
         total = keep.tile([P, T], F32, name="rows01", align_bytes=64)

@@ -168,9 +168,12 @@ def tile_moe_pre_lin_silu_kernel(tc, xT, w, b, gate, offs, pos1, pos2, out):
         for e in range(3):
             load_w(e)
         load_rows(0, 3)
-        for j in range(PACK - 1):
-            load_w(3 + j)
-            load_rows(1, j)
+        load_w(3)
+        load_rows(1, 0)
+        load_w(4)
+        load_rows(1, 1)
+        load_rows(1, 2)
+        load_w(5)
 
         rounded_a0 = rounded_tile(ring2, A + 2 * W_WORDS, "rounded")
         rounded_a1 = rounded_tile(ring2, A + 2 * W_WORDS, "rounded")
@@ -196,7 +199,7 @@ def tile_moe_pre_lin_silu_kernel(tc, xT, w, b, gate, offs, pos1, pos2, out):
                 load_w(e + W_BUFS)
         gather(1, 0, A)
         round_x(1, 0, A, rounded_a1)
-        early = operand_tiles(A + 6 * W_WORDS, "gate_first", "scales_early")
+        early = operand_tiles(A + 6 * W_WORDS, "codes_early", "scales_early")
         quantize(rounded_a0, 0, 1024, early, 0)
         quantize(rounded_a0, 1024, 2048, early, 1024)
         quantize(rounded_w4, 0, 1024, early, 2048)
@@ -222,7 +225,7 @@ def tile_moe_pre_lin_silu_kernel(tc, xT, w, b, gate, offs, pos1, pos2, out):
         gather(1, A, B)
         rounded_b1 = rounded_tile(ring2, B - A, "rounded")
         round_x(1, A, B, rounded_b1)
-        op_b0 = operand_tiles(B - A, "codes_b0", "scales_b0")
+        op_b0 = operand_tiles(B - A, "gate_first", "scales_b0")
         quantize(rounded_b0, 0, B - A, op_b0, 0)
         name_x(0, A, B, op_b0)
         op_w8 = operand_tiles(2 * W_WORDS, "codes_w8", "scales_w8")

@@ -62,7 +62,7 @@ def tile_moe_pre_lin_silu_kernel(tc, xT, w, b, gate, offs, pos1, pos2, out):
             [keep.tile([P, T + SPARE], F32, name="rows%d%d" % (g, j), align_bytes=64) for j in range(PACK)]
             for g in range(PASSES)
         ]
-        y = keep.tile([P, S], F32, name="y")
+        results = []
 
         x_view = xT.rearrange("(g p j) t -> g j p t", g=PASSES, j=PACK)
         w_view = w.rearrange("e (g p j) n -> p (e g) (j n)", g=PASSES, j=PACK)
@@ -111,12 +111,11 @@ def tile_moe_pre_lin_silu_kernel(tc, xT, w, b, gate, offs, pos1, pos2, out):
                         MULT,
                     )
 
-        def round_x(g, lo, hi, rounded):
-            for a, z in halves(lo, hi) if (g, hi) == (PASSES - 1, S) else [(lo, hi)]:
-                nc.scalar.copy(
-                    rounded[:, (a - lo) * PACK : (z - lo) * PACK].rearrange("p (c i j) -> p c j i", i=RUN, j=PACK),
-                    gathered[g, lo][:, :, a - lo : z - lo].rearrange("p j (c i) -> p c j i", i=RUN),
-                )
+        def round_x(g, lo, a, z, rounded):
+            nc.scalar.copy(
+                rounded[:, : (z - a) * PACK].rearrange("p (c i j) -> p c j i", i=RUN, j=PACK),
+                gathered[g, lo][:, :, a - lo : z - lo].rearrange("p j (c i) -> p c j i", i=RUN),
+            )
 
         def quantize(rounded, a, z, operand, at):
             codes, scales = operand
@@ -148,7 +147,7 @@ def tile_moe_pre_lin_silu_kernel(tc, xT, w, b, gate, offs, pos1, pos2, out):
                 stop=(g == PASSES - 1),
             )
             if g == PASSES - 1:
-                nc.scalar.activation(y[:, e * C + lo : e * C + hi], sums[e, lo][:], SILU, bias=bias[:, e : e + 1])
+                nc.scalar.activation(results[0][:, e * C + lo : e * C + hi], sums[e, lo][:], SILU, bias=bias[:, e : e + 1])
 
         def experts(e0, e1):
             for e in range(e0, e1):
@@ -191,76 +190,77 @@ def tile_moe_pre_lin_silu_kernel(tc, xT, w, b, gate, offs, pos1, pos2, out):
         round_w(3, rounded_a1, A + W_WORDS)
         load_w(9)
         gather(0, 0, A)
-        round_x(0, 0, A, rounded_a0)
-        rounded_w4 = rounded_tile(keep, 4 * W_WORDS, "rounded_w4")
-        for e in range(4, 8):
+        round_x(0, 0, 0, A, rounded_a0)
+        rounded_w4 = rounded_tile(keep, 2 * W_WORDS, "rounded_w4")
+        rounded_b0 = rounded_tile(keep, 6 * (C + W_WORDS), "rounded_b0")
+        blocks = [(6, 8), (8, 10), (10, 11), (11, 12)]
+
+        def block_at(e0):
+            return (e0 - 6) * (C + W_WORDS)
+
+        def round_block_w(e0, e1):
+            for e in range(e0, e1):
+                round_w(e, rounded_b0, block_at(e0) + (e1 - e0) * C + (e - e0) * W_WORDS)
+                if e + W_BUFS < E:
+                    load_w(e + W_BUFS)
+
+        def quantize_block(e0, e1, operand, at):
+            quantize(rounded_b0, block_at(e0), block_at(e1), operand, at)
+            name_x(0, e0 * C, e1 * C, [t[:, at:] for t in operand])
+            name_w(e0, e1, operand, at + (e1 - e0) * C)
+
+        for e in range(4, 6):
             round_w(e, rounded_w4, (e - 4) * W_WORDS)
-            if e + W_BUFS < E:
-                load_w(e + W_BUFS)
+            load_w(e + W_BUFS)
+        round_block_w(*blocks[0])
         gather(1, 0, A)
-        round_x(1, 0, A, rounded_a1)
-        early = operand_tiles(A + 6 * W_WORDS, "codes_early", "scales_early")
+        round_x(1, 0, 0, A, rounded_a1)
+        early = operand_tiles(A + 4 * W_WORDS, "codes_early", "scales_early")
         quantize(rounded_a0, 0, 1024, early, 0)
         quantize(rounded_a0, 1024, 2048, early, 1024)
-        quantize(rounded_w4, 0, 1024, early, 2048)
+        quantize(rounded_w4, 0, 512, early, 2048)
         name_x(0, 0, A, early)
         name_w(0, 2, early, A)
-        name_w(4, 8, early, 2048)
-        rounded_w8 = rounded_tile(keep, 2 * W_WORDS, "rounded_w8")
-        for e in range(8, 10):
-            round_w(e, rounded_w8, (e - 8) * W_WORDS)
+        name_w(4, 6, early, 2048)
+        for block in blocks[1:]:
+            round_block_w(*block)
 
-        gather(0, A, B)
-        rounded_b0 = rounded_tile(ring2, B - A, "rounded")
-        round_x(0, A, B, rounded_b0)
+        gather(0, A, S)
+        for e0, e1 in blocks:
+            round_x(0, A, e0 * C, e1 * C, rounded_b0[:, block_at(e0) * PACK :])
         op_a1 = operand_tiles(2048, "codes_a1", "scales_a1")
         quantize(rounded_a1, 0, 1024, op_a1, 0)
         quantize(rounded_a1, 1024, 2048, op_a1, 1024)
         name_x(1, 0, A, op_a1)
         name_w(2, 4, op_a1, A)
+        y = keep.tile([P, S], F32, name="rows02", align_bytes=64)
+        results.append(y)
         experts(0, 6)
-        rounded_c0 = rounded_tile(keep, 2 * (W_WORDS + C), "rounded_c0")
-        round_w(E - 2, rounded_c0, 0)
-        round_w(E - 1, rounded_c0, W_WORDS + 2 * C)
         gather(1, A, B)
         rounded_b1 = rounded_tile(ring2, B - A, "rounded")
-        round_x(1, A, B, rounded_b1)
-        op_b0 = operand_tiles(B - A, "gate_first", "scales_b0")
-        quantize(rounded_b0, 0, B - A, op_b0, 0)
-        name_x(0, A, B, op_b0)
-        op_w8 = operand_tiles(2 * W_WORDS, "codes_w8", "scales_w8")
-        quantize(rounded_w8, 0, 2 * W_WORDS, op_w8, 0)
-        name_w(8, 10, op_w8, 0)
-
-        gather(0, B, S)
-        round_x(0, B, S, rounded_c0[:, W_WORDS * PACK : (W_WORDS + 2 * C) * PACK])
-        op_b1 = operand_tiles(B - A, "codes_b1", "scales_b1")
-        quantize(rounded_b1, 0, B - A, op_b1, 0)
-        name_x(1, A, B, op_b1)
-        experts(6, 10)
+        round_x(1, A, A, B, rounded_b1)
+        op_b0 = operand_tiles(block_at(E - 1), "gate_first", "scales_b0")
+        for e0, e1 in blocks[:3]:
+            quantize_block(e0, e1, op_b0, block_at(e0))
         gather(1, B, LAST)
-        rounded_c1 = rounded_tile(ring2, C, "rounded")
-        round_x(1, B, LAST, rounded_c1)
-        op_10 = operand_tiles(W_WORDS + C, "codes_10", "scales_10")
-        quantize(rounded_c0, 0, W_WORDS + C, op_10, 0)
-        name_w(E - 2, E - 1, op_10, 0)
-        x_ops[0, E - 2] = [t[:, W_WORDS:] for t in op_10]
+        rounded_b2 = rounded_tile(ring2, C, "rounded")
+        round_x(1, B, B, LAST, rounded_b2)
+        op_b1 = operand_tiles(S - A, "rows03", "scales_b1")
+        name_x(1, A, S, op_b1)
+        quantize(rounded_b1, 0, B - A, op_b1, 0)
+        experts(6, 10)
         multiply(0, E - 2, 0, C)
         gather(1, LAST, S)
         rounded_last = rounded_tile(ring2, C, "rounded")
-        round_x(1, LAST, S, rounded_last)
-        op_c1 = operand_tiles(S - B, "codes_c1", "scales_c1")
-        name_x(1, B, S, op_c1)
-        quantize(rounded_c1, 0, C, op_c1, 0)
+        for lo, hi in halves(LAST, S):
+            round_x(1, LAST, lo, hi, rounded_last[:, (lo - LAST) * PACK :])
+        quantize(rounded_b2, 0, C, op_b1, B - A)
         multiply(1, E - 2, 0, C)
-        op_11 = operand_tiles(C + W_WORDS, "rows10", "scales_11")
-        quantize(rounded_c0, W_WORDS + C, 2 * (W_WORDS + C), op_11, 0)
-        x_ops[0, E - 1] = [t[:, :C] for t in op_11]
-        name_w(E - 1, E, op_11, C)
+        quantize_block(E - 1, E, operand_tiles(C + W_WORDS, "rows10", "scales_11"), 0)
         for lo, hi in halves(0, C):
             multiply(0, E - 1, lo, hi)
         for lo, hi in halves(0, C):
-            quantize(rounded_last, lo, hi, op_c1, C + lo)
+            quantize(rounded_last, lo, hi, op_b1, LAST - A + lo)
             multiply(1, E - 1, lo, hi)
 
         first = keep.tile([P, T], F32, name="rows00", align_bytes=64)

@@ -30,6 +30,7 @@ GATE_PIECES = (192, 448, 896)
 FIRST_PIECES = (768, 768)
 TOKEN_PIECES = (768, 384, 256, 128)
 W_BUFS = 6
+WHOLE = 2
 
 
 def spans(widths):
@@ -97,19 +98,18 @@ def tile_moe_pre_lin_silu_kernel(tc, xT, w, b, gate, offs, pos1, pos2, out):
 
         def gather(g, lo, hi):
             gathered[g, lo] = ring2.tile([P, PACK, hi - lo], F32, name="gathered")
-            for j in range(PACK):
-                cuts = [(lo, hi)]
-                if (g, lo, j) == (0, 0, 0):
-                    cuts = spans(GATE_PIECES)
-                if (g, hi, j) == (PASSES - 1, S, PACK - 1):
-                    cuts = halves(lo, hi)
-                for a, z in cuts:
-                    nc.vector.tensor_tensor(
-                        gathered[g, lo][:, j, a - lo : z - lo],
-                        rows[g][j][:].indirect(offs_sb[:, a // PER_COLUMN : z // PER_COLUMN]),
-                        gate_first[:, a:z] if lo < A else gate_rest[:, a - A : z - A],
-                        MULT,
-                    )
+            order = [(j, lo, hi) for j in range(PACK)]
+            if (g, lo) == (0, 0):
+                order = [(0, a, z) for a, z in spans(GATE_PIECES)] + order[1:]
+            if (g, lo) == (PASSES - 1, LAST):
+                order = order[:WHOLE] + [(j, a, z) for a, z in halves(lo, hi) for j in range(WHOLE, PACK)]
+            for j, a, z in order:
+                nc.vector.tensor_tensor(
+                    gathered[g, lo][:, j, a - lo : z - lo],
+                    rows[g][j][:].indirect(offs_sb[:, a // PER_COLUMN : z // PER_COLUMN]),
+                    gate_first[:, a:z] if lo < A else gate_rest[:, a - A : z - A],
+                    MULT,
+                )
 
         def round_x(g, lo, a, z, rounded):
             nc.scalar.copy(

@@ -23,14 +23,21 @@ PASSES = K // (P * PACK)
 PER_COLUMN = 16
 RUN = 4
 W_WORDS = PASSES * N
+WIDEST = 1024
+
+GROUP = E // 2
+SECOND = GROUP * C
+LAST_BUT_ONE = (E - 2) * C
+LAST = (E - 1) * C
+RIDERS = (2 * WIDEST - SECOND) // W_WORDS
+BLOCKS = ((6, 8), (8, 10), (10, 11), (11, 12))
+WHOLE = 2
 SPARE = 16
-A, B = 1536, 2560
-LAST = 2816
 GATE_PIECES = (192, 448, 896)
 FIRST_PIECES = (768, 768)
 TOKEN_PIECES = (768, 384, 256, 128)
 W_BUFS = 6
-WHOLE = 2
+BANKS = 8
 
 
 def spans(widths):
@@ -51,30 +58,29 @@ def tile_moe_pre_lin_silu_kernel(tc, xT, w, b, gate, offs, pos1, pos2, out):
         keep = ctx.enter_context(tc.tile_pool(name="keep", bufs=1))
         ring2 = ctx.enter_context(tc.tile_pool(name="ring2", bufs=2))
         w_ring = ctx.enter_context(tc.tile_pool(name="w_ring", bufs=W_BUFS))
-        psum = ctx.enter_context(tc.psum_pool(name="psum", bufs=8))
+        psum = ctx.enter_context(tc.psum_pool(name="psum", bufs=BANKS))
 
         offs_sb = keep.tile([P, S // PER_COLUMN], U16, name="offs_sb")
         pos1_sb = keep.tile([P, T // PER_COLUMN], U16, name="pos1_sb")
         pos2_sb = keep.tile([P, T // PER_COLUMN], U16, name="pos2_sb")
         bias = keep.tile([P, E], F32, name="bias")
-        gate_first = keep.tile([P, A], F32, name="gate_first", align_bytes=64)
-        gate_rest = keep.tile([P, S - A], F32, name="gate_rest")
-        rows = [
-            [keep.tile([P, T + SPARE], F32, name="rows%d%d" % (g, j), align_bytes=64) for j in range(PACK)]
+        gate_first = keep.tile([P, SECOND], F32, name="gate_first", align_bytes=64)
+        gate_second = keep.tile([P, S - SECOND], F32, name="gate_second")
+        planes = [
+            [keep.tile([P, T + SPARE], F32, name="plane%d%d" % (g, j), align_bytes=64) for j in range(PACK)]
             for g in range(PASSES)
         ]
-        results = []
 
         x_view = xT.rearrange("(g p j) t -> g j p t", g=PASSES, j=PACK)
         w_view = w.rearrange("e (g p j) n -> p (e g) (j n)", g=PASSES, j=PACK)
         w_raw = {}
         gathered = {}
-        x_ops = {}
-        w_ops = {}
+        x_operands = {}
+        w_operands = {}
         sums = {}
 
-        def load_rows(g, j):
-            nc.sync.dma_start(rows[g][j][:, :T], x_view[g, j])
+        def load_plane(g, j):
+            nc.sync.dma_start(planes[g][j][:, :T], x_view[g, j])
 
         def load_w(e):
             w_raw[e] = w_ring.tile([P, PASSES, PACK * N], F32, name="w_raw")
@@ -106,165 +112,172 @@ def tile_moe_pre_lin_silu_kernel(tc, xT, w, b, gate, offs, pos1, pos2, out):
             for j, a, z in order:
                 nc.vector.tensor_tensor(
                     gathered[g, lo][:, j, a - lo : z - lo],
-                    rows[g][j][:].indirect(offs_sb[:, a // PER_COLUMN : z // PER_COLUMN]),
-                    gate_first[:, a:z] if lo < A else gate_rest[:, a - A : z - A],
+                    planes[g][j][:].indirect(offs_sb[:, a // PER_COLUMN : z // PER_COLUMN]),
+                    gate_first[:, a:z] if lo < SECOND else gate_second[:, a - SECOND : z - SECOND],
                     MULT,
                 )
 
-        def round_x(g, lo, a, z, rounded):
+        def round_x(g, lo, a, z, rounded, word):
             nc.scalar.copy(
-                rounded[:, : (z - a) * PACK].rearrange("p (c i j) -> p c j i", i=RUN, j=PACK),
+                rounded[:, word * PACK : (word + z - a) * PACK].rearrange("p (c i j) -> p c j i", i=RUN, j=PACK),
                 gathered[g, lo][:, :, a - lo : z - lo].rearrange("p j (c i) -> p c j i", i=RUN),
             )
 
-        def quantize(rounded, a, z, operand, at):
+        def quantize(rounded, a, z, operand, word):
             codes, scales = operand
             nc.vector.quantize_mx(
-                out=codes[:, at : at + z - a].bitcast(FP8X4),
-                scales=scales[:, at : at + z - a],
+                out=codes[:, word : word + z - a].bitcast(FP8X4),
+                scales=scales[:, word : word + z - a],
                 in_=rounded[:, a * PACK : z * PACK],
             )
 
-        def name_x(g, lo, hi, operand):
-            for e in range(lo // C, hi // C):
-                x_ops[g, e] = [t[:, e * C - lo : (e + 1) * C - lo] for t in operand]
-
-        def name_w(e0, e1, operand, at):
+        def name_x(g, e0, e1, operand, word):
             for e in range(e0, e1):
-                a = at + (e - e0) * W_WORDS
-                w_ops[e] = [t[:, a : a + W_WORDS] for t in operand]
+                a = word + (e - e0) * C
+                x_operands[g, e] = [part[:, a : a + C] for part in operand]
+
+        def name_w(e0, e1, operand, word):
+            for e in range(e0, e1):
+                a = word + (e - e0) * W_WORDS
+                w_operands[e] = [part[:, a : a + W_WORDS] for part in operand]
 
         def multiply(g, e, lo, hi):
             if g == 0:
                 sums[e, lo] = psum.tile([P, hi - lo], F32, name="acc")
             nc.tensor.matmul_mx(
                 out=sums[e, lo][:],
-                lhsT=w_ops[e][0][:, g * N : (g + 1) * N].bitcast(FP8X4),
-                lhsT_scale=w_ops[e][1][:, g * N : (g + 1) * N],
-                rhs=x_ops[g, e][0][:, lo:hi].bitcast(FP8X4),
-                rhs_scale=x_ops[g, e][1][:, lo:hi],
+                lhsT=w_operands[e][0][:, g * N : (g + 1) * N].bitcast(FP8X4),
+                lhsT_scale=w_operands[e][1][:, g * N : (g + 1) * N],
+                rhs=x_operands[g, e][0][:, lo:hi].bitcast(FP8X4),
+                rhs_scale=x_operands[g, e][1][:, lo:hi],
                 start=(g == 0),
                 stop=(g == PASSES - 1),
             )
             if g == PASSES - 1:
-                nc.scalar.activation(results[0][:, e * C + lo : e * C + hi], sums[e, lo][:], SILU, bias=bias[:, e : e + 1])
+                nc.scalar.activation(y[:, e * C + lo : e * C + hi], sums[e, lo][:], SILU, bias=bias[:, e : e + 1])
 
         def experts(e0, e1):
             for e in range(e0, e1):
                 for g in range(PASSES):
                     multiply(g, e, 0, C)
 
-        for g in range(PASSES):
-            for j in range(PACK):
-                nc.gpsimd.memset(rows[g][j][:, T:], 0.0)
-
-        load_rows(0, 0)
-        nc.sync.dma_start(offs_sb[:], offs)
-        for a, z in spans(GATE_PIECES):
-            nc.sync.dma_start(gate_first[:, a:z], gate[0:P, a:z])
-        load_rows(0, 1)
-        load_rows(0, 2)
-        for e in range(3):
-            load_w(e)
-        load_rows(0, 3)
-        load_w(3)
-        load_rows(1, 0)
-        load_w(4)
-        load_rows(1, 1)
-        load_rows(1, 2)
-        load_w(5)
-
-        rounded_a0 = rounded_tile(ring2, A + 2 * W_WORDS, "rounded")
-        rounded_a1 = rounded_tile(ring2, A + 2 * W_WORDS, "rounded")
-        round_w(0, rounded_a0, A)
-        load_w(6)
-        load_rows(1, 3)
-        round_w(1, rounded_a0, A + W_WORDS)
-        load_w(7)
-        nc.sync.dma_start(gate_rest[:], gate[0:P, A:S])
-        nc.sync.dma_start(bias[:], b)
-        nc.sync.dma_start(pos1_sb[:], pos1)
-        nc.sync.dma_start(pos2_sb[:], pos2)
-        round_w(2, rounded_a1, A)
-        load_w(8)
-        round_w(3, rounded_a1, A + W_WORDS)
-        load_w(9)
-        gather(0, 0, A)
-        round_x(0, 0, 0, A, rounded_a0)
-        rounded_w4 = rounded_tile(keep, 2 * W_WORDS, "rounded_w4")
-        rounded_b0 = rounded_tile(keep, 6 * (C + W_WORDS), "rounded_b0")
-        blocks = [(6, 8), (8, 10), (10, 11), (11, 12)]
-
-        def block_at(e0):
-            return (e0 - 6) * (C + W_WORDS)
+        def block_word(e0):
+            return (e0 - GROUP) * (C + W_WORDS)
 
         def round_block_w(e0, e1):
             for e in range(e0, e1):
-                round_w(e, rounded_b0, block_at(e0) + (e1 - e0) * C + (e - e0) * W_WORDS)
-                if e + W_BUFS < E:
-                    load_w(e + W_BUFS)
+                round_w(e, rounded_blocks, block_word(e0) + (e1 - e0) * C + (e - e0) * W_WORDS)
 
-        def quantize_block(e0, e1, operand, at):
-            quantize(rounded_b0, block_at(e0), block_at(e1), operand, at)
-            name_x(0, e0 * C, e1 * C, [t[:, at:] for t in operand])
-            name_w(e0, e1, operand, at + (e1 - e0) * C)
+        def quantize_block(e0, e1, operand, word):
+            quantize(rounded_blocks, block_word(e0), block_word(e1), operand, word)
+            name_x(0, e0, e1, operand, word)
+            name_w(e0, e1, operand, word + (e1 - e0) * C)
 
-        for e in range(4, 6):
-            round_w(e, rounded_w4, (e - 4) * W_WORDS)
+        for g in range(PASSES):
+            for j in range(PACK):
+                nc.gpsimd.memset(planes[g][j][:, T:], 0.0)
+
+        load_plane(0, 0)
+        nc.sync.dma_start(offs_sb[:], offs)
+        for a, z in spans(GATE_PIECES):
+            nc.sync.dma_start(gate_first[:, a:z], gate[0:P, a:z])
+        load_plane(0, 1)
+        load_plane(0, 2)
+        for e in range(3):
+            load_w(e)
+        load_plane(0, 3)
+        load_w(3)
+        load_plane(1, 0)
+        load_w(4)
+        load_plane(1, 1)
+        load_plane(1, 2)
+        load_w(5)
+
+        rounded_first = [rounded_tile(ring2, 2 * WIDEST, "rounded") for g in range(PASSES)]
+        round_w(0, rounded_first[0], SECOND)
+        load_w(W_BUFS)
+        load_plane(1, 3)
+        round_w(1, rounded_first[0], SECOND + W_WORDS)
+        load_w(1 + W_BUFS)
+        nc.sync.dma_start(gate_second[:], gate[0:P, SECOND:S])
+        nc.sync.dma_start(bias[:], b)
+        nc.sync.dma_start(pos1_sb[:], pos1)
+        nc.sync.dma_start(pos2_sb[:], pos2)
+        for e in range(RIDERS, 2 * RIDERS):
+            round_w(e, rounded_first[1], SECOND + (e - RIDERS) * W_WORDS)
             load_w(e + W_BUFS)
-        round_block_w(*blocks[0])
-        gather(1, 0, A)
-        round_x(1, 0, 0, A, rounded_a1)
-        early = operand_tiles(A + 4 * W_WORDS, "codes_early", "scales_early")
-        quantize(rounded_a0, 0, 1024, early, 0)
-        quantize(rounded_a0, 1024, 2048, early, 1024)
-        quantize(rounded_w4, 0, 512, early, 2048)
-        name_x(0, 0, A, early)
-        name_w(0, 2, early, A)
-        name_w(4, 6, early, 2048)
-        for block in blocks[1:]:
+        gather(0, 0, SECOND)
+        round_x(0, 0, 0, SECOND, rounded_first[0], 0)
+        rounded_rest_w = rounded_tile(keep, (GROUP - 2 * RIDERS) * W_WORDS, "rounded_rest_w")
+        rounded_blocks = rounded_tile(keep, block_word(E), "rounded_blocks")
+        for e in range(2 * RIDERS, GROUP):
+            round_w(e, rounded_rest_w, (e - 2 * RIDERS) * W_WORDS)
+            load_w(e + W_BUFS)
+        round_block_w(*BLOCKS[0])
+        gather(1, 0, SECOND)
+        round_x(1, 0, 0, SECOND, rounded_first[1], 0)
+        rest_words = (GROUP - 2 * RIDERS) * W_WORDS
+        first0 = operand_tiles(2 * WIDEST + rest_words, "codes_first0", "scales_first0")
+        for a, z in halves(0, 2 * WIDEST):
+            quantize(rounded_first[0], a, z, first0, a)
+        quantize(rounded_rest_w, 0, rest_words, first0, 2 * WIDEST)
+        name_x(0, 0, GROUP, first0, 0)
+        name_w(0, RIDERS, first0, SECOND)
+        name_w(2 * RIDERS, GROUP, first0, 2 * WIDEST)
+        for block in BLOCKS[1:]:
             round_block_w(*block)
 
-        gather(0, A, S)
-        for e0, e1 in blocks:
-            round_x(0, A, e0 * C, e1 * C, rounded_b0[:, block_at(e0) * PACK :])
-        op_a1 = operand_tiles(2048, "codes_a1", "scales_a1")
-        quantize(rounded_a1, 0, 1024, op_a1, 0)
-        quantize(rounded_a1, 1024, 2048, op_a1, 1024)
-        name_x(1, 0, A, op_a1)
-        name_w(2, 4, op_a1, A)
-        y = keep.tile([P, S], F32, name="rows02", align_bytes=64)
-        results.append(y)
-        experts(0, 6)
-        gather(1, A, B)
-        rounded_b1 = rounded_tile(ring2, B - A, "rounded")
-        round_x(1, A, A, B, rounded_b1)
-        op_b0 = operand_tiles(block_at(E - 1), "gate_first", "scales_b0")
-        for e0, e1 in blocks[:3]:
-            quantize_block(e0, e1, op_b0, block_at(e0))
-        gather(1, B, LAST)
-        rounded_b2 = rounded_tile(ring2, C, "rounded")
-        round_x(1, B, B, LAST, rounded_b2)
-        op_b1 = operand_tiles(S - A, "rows03", "scales_b1")
-        name_x(1, A, S, op_b1)
-        quantize(rounded_b1, 0, B - A, op_b1, 0)
-        experts(6, 10)
+        gather(0, SECOND, S)
+        for e0, e1 in BLOCKS:
+            round_x(0, SECOND, e0 * C, e1 * C, rounded_blocks, block_word(e0))
+        first1 = operand_tiles(2 * WIDEST, "codes_first1", "scales_first1")
+        for a, z in halves(0, 2 * WIDEST):
+            quantize(rounded_first[1], a, z, first1, a)
+        name_x(1, 0, GROUP, first1, 0)
+        name_w(RIDERS, 2 * RIDERS, first1, SECOND)
+        y = keep.tile([P, S], F32, name="plane02", align_bytes=64)
+        experts(0, GROUP)
+
+        gather(1, SECOND, LAST_BUT_ONE)
+        rounded_long = rounded_tile(ring2, LAST_BUT_ONE - SECOND, "rounded")
+        round_x(1, SECOND, SECOND, LAST_BUT_ONE, rounded_long, 0)
+        second0 = operand_tiles(block_word(E - 1), "gate_first", "scales_second0")
+        for e0, e1 in BLOCKS[:-1]:
+            quantize_block(e0, e1, second0, block_word(e0))
+        gather(1, LAST_BUT_ONE, LAST)
+        rounded_short = rounded_tile(ring2, C, "rounded")
+        round_x(1, LAST_BUT_ONE, LAST_BUT_ONE, LAST, rounded_short, 0)
+        second1 = operand_tiles(S - SECOND, "plane03", "scales_second1")
+        name_x(1, GROUP, E, second1, 0)
+        quantize(rounded_long, 0, LAST_BUT_ONE - SECOND, second1, 0)
+        experts(GROUP, E - 2)
         multiply(0, E - 2, 0, C)
+        unread = psum.tile([P, 2 * C], F32, name="acc")
+        for a, z in halves(0, LAST_BUT_ONE - SECOND):
+            nc.tensor.matmul_mx(
+                out=unread[:],
+                lhsT=w_operands[E - 2][0][:, N:].bitcast(FP8X4),
+                lhsT_scale=w_operands[E - 2][1][:, N:],
+                rhs=second1[0][:, a:z].bitcast(FP8X4),
+                rhs_scale=second1[1][:, a:z],
+                start=True,
+                stop=True,
+            )
         gather(1, LAST, S)
         rounded_last = rounded_tile(ring2, C, "rounded")
-        for lo, hi in halves(LAST, S):
-            round_x(1, LAST, lo, hi, rounded_last[:, (lo - LAST) * PACK :])
-        quantize(rounded_b2, 0, C, op_b1, B - A)
+        for a, z in halves(LAST, S):
+            round_x(1, LAST, a, z, rounded_last, a - LAST)
+        quantize(rounded_short, 0, C, second1, LAST_BUT_ONE - SECOND)
         multiply(1, E - 2, 0, C)
-        quantize_block(E - 1, E, operand_tiles(C + W_WORDS, "rows10", "scales_11"), 0)
+        quantize_block(*BLOCKS[-1], operand_tiles(C + W_WORDS, "plane10", "scales_last"), 0)
         for lo, hi in halves(0, C):
             multiply(0, E - 1, lo, hi)
         for lo, hi in halves(0, C):
-            quantize(rounded_last, lo, hi, op_b1, LAST - A + lo)
+            quantize(rounded_last, lo, hi, second1, LAST - SECOND + lo)
             multiply(1, E - 1, lo, hi)
 
-        first = keep.tile([P, T], F32, name="rows00", align_bytes=64)
-        total = keep.tile([P, T], F32, name="rows01", align_bytes=64)
+        first = keep.tile([P, T], F32, name="plane00", align_bytes=64)
+        total = keep.tile([P, T], F32, name="plane01", align_bytes=64)
         for lo, hi in spans(FIRST_PIECES):
             nc.vector.tensor_copy(first[:, lo:hi], y[:].indirect(pos1_sb[:, lo // PER_COLUMN : hi // PER_COLUMN]))
         for lo, hi in spans(TOKEN_PIECES):

@@ -1,6 +1,7 @@
 from contextlib import ExitStack
 
 import concourse.mybir as mybir
+from concourse.masks import make_identity
 
 K, T, E, C, N = 1024, 1536, 12, 256, 128
 S = E * C
@@ -15,6 +16,7 @@ U8 = mybir.dt.uint8
 FP8X4 = mybir.dt.float8_e4m3fn_x4
 MULT = mybir.AluOpType.mult
 ADD = mybir.AluOpType.add
+COPY = mybir.ActivationFunctionType.Copy
 SILU = mybir.ActivationFunctionType.Silu
 
 P = 128
@@ -23,21 +25,17 @@ PASSES = K // (P * PACK)
 PER_COLUMN = 16
 RUN = 4
 W_WORDS = PASSES * N
-WIDEST = 1024
-
-GROUP = E // 2
-SECOND = GROUP * C
-LAST_BUT_ONE = (E - 2) * C
-LAST = (E - 1) * C
-RIDERS = (2 * WIDEST - SECOND) // W_WORDS
-BLOCKS = ((6, 8), (8, 10), (10, 11), (11, 12))
-WHOLE = 2
-SPARE = 16
-GATE_PIECES = (192, 448, 896)
-FIRST_PIECES = (768, 768)
-TOKEN_PIECES = (768, 384, 256, 128)
+BLOCK = 512
+BLOCKS = S // BLOCK
+VECTOR_SLOTS = 1280
+SCALAR_CHUNKS = (
+    ((VECTOR_SLOTS, 2048, "b"), (2048, S, "c")),
+    ((0, 1024, "d"), (1024, 2048, "a"), (2048, 2560, "b"), (2560, S, "c")),
+)
+TOKEN_PIECES = (256, 256, 256, 256, 256, 128, 128)
 W_BUFS = 6
-BANKS = 8
+ROUNDED_BUFS = 3
+DOUBLE_RIDERS = 2
 
 
 def spans(widths):
@@ -48,239 +46,204 @@ def spans(widths):
     return result
 
 
-def halves(lo, hi):
-    return [(lo, (lo + hi) // 2), ((lo + hi) // 2, hi)]
-
-
 def tile_moe_pre_lin_silu_kernel(tc, xT, w, b, gate, offs, pos1, pos2, out):
     nc = tc.nc
     with ExitStack() as ctx:
         keep = ctx.enter_context(tc.tile_pool(name="keep", bufs=1))
-        ring2 = ctx.enter_context(tc.tile_pool(name="ring2", bufs=2))
+        rounded_ring = ctx.enter_context(tc.tile_pool(name="rounded_ring", bufs=ROUNDED_BUFS))
         w_ring = ctx.enter_context(tc.tile_pool(name="w_ring", bufs=W_BUFS))
-        psum = ctx.enter_context(tc.psum_pool(name="psum", bufs=BANKS))
+        psum = ctx.enter_context(tc.psum_pool(name="psum", bufs=1))
 
         offs_sb = keep.tile([P, S // PER_COLUMN], U16, name="offs_sb")
         pos1_sb = keep.tile([P, T // PER_COLUMN], U16, name="pos1_sb")
         pos2_sb = keep.tile([P, T // PER_COLUMN], U16, name="pos2_sb")
         bias = keep.tile([P, E], F32, name="bias")
-        gate_first = keep.tile([P, SECOND], F32, name="gate_first", align_bytes=64)
-        gate_second = keep.tile([P, S - SECOND], F32, name="gate_second")
+        identity = keep.tile([P, P], F32, name="identity")
+        gate_rows = keep.tile([P, P], F32, name="gate_rows")
+        gate_columns = keep.tile([P, S // P], F32, name="gate_columns")
         planes = [
-            [keep.tile([P, T + SPARE], F32, name="plane%d%d" % (g, j), align_bytes=64) for j in range(PACK)]
+            [keep.tile([P, T], F32, name="plane%d%d" % (g, j), align_bytes=64) for j in range(PACK)]
             for g in range(PASSES)
         ]
+        x_codes = keep.tile([P, PASSES * S], U32, name="x_codes", align_bytes=64)
+        x_scales = keep.tile([P, PASSES * S], U8, name="x_scales", align_bytes=64)
+        w_codes = keep.tile([P, E * W_WORDS], U32, name="w_codes", align_bytes=64)
+        w_scales = keep.tile([P, E * W_WORDS], U8, name="w_scales", align_bytes=64)
+        y = keep.tile([P, S], F32, name="y", align_bytes=64)
 
         x_view = xT.rearrange("(g p j) t -> g j p t", g=PASSES, j=PACK)
         w_view = w.rearrange("e (g p j) n -> p (e g) (j n)", g=PASSES, j=PACK)
         w_raw = {}
-        gathered = {}
-        x_operands = {}
-        w_operands = {}
-        sums = {}
+        chunks = [[], []]
+        rounded = {}
 
         def load_plane(g, j):
-            nc.sync.dma_start(planes[g][j][:, :T], x_view[g, j])
+            nc.sync.dma_start(planes[g][j][:], x_view[g, j])
 
         def load_w(e):
             w_raw[e] = w_ring.tile([P, PASSES, PACK * N], F32, name="w_raw")
             nc.sync.dma_start(w_raw[e][:], w_view[:, PASSES * e : PASSES * (e + 1), :])
 
-        def rounded_tile(pool, words, name):
-            return pool.tile([P, words * PACK], BF16, name=name, align_bytes=64)
+        def new_chunk(g, lo, hi, buffer):
+            tile = keep.tile([P, PACK, hi - lo], F32, name="gathered_" + buffer, align_bytes=64)
+            chunks[g].append((lo, hi, tile))
+            return tile
 
-        def operand_tiles(words, codes_name, scales_name):
-            codes = keep.tile([P, words], U32, name=codes_name, align_bytes=64)
-            scales = keep.tile([P, words], U8, name=scales_name, align_bytes=64)
-            return codes, scales
+        def window(g, j, lo, hi):
+            return planes[g][j][:].indirect(offs_sb[:, lo // PER_COLUMN : hi // PER_COLUMN])
 
-        def round_w(e, rounded, word):
-            nc.scalar.copy(
-                rounded[:, word * PACK : (word + W_WORDS) * PACK].rearrange(
-                    "p (g c i j) -> p g c j i", g=PASSES, i=RUN, j=PACK
-                ),
-                w_raw[e][:].rearrange("p g (j c i) -> p g c j i", i=RUN, j=PACK),
-            )
+        def scalar_chunk(g, index):
+            lo, hi, buffer = SCALAR_CHUNKS[g][index]
+            tile = new_chunk(g, lo, hi, buffer)
+            for j in range(PACK):
+                nc.scalar.activation(tile[:, j, :], window(g, j, lo, hi), COPY)
 
-        def gather(g, lo, hi):
-            gathered[g, lo] = ring2.tile([P, PACK, hi - lo], F32, name="gathered")
-            order = [(j, lo, hi) for j in range(PACK)]
-            if (g, lo) == (0, 0):
-                order = [(0, a, z) for a, z in spans(GATE_PIECES)] + order[1:]
-            if (g, lo) == (PASSES - 1, LAST):
-                order = order[:WHOLE] + [(j, a, z) for a, z in halves(lo, hi) for j in range(WHOLE, PACK)]
-            for j, a, z in order:
-                nc.vector.tensor_tensor(
-                    gathered[g, lo][:, j, a - lo : z - lo],
-                    planes[g][j][:].indirect(offs_sb[:, a // PER_COLUMN : z // PER_COLUMN]),
-                    gate_first[:, a:z] if lo < SECOND else gate_second[:, a - SECOND : z - SECOND],
-                    MULT,
-                )
+        def riders(unit):
+            if unit < DOUBLE_RIDERS:
+                return range(2 * unit, 2 * unit + 2)
+            return range(min(unit + DOUBLE_RIDERS, E), min(unit + DOUBLE_RIDERS + 1, E))
 
-        def round_x(g, lo, a, z, rounded, word):
-            nc.scalar.copy(
-                rounded[:, word * PACK : (word + z - a) * PACK].rearrange("p (c i j) -> p c j i", i=RUN, j=PACK),
-                gathered[g, lo][:, :, a - lo : z - lo].rearrange("p j (c i) -> p c j i", i=RUN),
-            )
+        def open_unit(unit):
+            rounded[unit] = rounded_ring.tile([P, 2 * BLOCK * PACK], BF16, name="rounded", align_bytes=64)
+            for place, e in enumerate(riders(unit)):
+                for g in range(PASSES):
+                    word = BLOCK + place * W_WORDS + g * N
+                    nc.gpsimd.tensor_scalar(
+                        rounded[unit][:, word * PACK : (word + N) * PACK].rearrange("p (n j) -> p n j", j=PACK),
+                        w_raw[e][:, g, :].rearrange("p (j n) -> p n j", j=PACK),
+                        1.0,
+                        0.0,
+                        MULT,
+                        ADD,
+                    )
+                if e + W_BUFS < E:
+                    load_w(e + W_BUFS)
 
-        def quantize(rounded, a, z, operand, word):
-            codes, scales = operand
+        def times_gate(unit, lo, hi):
+            g, block = divmod(unit, BLOCKS)
+            base = block * BLOCK
+            for first, end, tile in chunks[g]:
+                a, z = max(lo, first), min(hi, end)
+                if a < z:
+                    nc.vector.tensor_tensor(
+                        rounded[unit][:, (a - base) * PACK : (z - base) * PACK].rearrange(
+                            "p (c i j) -> p c j i", i=RUN, j=PACK
+                        ),
+                        tile[:, :, a - first : z - first].rearrange("p j (c i) -> p c j i", i=RUN),
+                        gate_banks[block][:, a - base : z - base]
+                        .rearrange("p (c i) -> p c i", i=RUN)
+                        .unsqueeze(2)
+                        .to_broadcast([P, (z - a) // RUN, PACK, RUN]),
+                        MULT,
+                    )
+
+        def quantize(source, a, z, codes, scales, word):
             nc.vector.quantize_mx(
                 out=codes[:, word : word + z - a].bitcast(FP8X4),
                 scales=scales[:, word : word + z - a],
-                in_=rounded[:, a * PACK : z * PACK],
+                in_=source[:, a * PACK : z * PACK],
             )
 
-        def name_x(g, e0, e1, operand, word):
-            for e in range(e0, e1):
-                a = word + (e - e0) * C
-                x_operands[g, e] = [part[:, a : a + C] for part in operand]
+        def quantize_x(unit, lo, hi):
+            g, block = divmod(unit, BLOCKS)
+            quantize(rounded[unit], lo - block * BLOCK, hi - block * BLOCK, x_codes, x_scales, g * S + lo)
 
-        def name_w(e0, e1, operand, word):
-            for e in range(e0, e1):
-                a = word + (e - e0) * W_WORDS
-                w_operands[e] = [part[:, a : a + W_WORDS] for part in operand]
+        def quantize_riders(unit):
+            along = riders(unit)
+            if len(along):
+                quantize(rounded[unit], BLOCK, BLOCK + len(along) * W_WORDS, w_codes, w_scales, along[0] * W_WORDS)
 
-        def multiply(g, e, lo, hi):
-            if g == 0:
-                sums[e, lo] = psum.tile([P, hi - lo], F32, name="acc")
-            nc.tensor.matmul_mx(
-                out=sums[e, lo][:],
-                lhsT=w_operands[e][0][:, g * N : (g + 1) * N].bitcast(FP8X4),
-                lhsT_scale=w_operands[e][1][:, g * N : (g + 1) * N],
-                rhs=x_operands[g, e][0][:, lo:hi].bitcast(FP8X4),
-                rhs_scale=x_operands[g, e][1][:, lo:hi],
-                start=(g == 0),
-                stop=(g == PASSES - 1),
-            )
-            if g == PASSES - 1:
-                nc.scalar.activation(y[:, e * C + lo : e * C + hi], sums[e, lo][:], SILU, bias=bias[:, e : e + 1])
+        def multiply(lo, hi, sums):
+            e = lo // C
+            for g in range(PASSES):
+                a = e * W_WORDS + g * N
+                nc.tensor.matmul_mx(
+                    out=sums,
+                    lhsT=w_codes[:, a : a + N].bitcast(FP8X4),
+                    lhsT_scale=w_scales[:, a : a + N],
+                    rhs=x_codes[:, g * S + lo : g * S + hi].bitcast(FP8X4),
+                    rhs_scale=x_scales[:, g * S + lo : g * S + hi],
+                    start=(g == 0),
+                    stop=(g == PASSES - 1),
+                )
 
-        def experts(e0, e1):
-            for e in range(e0, e1):
-                for g in range(PASSES):
-                    multiply(g, e, 0, C)
+        def activate(lo, hi, sums):
+            e = lo // C
+            nc.scalar.activation(y[:, lo:hi], sums, SILU, bias=bias[:, e : e + 1])
 
-        def block_word(e0):
-            return (e0 - GROUP) * (C + W_WORDS)
-
-        def round_block_w(e0, e1):
-            for e in range(e0, e1):
-                round_w(e, rounded_blocks, block_word(e0) + (e1 - e0) * C + (e - e0) * W_WORDS)
-
-        def quantize_block(e0, e1, operand, word):
-            quantize(rounded_blocks, block_word(e0), block_word(e1), operand, word)
-            name_x(0, e0, e1, operand, word)
-            name_w(e0, e1, operand, word + (e1 - e0) * C)
-
-        for g in range(PASSES):
-            for j in range(PACK):
-                nc.gpsimd.memset(planes[g][j][:, T:], 0.0)
+        nc.gpsimd.memset(gate_rows[:], 0.0)
+        make_identity(nc, identity[:])
 
         load_plane(0, 0)
         nc.sync.dma_start(offs_sb[:], offs)
-        for a, z in spans(GATE_PIECES):
-            nc.sync.dma_start(gate_first[:, a:z], gate[0:P, a:z])
         load_plane(0, 1)
+        nc.sync.dma_start(gate_rows[0 : S // P, :], gate[0, :].rearrange("(c s) -> c s", s=P))
+        load_w(0)
         load_plane(0, 2)
-        for e in range(3):
-            load_w(e)
+        load_w(1)
         load_plane(0, 3)
+        load_w(2)
         load_w(3)
-        load_plane(1, 0)
+        for j in range(PACK):
+            load_plane(1, j)
         load_w(4)
-        load_plane(1, 1)
-        load_plane(1, 2)
         load_w(5)
-
-        rounded_first = [rounded_tile(ring2, 2 * WIDEST, "rounded") for g in range(PASSES)]
-        round_w(0, rounded_first[0], SECOND)
-        load_w(W_BUFS)
-        load_plane(1, 3)
-        round_w(1, rounded_first[0], SECOND + W_WORDS)
-        load_w(1 + W_BUFS)
-        nc.sync.dma_start(gate_second[:], gate[0:P, SECOND:S])
         nc.sync.dma_start(bias[:], b)
         nc.sync.dma_start(pos1_sb[:], pos1)
         nc.sync.dma_start(pos2_sb[:], pos2)
-        for e in range(RIDERS, 2 * RIDERS):
-            round_w(e, rounded_first[1], SECOND + (e - RIDERS) * W_WORDS)
-            load_w(e + W_BUFS)
-        gather(0, 0, SECOND)
-        round_x(0, 0, 0, SECOND, rounded_first[0], 0)
-        rounded_rest_w = rounded_tile(keep, (GROUP - 2 * RIDERS) * W_WORDS, "rounded_rest_w")
-        rounded_blocks = rounded_tile(keep, block_word(E), "rounded_blocks")
-        for e in range(2 * RIDERS, GROUP):
-            round_w(e, rounded_rest_w, (e - 2 * RIDERS) * W_WORDS)
-            load_w(e + W_BUFS)
-        round_block_w(*BLOCKS[0])
-        gather(1, 0, SECOND)
-        round_x(1, 0, 0, SECOND, rounded_first[1], 0)
-        rest_words = (GROUP - 2 * RIDERS) * W_WORDS
-        first0 = operand_tiles(2 * WIDEST + rest_words, "codes_first0", "scales_first0")
-        for a, z in halves(0, 2 * WIDEST):
-            quantize(rounded_first[0], a, z, first0, a)
-        quantize(rounded_rest_w, 0, rest_words, first0, 2 * WIDEST)
-        name_x(0, 0, GROUP, first0, 0)
-        name_w(0, RIDERS, first0, SECOND)
-        name_w(2 * RIDERS, GROUP, first0, 2 * WIDEST)
-        for block in BLOCKS[1:]:
-            round_block_w(*block)
 
-        gather(0, SECOND, S)
-        for e0, e1 in BLOCKS:
-            round_x(0, SECOND, e0 * C, e1 * C, rounded_blocks, block_word(e0))
-        first1 = operand_tiles(2 * WIDEST, "codes_first1", "scales_first1")
-        for a, z in halves(0, 2 * WIDEST):
-            quantize(rounded_first[1], a, z, first1, a)
-        name_x(1, 0, GROUP, first1, 0)
-        name_w(RIDERS, 2 * RIDERS, first1, SECOND)
-        y = keep.tile([P, S], F32, name="plane02", align_bytes=64)
-        experts(0, GROUP)
+        own = new_chunk(0, 0, VECTOR_SLOTS, "a")
+        others = [(lo, hi, new_chunk(0, lo, hi, buffer)) for lo, hi, buffer in SCALAR_CHUNKS[0]]
+        for j in range(PACK):
+            nc.vector.tensor_copy(own[:, j, :], window(0, j, 0, VECTOR_SLOTS))
+            for lo, hi, tile in others:
+                nc.scalar.activation(tile[:, j, :], window(0, j, lo, hi), COPY)
 
-        gather(1, SECOND, LAST_BUT_ONE)
-        rounded_long = rounded_tile(ring2, LAST_BUT_ONE - SECOND, "rounded")
-        round_x(1, SECOND, SECOND, LAST_BUT_ONE, rounded_long, 0)
-        second0 = operand_tiles(block_word(E - 1), "gate_first", "scales_second0")
-        for e0, e1 in BLOCKS[:-1]:
-            quantize_block(e0, e1, second0, block_word(e0))
-        gather(1, LAST_BUT_ONE, LAST)
-        rounded_short = rounded_tile(ring2, C, "rounded")
-        round_x(1, LAST_BUT_ONE, LAST_BUT_ONE, LAST, rounded_short, 0)
-        second1 = operand_tiles(S - SECOND, "plane03", "scales_second1")
-        name_x(1, GROUP, E, second1, 0)
-        quantize(rounded_long, 0, LAST_BUT_ONE - SECOND, second1, 0)
-        experts(GROUP, E - 2)
-        multiply(0, E - 2, 0, C)
-        unread = psum.tile([P, 2 * C], F32, name="acc")
-        for a, z in halves(0, LAST_BUT_ONE - SECOND):
-            nc.tensor.matmul_mx(
-                out=unread[:],
-                lhsT=w_operands[E - 2][0][:, N:].bitcast(FP8X4),
-                lhsT_scale=w_operands[E - 2][1][:, N:],
-                rhs=second1[0][:, a:z].bitcast(FP8X4),
-                rhs_scale=second1[1][:, a:z],
-                start=True,
-                stop=True,
+        turned = psum.tile([P, P], F32, name="spare0")
+        nc.tensor.transpose(turned[:], gate_rows[:], identity[:])
+        nc.vector.tensor_copy(gate_columns[:], turned[:, 0 : S // P])
+        gate_banks = [psum.tile([P, BLOCK], F32, name="bank%d" % block) for block in range(BLOCKS)]
+        for c in range(S // P):
+            block, place = divmod(c * P, BLOCK)
+            nc.tensor.transpose(
+                gate_banks[block][:, place : place + P], gate_columns[:, c : c + 1].to_broadcast([P, P]), identity[:]
             )
-        gather(1, LAST, S)
-        rounded_last = rounded_tile(ring2, C, "rounded")
-        for a, z in halves(LAST, S):
-            round_x(1, LAST, a, z, rounded_last, a - LAST)
-        quantize(rounded_short, 0, C, second1, LAST_BUT_ONE - SECOND)
-        multiply(1, E - 2, 0, C)
-        quantize_block(*BLOCKS[-1], operand_tiles(C + W_WORDS, "plane10", "scales_last"), 0)
-        for lo, hi in halves(0, C):
-            multiply(0, E - 1, lo, hi)
-        for lo, hi in halves(0, C):
-            quantize(rounded_last, lo, hi, second1, LAST - SECOND + lo)
-            multiply(1, E - 1, lo, hi)
+
+        scalar_chunk(1, 0)
+        last = PASSES * BLOCKS - 1
+        for unit in range(ROUNDED_BUFS):
+            open_unit(unit)
+        times_gate(0, 0, BLOCK)
+        for unit in range(last):
+            g, block = divmod(unit, BLOCKS)
+            ahead = (unit + 1) % BLOCKS * BLOCK
+            times_gate(unit + 1, ahead, ahead + (BLOCK if unit + 1 < last else C))
+            if unit + 1 in (2, 3, 5):
+                scalar_chunk(1, (2, 3, 5).index(unit + 1) + 1)
+            quantize_x(unit, block * BLOCK, (block + 1) * BLOCK)
+            quantize_riders(unit)
+            if unit + ROUNDED_BUFS <= last:
+                open_unit(unit + ROUNDED_BUFS)
+            if g == PASSES - 1:
+                sums = psum.tile([P, BLOCK], F32, name="bank%d" % block)
+                for place in range(0, BLOCK, C):
+                    multiply(block * BLOCK + place, block * BLOCK + place + C, sums[:, place : place + C])
+                for place in range(0, BLOCK, C):
+                    activate(block * BLOCK + place, block * BLOCK + place + C, sums[:, place : place + C])
+
+        ends = ((S - 2 * C, S - C, "spare0"), (S - C, S - C // 2, "spare1"), (S - C // 2, S, "bank0"))
+        for index, (lo, hi, bank) in enumerate(ends):
+            if index + 1 < len(ends):
+                times_gate(last, ends[index + 1][0], ends[index + 1][1])
+            quantize_x(last, lo, hi)
+            sums = psum.tile([P, hi - lo], F32, name=bank)
+            multiply(lo, hi, sums[:])
+            activate(lo, hi, sums[:])
 
         first = keep.tile([P, T], F32, name="plane00", align_bytes=64)
         total = keep.tile([P, T], F32, name="plane01", align_bytes=64)
-        for lo, hi in spans(FIRST_PIECES):
-            nc.vector.tensor_copy(first[:, lo:hi], y[:].indirect(pos1_sb[:, lo // PER_COLUMN : hi // PER_COLUMN]))
         for lo, hi in spans(TOKEN_PIECES):
+            nc.scalar.activation(first[:, lo:hi], y[:].indirect(pos1_sb[:, lo // PER_COLUMN : hi // PER_COLUMN]), COPY)
             nc.vector.tensor_tensor(
                 total[:, lo:hi],
                 y[:].indirect(pos2_sb[:, lo // PER_COLUMN : hi // PER_COLUMN]),

@@ -171,6 +171,11 @@ def tile_moe_pre_lin_silu_kernel(tc, xT, w, b, gate, offs, pos1, pos2, out):
             e = lo // C
             nc.scalar.activation(y[:, lo:hi], sums, SILU, bias=bias[:, e : e + 1])
 
+        warm_in = keep.tile([P, 1], F32, name="warm_in")
+        warm_out = keep.tile([P, 1], F32, name="warm_out")
+        nc.gpsimd.memset(warm_in[:], 0.0)
+        nc.scalar.activation(warm_out[:], warm_in[:], SILU)
+
         nc.gpsimd.memset(gate_rows[:], 0.0)
         make_identity(nc, identity[:])
 

@@ -27,15 +27,18 @@ RUN = 4
 W_WORDS = PASSES * N
 BLOCK = 512
 BLOCKS = S // BLOCK
-VECTOR_SLOTS = 1280
+VECTOR_SLOTS = 1216
+SPARE = S - VECTOR_SLOTS + 32 - T
+ORDER = (0, 1, 3, 4, 2, 5)
 SCALAR_CHUNKS = (
-    ((VECTOR_SLOTS, 2048, "b"), (2048, S, "c")),
-    ((0, 1024, "d"), (1024, 2048, "a"), (2048, 2560, "b"), (2560, S, "c")),
+    ((VECTOR_SLOTS, S, "b"),),
+    ((0, 1280, "c"), (1280, 2176, "a"), (2176, 2816, "b"), (2816, S, "c")),
 )
-TOKEN_PIECES = (256, 256, 256, 256, 256, 128, 128)
+FREED_AFTER = (4, 5, 8)
+TOKEN_PIECES = (192, 192, 384, 384, 192, 192)
 W_BUFS = 6
 ROUNDED_BUFS = 3
-DOUBLE_RIDERS = 2
+LATE_RIDERS = 5
 
 
 def spans(widths):
@@ -44,6 +47,11 @@ def spans(widths):
         result.append((start, start + width))
         start += width
     return result
+
+
+def place_of(unit):
+    g, index = divmod(unit, BLOCKS)
+    return g, ORDER[index] if g == 0 else index
 
 
 def tile_moe_pre_lin_silu_kernel(tc, xT, w, b, gate, offs, pos1, pos2, out):
@@ -62,14 +70,13 @@ def tile_moe_pre_lin_silu_kernel(tc, xT, w, b, gate, offs, pos1, pos2, out):
         gate_rows = keep.tile([P, P], F32, name="gate_rows")
         gate_columns = keep.tile([P, S // P], F32, name="gate_columns")
         planes = [
-            [keep.tile([P, T], F32, name="plane%d%d" % (g, j), align_bytes=64) for j in range(PACK)]
+            [keep.tile([P, T + (SPARE if g == 0 else 0)], F32, name="plane%d%d" % (g, j), align_bytes=64) for j in range(PACK)]
             for g in range(PASSES)
         ]
         x_codes = keep.tile([P, PASSES * S], U32, name="x_codes", align_bytes=64)
         x_scales = keep.tile([P, PASSES * S], U8, name="x_scales", align_bytes=64)
         w_codes = keep.tile([P, E * W_WORDS], U32, name="w_codes", align_bytes=64)
         w_scales = keep.tile([P, E * W_WORDS], U8, name="w_scales", align_bytes=64)
-        y = keep.tile([P, S], F32, name="y", align_bytes=64)
 
         x_view = xT.rearrange("(g p j) t -> g j p t", g=PASSES, j=PACK)
         w_view = w.rearrange("e (g p j) n -> p (e g) (j n)", g=PASSES, j=PACK)
@@ -78,7 +85,7 @@ def tile_moe_pre_lin_silu_kernel(tc, xT, w, b, gate, offs, pos1, pos2, out):
         rounded = {}
 
         def load_plane(g, j):
-            nc.sync.dma_start(planes[g][j][:], x_view[g, j])
+            nc.sync.dma_start(planes[g][j][:, :T], x_view[g, j])
 
         def load_w(e):
             w_raw[e] = w_ring.tile([P, PASSES, PACK * N], F32, name="w_raw")
@@ -99,9 +106,10 @@ def tile_moe_pre_lin_silu_kernel(tc, xT, w, b, gate, offs, pos1, pos2, out):
                 nc.scalar.activation(tile[:, j, :], window(g, j, lo, hi), COPY)
 
         def riders(unit):
-            if unit < DOUBLE_RIDERS:
+            if unit < ROUNDED_BUFS:
                 return range(2 * unit, 2 * unit + 2)
-            return range(min(unit + DOUBLE_RIDERS, E), min(unit + DOUBLE_RIDERS + 1, E))
+            e = unit - LATE_RIDERS + 2 * ROUNDED_BUFS
+            return range(e, e + 1) if 2 * ROUNDED_BUFS <= e < E else range(0)
 
         def open_unit(unit):
             rounded[unit] = rounded_ring.tile([P, 2 * BLOCK * PACK], BF16, name="rounded", align_bytes=64)
@@ -120,7 +128,7 @@ def tile_moe_pre_lin_silu_kernel(tc, xT, w, b, gate, offs, pos1, pos2, out):
                     load_w(e + W_BUFS)
 
         def times_gate(unit, lo, hi):
-            g, block = divmod(unit, BLOCKS)
+            g, block = place_of(unit)
             base = block * BLOCK
             for first, end, tile in chunks[g]:
                 a, z = max(lo, first), min(hi, end)
@@ -145,7 +153,7 @@ def tile_moe_pre_lin_silu_kernel(tc, xT, w, b, gate, offs, pos1, pos2, out):
             )
 
         def quantize_x(unit, lo, hi):
-            g, block = divmod(unit, BLOCKS)
+            g, block = place_of(unit)
             quantize(rounded[unit], lo - block * BLOCK, hi - block * BLOCK, x_codes, x_scales, g * S + lo)
 
         def quantize_riders(unit):
@@ -153,9 +161,9 @@ def tile_moe_pre_lin_silu_kernel(tc, xT, w, b, gate, offs, pos1, pos2, out):
             if len(along):
                 quantize(rounded[unit], BLOCK, BLOCK + len(along) * W_WORDS, w_codes, w_scales, along[0] * W_WORDS)
 
-        def multiply(lo, hi, sums):
+        def multiply(lo, hi, sums, passes=range(PASSES)):
             e = lo // C
-            for g in range(PASSES):
+            for g in passes:
                 a = e * W_WORDS + g * N
                 nc.tensor.matmul_mx(
                     out=sums,
@@ -176,6 +184,8 @@ def tile_moe_pre_lin_silu_kernel(tc, xT, w, b, gate, offs, pos1, pos2, out):
         nc.gpsimd.memset(warm_in[:], 0.0)
         nc.scalar.activation(warm_out[:], warm_in[:], SILU)
 
+        for j in range(PACK):
+            nc.gpsimd.memset(planes[0][j][:, T:], 0.0)
         nc.gpsimd.memset(gate_rows[:], 0.0)
         make_identity(nc, identity[:])
 
@@ -187,12 +197,10 @@ def tile_moe_pre_lin_silu_kernel(tc, xT, w, b, gate, offs, pos1, pos2, out):
         load_plane(0, 2)
         load_w(1)
         load_plane(0, 3)
-        load_w(2)
-        load_w(3)
+        for e in range(2, W_BUFS):
+            load_w(e)
         for j in range(PACK):
             load_plane(1, j)
-        load_w(4)
-        load_w(5)
         nc.sync.dma_start(bias[:], b)
         nc.sync.dma_start(pos1_sb[:], pos1)
         nc.sync.dma_start(pos2_sb[:], pos2)
@@ -216,15 +224,16 @@ def tile_moe_pre_lin_silu_kernel(tc, xT, w, b, gate, offs, pos1, pos2, out):
 
         scalar_chunk(1, 0)
         last = PASSES * BLOCKS - 1
+        waiting = []
         for unit in range(ROUNDED_BUFS):
             open_unit(unit)
         times_gate(0, 0, BLOCK)
         for unit in range(last):
-            g, block = divmod(unit, BLOCKS)
-            ahead = (unit + 1) % BLOCKS * BLOCK
+            g, block = place_of(unit)
+            ahead = place_of(unit + 1)[1] * BLOCK
             times_gate(unit + 1, ahead, ahead + (BLOCK if unit + 1 < last else C))
-            if unit + 1 in (2, 3, 5):
-                scalar_chunk(1, (2, 3, 5).index(unit + 1) + 1)
+            if unit + 1 in FREED_AFTER:
+                scalar_chunk(1, FREED_AFTER.index(unit + 1) + 1)
             quantize_x(unit, block * BLOCK, (block + 1) * BLOCK)
             quantize_riders(unit)
             if unit + ROUNDED_BUFS <= last:
@@ -233,26 +242,41 @@ def tile_moe_pre_lin_silu_kernel(tc, xT, w, b, gate, offs, pos1, pos2, out):
                 sums = psum.tile([P, BLOCK], F32, name="bank%d" % block)
                 for place in range(0, BLOCK, C):
                     multiply(block * BLOCK + place, block * BLOCK + place + C, sums[:, place : place + C])
-                for place in range(0, BLOCK, C):
-                    activate(block * BLOCK + place, block * BLOCK + place + C, sums[:, place : place + C])
+                    waiting.append((block * BLOCK + place, sums[:, place : place + C]))
 
-        ends = ((S - 2 * C, S - C, "spare0"), (S - C, S - C // 2, "spare1"), (S - C // 2, S, "bank0"))
+        y = keep.tile([P, S], F32, name="plane10", align_bytes=64)
+        for lo, sums in waiting:
+            activate(lo, lo + C, sums)
+        ends = ((S - 2 * C, S - C, "spare0"), (S - C, S - C // 2, "spare1"), (S - C // 2, S, "bank5"))
+        end_sums = []
         for index, (lo, hi, bank) in enumerate(ends):
             if index + 1 < len(ends):
                 times_gate(last, ends[index + 1][0], ends[index + 1][1])
+            end_sums.append(psum.tile([P, hi - lo], F32, name=bank))
+            multiply(lo, hi, end_sums[index][:], range(PASSES - 1))
             quantize_x(last, lo, hi)
-            sums = psum.tile([P, hi - lo], F32, name=bank)
-            multiply(lo, hi, sums[:])
-            activate(lo, hi, sums[:])
+            multiply(lo, hi, end_sums[index][:], range(PASSES - 1, PASSES))
+            activate(lo, hi, end_sums[index][:])
 
         first = keep.tile([P, T], F32, name="plane00", align_bytes=64)
         total = keep.tile([P, T], F32, name="plane01", align_bytes=64)
-        for lo, hi in spans(TOKEN_PIECES):
-            nc.scalar.activation(first[:, lo:hi], y[:].indirect(pos1_sb[:, lo // PER_COLUMN : hi // PER_COLUMN]), COPY)
-            nc.vector.tensor_tensor(
-                total[:, lo:hi],
-                y[:].indirect(pos2_sb[:, lo // PER_COLUMN : hi // PER_COLUMN]),
-                first[:, lo:hi],
-                ADD,
-            )
-            nc.sync.dma_start(out[:, lo:hi], total[:, lo:hi])
+
+        def results(places, lo, hi):
+            return y[:].indirect(places[:, lo // PER_COLUMN : hi // PER_COLUMN])
+
+        pieces = spans(TOKEN_PIECES)
+        for index, (lo, hi) in enumerate(pieces):
+            if index == 1:
+                nc.vector.tensor_copy(first[:, lo:hi], results(pos1_sb, lo, hi))
+            else:
+                nc.scalar.activation(first[:, lo:hi], results(pos1_sb, lo, hi), COPY)
+        lo, hi = pieces[-1]
+        second = keep.tile([P, hi - lo], F32, name="plane02", align_bytes=64)
+        nc.scalar.activation(second[:], results(pos2_sb, lo, hi), COPY)
+        stored = 0
+        for index, (lo, hi) in enumerate(pieces):
+            other = second[:] if hi == T else results(pos2_sb, lo, hi)
+            nc.vector.tensor_tensor(total[:, lo:hi], other, first[:, lo:hi], ADD)
+            if index > 0:
+                nc.sync.dma_start(out[:, stored:hi], total[:, stored:hi])
+                stored = hi

@@ -23,7 +23,7 @@ P = 128
 PACK = 4
 PASSES = K // (P * PACK)
 PER_COLUMN = 16
-RUN = 4
+RUN = 2
 W_WORDS = PASSES * N
 BLOCK = 512
 BLOCKS = S // BLOCK

@@ -27,18 +27,19 @@ RUN = 2
 W_WORDS = PASSES * N
 BLOCK = 512
 BLOCKS = S // BLOCK
-VECTOR_SLOTS = 1216
+VECTOR_SLOTS = 1344
 SPARE = S - VECTOR_SLOTS + 32 - T
-ORDER = (0, 1, 3, 4, 2, 5)
+ORDER = (0, 1, 3, 4, 5, 2)
 SCALAR_CHUNKS = (
     ((VECTOR_SLOTS, S, "b"),),
-    ((0, 1280, "c"), (1280, 2176, "a"), (2176, 2816, "b"), (2816, S, "c")),
+    ((0, 1248, "c"), (1248, 2112, "a"), (2112, 2688, "b"), (2688, S, "c")),
 )
-FREED_AFTER = (4, 5, 8)
+FREED_AFTER = (5, 6, 8)
 TOKEN_PIECES = (192, 192, 384, 384, 192, 192)
 W_BUFS = 6
 ROUNDED_BUFS = 3
-LATE_RIDERS = 5
+HELPED_UNITS = (2, 3, 4)
+HELPED = 128
 
 
 def spans(widths):
@@ -68,6 +69,7 @@ def tile_moe_pre_lin_silu_kernel(tc, xT, w, b, gate, offs, pos1, pos2, out):
         bias = keep.tile([P, E], F32, name="bias")
         identity = keep.tile([P, P], F32, name="identity")
         gate_rows = keep.tile([P, P], F32, name="gate_rows")
+        gate_ends = keep.tile([P, len(HELPED_UNITS), HELPED], F32, name="gate_ends")
         gate_columns = keep.tile([P, S // P], F32, name="gate_columns")
         planes = [
             [keep.tile([P, T + (SPARE if g == 0 else 0)], F32, name="plane%d%d" % (g, j), align_bytes=64) for j in range(PACK)]
@@ -105,31 +107,26 @@ def tile_moe_pre_lin_silu_kernel(tc, xT, w, b, gate, offs, pos1, pos2, out):
             for j in range(PACK):
                 nc.scalar.activation(tile[:, j, :], window(g, j, lo, hi), COPY)
 
-        def riders(unit):
-            if unit < ROUNDED_BUFS:
-                return range(2 * unit, 2 * unit + 2)
-            e = unit - LATE_RIDERS + 2 * ROUNDED_BUFS
-            return range(e, e + 1) if 2 * ROUNDED_BUFS <= e < E else range(0)
+        def round_w(e, tile, word):
+            for g in range(PASSES):
+                a = word + g * N
+                nc.gpsimd.tensor_scalar(
+                    tile[:, a * PACK : (a + N) * PACK].rearrange("p (n j) -> p n j", j=PACK),
+                    w_raw[e][:, g, :].rearrange("p (j n) -> p n j", j=PACK),
+                    1.0,
+                    0.0,
+                    MULT,
+                    ADD,
+                )
+            if e + W_BUFS < E:
+                load_w(e + W_BUFS)
 
-        def open_unit(unit):
-            rounded[unit] = rounded_ring.tile([P, 2 * BLOCK * PACK], BF16, name="rounded", align_bytes=64)
-            for place, e in enumerate(riders(unit)):
-                for g in range(PASSES):
-                    word = BLOCK + place * W_WORDS + g * N
-                    nc.gpsimd.tensor_scalar(
-                        rounded[unit][:, word * PACK : (word + N) * PACK].rearrange("p (n j) -> p n j", j=PACK),
-                        w_raw[e][:, g, :].rearrange("p (j n) -> p n j", j=PACK),
-                        1.0,
-                        0.0,
-                        MULT,
-                        ADD,
-                    )
-                if e + W_BUFS < E:
-                    load_w(e + W_BUFS)
+        def first_own(unit):
+            return place_of(unit)[1] * BLOCK + (HELPED if unit in HELPED_UNITS else 0)
 
         def times_gate(unit, lo, hi):
             g, block = place_of(unit)
-            base = block * BLOCK
+            base = first_own(unit)
             for first, end, tile in chunks[g]:
                 a, z = max(lo, first), min(hi, end)
                 if a < z:
@@ -138,12 +135,34 @@ def tile_moe_pre_lin_silu_kernel(tc, xT, w, b, gate, offs, pos1, pos2, out):
                             "p (c i j) -> p c j i", i=RUN, j=PACK
                         ),
                         tile[:, :, a - first : z - first].rearrange("p j (c i) -> p c j i", i=RUN),
-                        gate_banks[block][:, a - base : z - base]
+                        gate_banks[block][:, a - block * BLOCK : z - block * BLOCK]
                         .rearrange("p (c i) -> p c i", i=RUN)
                         .unsqueeze(2)
                         .to_broadcast([P, (z - a) // RUN, PACK, RUN]),
                         MULT,
                     )
+
+        def unit_times_gate(unit):
+            rounded[unit] = rounded_ring.tile([P, BLOCK * PACK], BF16, name="rounded", align_bytes=64)
+            end = (place_of(unit)[1] + 1) * BLOCK
+            times_gate(unit, first_own(unit), end if unit < last else SCALAR_CHUNKS[1][-1][0])
+
+        def beside(unit):
+            tile = keep.tile([P, 2 * W_WORDS * PACK], BF16, name="early0", align_bytes=64)
+            if unit in HELPED_UNITS:
+                g, block = place_of(unit)
+                lo, hi = block * BLOCK, block * BLOCK + HELPED
+                first, end, source = [chunk for chunk in chunks[g] if chunk[0] <= lo and hi <= chunk[1]][0]
+                nc.gpsimd.tensor_tensor(
+                    tile[:, 0 : HELPED * PACK].rearrange("p (s j) -> p s j", j=PACK),
+                    source[:, :, lo - first : hi - first].rearrange("p j s -> p s j"),
+                    gate_ends[:, HELPED_UNITS.index(unit), :].unsqueeze(2).to_broadcast([P, HELPED, PACK]),
+                    MULT,
+                )
+                return (tile, 0, HELPED, x_codes, x_scales, g * S + lo)
+            e = unit + E - last
+            round_w(e, tile, 0)
+            return (tile, 0, W_WORDS, w_codes, w_scales, e * W_WORDS)
 
         def quantize(source, a, z, codes, scales, word):
             nc.vector.quantize_mx(
@@ -153,13 +172,8 @@ def tile_moe_pre_lin_silu_kernel(tc, xT, w, b, gate, offs, pos1, pos2, out):
             )
 
         def quantize_x(unit, lo, hi):
-            g, block = place_of(unit)
-            quantize(rounded[unit], lo - block * BLOCK, hi - block * BLOCK, x_codes, x_scales, g * S + lo)
-
-        def quantize_riders(unit):
-            along = riders(unit)
-            if len(along):
-                quantize(rounded[unit], BLOCK, BLOCK + len(along) * W_WORDS, w_codes, w_scales, along[0] * W_WORDS)
+            base = first_own(unit)
+            quantize(rounded[unit], lo - base, hi - base, x_codes, x_scales, place_of(unit)[0] * S + lo)
 
         def multiply(lo, hi, sums, passes=range(PASSES)):
             e = lo // C
@@ -196,9 +210,14 @@ def tile_moe_pre_lin_silu_kernel(tc, xT, w, b, gate, offs, pos1, pos2, out):
         load_w(0)
         load_plane(0, 2)
         load_w(1)
+        load_w(2)
         load_plane(0, 3)
-        for e in range(2, W_BUFS):
+        for e in range(3, W_BUFS):
             load_w(e)
+        helped_blocks = slice(ORDER[HELPED_UNITS[0]], ORDER[HELPED_UNITS[-1]] + 1)
+        nc.sync.dma_start(
+            gate_ends[:], gate[0:P, :].rearrange("p (b s) -> p b s", s=BLOCK)[:, helped_blocks, 0:HELPED]
+        )
         for j in range(PACK):
             load_plane(1, j)
         nc.sync.dma_start(bias[:], b)
@@ -225,19 +244,23 @@ def tile_moe_pre_lin_silu_kernel(tc, xT, w, b, gate, offs, pos1, pos2, out):
         scalar_chunk(1, 0)
         last = PASSES * BLOCKS - 1
         waiting = []
-        for unit in range(ROUNDED_BUFS):
-            open_unit(unit)
-        times_gate(0, 0, BLOCK)
+        early = []
+        for pair in range(W_BUFS // 2):
+            early.append(keep.tile([P, 2 * W_WORDS * PACK], BF16, name="early%d" % pair, align_bytes=64))
+            for place in range(2):
+                round_w(2 * pair + place, early[pair], place * W_WORDS)
+        unit_times_gate(0)
         for unit in range(last):
             g, block = place_of(unit)
-            ahead = place_of(unit + 1)[1] * BLOCK
-            times_gate(unit + 1, ahead, ahead + (BLOCK if unit + 1 < last else C))
+            helped = beside(unit + 1) if HELPED_UNITS[0] <= unit + 1 < last else None
+            unit_times_gate(unit + 1)
             if unit + 1 in FREED_AFTER:
                 scalar_chunk(1, FREED_AFTER.index(unit + 1) + 1)
-            quantize_x(unit, block * BLOCK, (block + 1) * BLOCK)
-            quantize_riders(unit)
-            if unit + ROUNDED_BUFS <= last:
-                open_unit(unit + ROUNDED_BUFS)
+            quantize_x(unit, first_own(unit), (block + 1) * BLOCK)
+            if unit < len(early):
+                quantize(early[unit], 0, 2 * W_WORDS, w_codes, w_scales, 2 * unit * W_WORDS)
+            if helped:
+                quantize(*helped)
             if g == PASSES - 1:
                 sums = psum.tile([P, BLOCK], F32, name="bank%d" % block)
                 for place in range(0, BLOCK, C):
@@ -249,6 +272,7 @@ def tile_moe_pre_lin_silu_kernel(tc, xT, w, b, gate, offs, pos1, pos2, out):
             activate(lo, lo + C, sums)
         ends = ((S - 2 * C, S - C, "spare0"), (S - C, S - C // 2, "spare1"), (S - C // 2, S, "bank5"))
         end_sums = []
+        times_gate(last, SCALAR_CHUNKS[1][-1][0], S - C)
         for index, (lo, hi, bank) in enumerate(ends):
             if index + 1 < len(ends):
                 times_gate(last, ends[index + 1][0], ends[index + 1][1])

@@ -25,21 +25,22 @@ PASSES = K // (P * PACK)
 PER_COLUMN = 16
 RUN = 2
 W_WORDS = PASSES * N
-BLOCK = 512
-BLOCKS = S // BLOCK
-VECTOR_SLOTS = 1344
-SPARE = S - VECTOR_SLOTS + 32 - T
-ORDER = (0, 1, 3, 4, 5, 2)
-SCALAR_CHUNKS = (
-    ((VECTOR_SLOTS, S, "b"),),
-    ((0, 1248, "c"), (1248, 2112, "a"), (2112, 2688, "b"), (2688, S, "c")),
-)
-FREED_AFTER = (5, 6, 8)
+GROUP = 512
+GROUPS = S // GROUP
+LAST = PASSES * GROUPS - 1
+WIDTHS = (512, 384, 256, 128, 64)
+
+VECTOR_SLOTS = 1376
+SPARE = S - VECTOR_SLOTS + 2 * PER_COLUMN - T
+ORDER = (0, 1, 3, 4, 2, 5)
+LONG, SHORT = 128, 64
+HELP = {2: LONG, 3: LONG, 4: LONG, LAST: SHORT}
+CHUNKS = ((0, 1280, "c"), (1280, 2112, "a"), (2112, 2688, "b"), (2688, S, "c"))
+CHUNK_AFTER = (5, 6, 8)
 TOKEN_PIECES = (192, 192, 384, 384, 192, 192)
-W_BUFS = 6
+OWN_PIECE = 1
+EARLY = 6
 ROUNDED_BUFS = 3
-HELPED_UNITS = (2, 3, 4)
-HELPED = 128
 
 
 def spans(widths):
@@ -51,8 +52,13 @@ def spans(widths):
 
 
 def place_of(unit):
-    g, index = divmod(unit, BLOCKS)
+    g, index = divmod(unit, GROUPS)
     return g, ORDER[index] if g == 0 else index
+
+
+def vector_part(unit):
+    group = place_of(unit)[1]
+    return group * GROUP + HELP.get(unit, 0), (group + 1) * GROUP
 
 
 def tile_moe_pre_lin_silu_kernel(tc, xT, w, b, gate, offs, pos1, pos2, out):
@@ -60,7 +66,7 @@ def tile_moe_pre_lin_silu_kernel(tc, xT, w, b, gate, offs, pos1, pos2, out):
     with ExitStack() as ctx:
         keep = ctx.enter_context(tc.tile_pool(name="keep", bufs=1))
         rounded_ring = ctx.enter_context(tc.tile_pool(name="rounded_ring", bufs=ROUNDED_BUFS))
-        w_ring = ctx.enter_context(tc.tile_pool(name="w_ring", bufs=W_BUFS))
+        w_ring = ctx.enter_context(tc.tile_pool(name="w_ring", bufs=EARLY))
         psum = ctx.enter_context(tc.psum_pool(name="psum", bufs=1))
 
         offs_sb = keep.tile([P, S // PER_COLUMN], U16, name="offs_sb")
@@ -69,10 +75,14 @@ def tile_moe_pre_lin_silu_kernel(tc, xT, w, b, gate, offs, pos1, pos2, out):
         bias = keep.tile([P, E], F32, name="bias")
         identity = keep.tile([P, P], F32, name="identity")
         gate_rows = keep.tile([P, P], F32, name="gate_rows")
-        gate_ends = keep.tile([P, len(HELPED_UNITS), HELPED], F32, name="gate_ends")
+        gate_long = keep.tile([P, 3, LONG], F32, name="gate_long")
+        gate_short = keep.tile([P, SHORT], F32, name="gate_short")
         gate_columns = keep.tile([P, S // P], F32, name="gate_columns")
         planes = [
-            [keep.tile([P, T + (SPARE if g == 0 else 0)], F32, name="plane%d%d" % (g, j), align_bytes=64) for j in range(PACK)]
+            [
+                keep.tile([P, T + (SPARE if g == 0 else 0)], F32, name="plane%d%d" % (g, j), align_bytes=64)
+                for j in range(PACK)
+            ]
             for g in range(PASSES)
         ]
         x_codes = keep.tile([P, PASSES * S], U32, name="x_codes", align_bytes=64)
@@ -98,14 +108,14 @@ def tile_moe_pre_lin_silu_kernel(tc, xT, w, b, gate, offs, pos1, pos2, out):
             chunks[g].append((lo, hi, tile))
             return tile
 
-        def window(g, j, lo, hi):
+        def tokens(g, j, lo, hi):
             return planes[g][j][:].indirect(offs_sb[:, lo // PER_COLUMN : hi // PER_COLUMN])
 
-        def scalar_chunk(g, index):
-            lo, hi, buffer = SCALAR_CHUNKS[g][index]
-            tile = new_chunk(g, lo, hi, buffer)
+        def gather_chunk(index):
+            lo, hi, buffer = CHUNKS[index]
+            tile = new_chunk(PASSES - 1, lo, hi, buffer)
             for j in range(PACK):
-                nc.scalar.activation(tile[:, j, :], window(g, j, lo, hi), COPY)
+                nc.scalar.activation(tile[:, j, :], tokens(PASSES - 1, j, lo, hi), COPY)
 
         def round_w(e, tile, word):
             for g in range(PASSES):
@@ -118,15 +128,10 @@ def tile_moe_pre_lin_silu_kernel(tc, xT, w, b, gate, offs, pos1, pos2, out):
                     MULT,
                     ADD,
                 )
-            if e + W_BUFS < E:
-                load_w(e + W_BUFS)
-
-        def first_own(unit):
-            return place_of(unit)[1] * BLOCK + (HELPED if unit in HELPED_UNITS else 0)
 
         def times_gate(unit, lo, hi):
-            g, block = place_of(unit)
-            base = first_own(unit)
+            g, group = place_of(unit)
+            base = vector_part(unit)[0]
             for first, end, tile in chunks[g]:
                 a, z = max(lo, first), min(hi, end)
                 if a < z:
@@ -135,73 +140,88 @@ def tile_moe_pre_lin_silu_kernel(tc, xT, w, b, gate, offs, pos1, pos2, out):
                             "p (c i j) -> p c j i", i=RUN, j=PACK
                         ),
                         tile[:, :, a - first : z - first].rearrange("p j (c i) -> p c j i", i=RUN),
-                        gate_banks[block][:, a - block * BLOCK : z - block * BLOCK]
+                        gate_banks[group][:, a - group * GROUP : z - group * GROUP]
                         .rearrange("p (c i) -> p c i", i=RUN)
                         .unsqueeze(2)
                         .to_broadcast([P, (z - a) // RUN, PACK, RUN]),
                         MULT,
                     )
 
-        def unit_times_gate(unit):
-            rounded[unit] = rounded_ring.tile([P, BLOCK * PACK], BF16, name="rounded", align_bytes=64)
-            end = (place_of(unit)[1] + 1) * BLOCK
-            times_gate(unit, first_own(unit), end if unit < last else SCALAR_CHUNKS[1][-1][0])
+        def multiply_unit(unit):
+            rounded[unit] = rounded_ring.tile([P, GROUP * PACK], BF16, name="rounded", align_bytes=64)
+            lo, hi = vector_part(unit)
+            times_gate(unit, lo, hi if unit < LAST else CHUNKS[-1][0])
 
         def beside(unit):
             tile = keep.tile([P, 2 * W_WORDS * PACK], BF16, name="early0", align_bytes=64)
-            if unit in HELPED_UNITS:
-                g, block = place_of(unit)
-                lo, hi = block * BLOCK, block * BLOCK + HELPED
-                first, end, source = [chunk for chunk in chunks[g] if chunk[0] <= lo and hi <= chunk[1]][0]
-                nc.gpsimd.tensor_tensor(
-                    tile[:, 0 : HELPED * PACK].rearrange("p (s j) -> p s j", j=PACK),
-                    source[:, :, lo - first : hi - first].rearrange("p j s -> p s j"),
-                    gate_ends[:, HELPED_UNITS.index(unit), :].unsqueeze(2).to_broadcast([P, HELPED, PACK]),
-                    MULT,
-                )
-                return (tile, 0, HELPED, x_codes, x_scales, g * S + lo)
-            e = unit + E - last
-            round_w(e, tile, 0)
-            return (tile, 0, W_WORDS, w_codes, w_scales, e * W_WORDS)
-
-        def quantize(source, a, z, codes, scales, word):
-            nc.vector.quantize_mx(
-                out=codes[:, word : word + z - a].bitcast(FP8X4),
-                scales=scales[:, word : word + z - a],
-                in_=source[:, a * PACK : z * PACK],
+            if unit not in HELP:
+                e = unit + E - LAST
+                round_w(e, tile, 0)
+                return (tile, 0, W_WORDS, w_codes, w_scales, e * W_WORDS)
+            g, group = place_of(unit)
+            count = HELP[unit]
+            lo = group * GROUP
+            first, end, source = [chunk for chunk in chunks[g] if chunk[0] <= lo < chunk[1]][0]
+            gates = gate_short[:] if unit == LAST else gate_long[:, group - 2, :]
+            nc.gpsimd.tensor_tensor(
+                tile[:, 0 : count * PACK].rearrange("p (s j) -> p s j", j=PACK),
+                source[:, :, lo - first : lo - first + count].rearrange("p j s -> p s j"),
+                gates.unsqueeze(2).to_broadcast([P, count, PACK]),
+                MULT,
             )
+            return (tile, 0, count, x_codes, x_scales, g * S + lo)
 
-        def quantize_x(unit, lo, hi):
-            base = first_own(unit)
+        def quantize(source, a, z, codes, scales, column):
+            width = max(width for width in WIDTHS if width <= z - a)
+            nc.vector.quantize_mx(
+                out=codes[:, column : column + width].bitcast(FP8X4),
+                scales=scales[:, column : column + width],
+                in_=source[:, a * PACK : (a + width) * PACK],
+            )
+            if a + width < z:
+                quantize(source, a + width, z, codes, scales, column + width)
+
+        def quantize_slots(unit, lo, hi):
+            base = vector_part(unit)[0]
             quantize(rounded[unit], lo - base, hi - base, x_codes, x_scales, place_of(unit)[0] * S + lo)
 
-        def multiply(lo, hi, sums, passes=range(PASSES)):
-            e = lo // C
-            for g in passes:
-                a = e * W_WORDS + g * N
-                nc.tensor.matmul_mx(
-                    out=sums,
-                    lhsT=w_codes[:, a : a + N].bitcast(FP8X4),
-                    lhsT_scale=w_scales[:, a : a + N],
-                    rhs=x_codes[:, g * S + lo : g * S + hi].bitcast(FP8X4),
-                    rhs_scale=x_scales[:, g * S + lo : g * S + hi],
-                    start=(g == 0),
-                    stop=(g == PASSES - 1),
-                )
+        def quantize_unit(unit):
+            quantize_slots(unit, *vector_part(unit))
+
+        def matmul_pass(g, lo, hi, sums):
+            column = lo // C * W_WORDS + g * N
+            nc.tensor.matmul_mx(
+                out=sums,
+                lhsT=w_codes[:, column : column + N].bitcast(FP8X4),
+                lhsT_scale=w_scales[:, column : column + N],
+                rhs=x_codes[:, g * S + lo : g * S + hi].bitcast(FP8X4),
+                rhs_scale=x_scales[:, g * S + lo : g * S + hi],
+                start=(g == 0),
+                stop=(g == PASSES - 1),
+            )
+
+        def matmul_group(unit):
+            g, group = place_of(unit)
+            if g == PASSES - 1:
+                bank = psum.tile([P, GROUP], F32, name="bank%d" % group)
+                for place in range(0, GROUP, C):
+                    lo = group * GROUP + place
+                    for each in range(PASSES):
+                        matmul_pass(each, lo, lo + C, bank[:, place : place + C])
+                    summed.append((lo, bank[:, place : place + C]))
 
         def activate(lo, hi, sums):
-            e = lo // C
-            nc.scalar.activation(y[:, lo:hi], sums, SILU, bias=bias[:, e : e + 1])
+            nc.scalar.activation(y[:, lo:hi], sums, SILU, bias=bias[:, lo // C : lo // C + 1])
 
         warm_in = keep.tile([P, 1], F32, name="warm_in")
         warm_out = keep.tile([P, 1], F32, name="warm_out")
         nc.gpsimd.memset(warm_in[:], 0.0)
         nc.scalar.activation(warm_out[:], warm_in[:], SILU)
 
-        for j in range(PACK):
-            nc.gpsimd.memset(planes[0][j][:, T:], 0.0)
         nc.gpsimd.memset(gate_rows[:], 0.0)
         make_identity(nc, identity[:])
+        for j in range(PACK):
+            nc.vector.memset(planes[0][j][:, T:], 0.0)
 
         load_plane(0, 0)
         nc.sync.dma_start(offs_sb[:], offs)
@@ -212,75 +232,72 @@ def tile_moe_pre_lin_silu_kernel(tc, xT, w, b, gate, offs, pos1, pos2, out):
         load_w(1)
         load_w(2)
         load_plane(0, 3)
-        for e in range(3, W_BUFS):
+        for e in range(3, EARLY):
             load_w(e)
-        helped_blocks = slice(ORDER[HELPED_UNITS[0]], ORDER[HELPED_UNITS[-1]] + 1)
-        nc.sync.dma_start(
-            gate_ends[:], gate[0:P, :].rearrange("p (b s) -> p b s", s=BLOCK)[:, helped_blocks, 0:HELPED]
-        )
+        nc.sync.dma_start(gate_long[:], gate[0:P, :].rearrange("p (b s) -> p b s", s=GROUP)[:, 2:5, 0:LONG])
         for j in range(PACK):
             load_plane(1, j)
-        nc.sync.dma_start(bias[:], b)
-        nc.sync.dma_start(pos1_sb[:], pos1)
-        nc.sync.dma_start(pos2_sb[:], pos2)
 
-        own = new_chunk(0, 0, VECTOR_SLOTS, "a")
-        others = [(lo, hi, new_chunk(0, lo, hi, buffer)) for lo, hi, buffer in SCALAR_CHUNKS[0]]
+        by_vector = new_chunk(0, 0, VECTOR_SLOTS, "a")
+        by_scalar = new_chunk(0, VECTOR_SLOTS, S, "b")
         for j in range(PACK):
-            nc.vector.tensor_copy(own[:, j, :], window(0, j, 0, VECTOR_SLOTS))
-            for lo, hi, tile in others:
-                nc.scalar.activation(tile[:, j, :], window(0, j, lo, hi), COPY)
+            nc.vector.tensor_copy(by_vector[:, j, :], tokens(0, j, 0, VECTOR_SLOTS))
+            nc.scalar.activation(by_scalar[:, j, :], tokens(0, j, VECTOR_SLOTS, S), COPY)
 
         turned = psum.tile([P, P], F32, name="spare0")
         nc.tensor.transpose(turned[:], gate_rows[:], identity[:])
         nc.vector.tensor_copy(gate_columns[:], turned[:, 0 : S // P])
-        gate_banks = [psum.tile([P, BLOCK], F32, name="bank%d" % block) for block in range(BLOCKS)]
+        gate_banks = [psum.tile([P, GROUP], F32, name="bank%d" % group) for group in range(GROUPS)]
         for c in range(S // P):
-            block, place = divmod(c * P, BLOCK)
+            group, place = divmod(c * P, GROUP)
             nc.tensor.transpose(
-                gate_banks[block][:, place : place + P], gate_columns[:, c : c + 1].to_broadcast([P, P]), identity[:]
+                gate_banks[group][:, place : place + P], gate_columns[:, c : c + 1].to_broadcast([P, P]), identity[:]
             )
 
-        scalar_chunk(1, 0)
-        last = PASSES * BLOCKS - 1
-        waiting = []
+        gather_chunk(0)
         early = []
-        for pair in range(W_BUFS // 2):
+        for pair in range(EARLY // 2):
             early.append(keep.tile([P, 2 * W_WORDS * PACK], BF16, name="early%d" % pair, align_bytes=64))
             for place in range(2):
                 round_w(2 * pair + place, early[pair], place * W_WORDS)
-        unit_times_gate(0)
-        for unit in range(last):
-            g, block = place_of(unit)
-            helped = beside(unit + 1) if HELPED_UNITS[0] <= unit + 1 < last else None
-            unit_times_gate(unit + 1)
-            if unit + 1 in FREED_AFTER:
-                scalar_chunk(1, FREED_AFTER.index(unit + 1) + 1)
-            quantize_x(unit, first_own(unit), (block + 1) * BLOCK)
+                load_w(2 * pair + place + EARLY)
+        nc.sync.dma_start(gate_short[:], gate[0:P, S - GROUP : S - GROUP + SHORT])
+        nc.sync.dma_start(bias[:], b)
+        nc.sync.dma_start(pos1_sb[:], pos1)
+        nc.sync.dma_start(pos2_sb[:], pos2)
+
+        summed = []
+        multiply_unit(0)
+        for unit in range(LAST):
+            if unit + 1 >= min(HELP):
+                helped = beside(unit + 1)
+            multiply_unit(unit + 1)
+            if unit + 1 in CHUNK_AFTER:
+                gather_chunk(CHUNK_AFTER.index(unit + 1) + 1)
+            quantize_unit(unit)
             if unit < len(early):
                 quantize(early[unit], 0, 2 * W_WORDS, w_codes, w_scales, 2 * unit * W_WORDS)
-            if helped:
+            if min(HELP) <= unit + 1 < LAST:
                 quantize(*helped)
-            if g == PASSES - 1:
-                sums = psum.tile([P, BLOCK], F32, name="bank%d" % block)
-                for place in range(0, BLOCK, C):
-                    multiply(block * BLOCK + place, block * BLOCK + place + C, sums[:, place : place + C])
-                    waiting.append((block * BLOCK + place, sums[:, place : place + C]))
+            matmul_group(unit)
 
         y = keep.tile([P, S], F32, name="plane10", align_bytes=64)
-        for lo, sums in waiting:
+        for lo, sums in reversed(summed):
             activate(lo, lo + C, sums)
-        ends = ((S - 2 * C, S - C, "spare0"), (S - C, S - C // 2, "spare1"), (S - C // 2, S, "bank5"))
-        end_sums = []
-        times_gate(last, SCALAR_CHUNKS[1][-1][0], S - C)
+
+        ends = ((S - 2 * C, S - C, "spare0"), (S - C, S - C // 2, "spare1"), (S - C // 2, S, "bank%d" % (GROUPS - 1)))
+        own = vector_part(LAST)[0]
+        times_gate(LAST, CHUNKS[-1][0], S - C)
         for index, (lo, hi, bank) in enumerate(ends):
             if index + 1 < len(ends):
-                times_gate(last, ends[index + 1][0], ends[index + 1][1])
-            end_sums.append(psum.tile([P, hi - lo], F32, name=bank))
-            multiply(lo, hi, end_sums[index][:], range(PASSES - 1))
-            quantize_x(last, lo, hi)
-            multiply(lo, hi, end_sums[index][:], range(PASSES - 1, PASSES))
-            activate(lo, hi, end_sums[index][:])
+                times_gate(LAST, *ends[index + 1][:2])
+            sums = psum.tile([P, hi - lo], F32, name=bank)
+            matmul_pass(0, lo, hi, sums[:])
+            quantize_slots(LAST, max(lo, own), hi)
+            if lo < own:
+                quantize(*helped)
+            matmul_pass(PASSES - 1, lo, hi, sums[:])
+            activate(lo, hi, sums[:])
 
         first = keep.tile([P, T], F32, name="plane00", align_bytes=64)
         total = keep.tile([P, T], F32, name="plane01", align_bytes=64)
@@ -290,17 +307,16 @@ def tile_moe_pre_lin_silu_kernel(tc, xT, w, b, gate, offs, pos1, pos2, out):
 
         pieces = spans(TOKEN_PIECES)
         for index, (lo, hi) in enumerate(pieces):
-            if index == 1:
+            if index == OWN_PIECE:
                 nc.vector.tensor_copy(first[:, lo:hi], results(pos1_sb, lo, hi))
             else:
                 nc.scalar.activation(first[:, lo:hi], results(pos1_sb, lo, hi), COPY)
-        lo, hi = pieces[-1]
-        second = keep.tile([P, hi - lo], F32, name="plane02", align_bytes=64)
-        nc.scalar.activation(second[:], results(pos2_sb, lo, hi), COPY)
+        second = keep.tile([P, TOKEN_PIECES[-1]], F32, name="plane02", align_bytes=64)
+        nc.scalar.activation(second[:], results(pos2_sb, *pieces[-1]), COPY)
         stored = 0
         for index, (lo, hi) in enumerate(pieces):
             other = second[:] if hi == T else results(pos2_sb, lo, hi)
             nc.vector.tensor_tensor(total[:, lo:hi], other, first[:, lo:hi], ADD)
-            if index > 0:
+            if index >= OWN_PIECE:
                 nc.sync.dma_start(out[:, stored:hi], total[:, stored:hi])
                 stored = hi

@@ -25,25 +25,34 @@ PASSES = K // (P * PACK)
 PER_COLUMN = 16
 RUN = 2
 W_WORDS = PASSES * N
+W_RAW = PACK * W_WORDS
 GROUP = 512
-GROUPS = S // GROUP
-LAST = PASSES * GROUPS - 1
-WIDTHS = (512, 384, 256, 128, 64)
+TRIO = 3
+X_WORDS = 4 * C
+HALF = X_WORDS + TRIO * W_WORDS
 
-VECTOR_SLOTS = 1376
+VECTOR_SLOTS = 1472
 SPARE = S - VECTOR_SLOTS + 2 * PER_COLUMN - T
-ORDER = (0, 1, 3, 4, 2, 5)
-LONG, SHORT = 128, 64
-HELP = {2: LONG, 3: LONG, 4: LONG, LAST: SHORT}
-CHUNKS = ((0, 1280, "c"), (1280, 2112, "a"), (2112, 2688, "b"), (2688, S, "c"))
-CHUNK_AFTER = (5, 6, 8)
+CHUNKS = ((0, 1408, "c"), (1408, 2176, "a"), (2176, 2688, "b"), (2688, S, "c"))
+CHUNK_AFTER = {1: 2, 2: 2, 3: 4}
+SPANS = (
+    (0, ((0, 3 * C, 0), (4 * C, 5 * C, 3 * C)), ((0, 2 * C), (2 * C, 3 * C), (3 * C, HALF)), 0),
+    (0, ((6 * C, 10 * C, 0),), ((0, 2 * C), (2 * C, 3 * C), (3 * C, HALF)), 1),
+    (0, ((10 * C, 12 * C, 0), (3 * C, 4 * C, 2 * C), (5 * C, 6 * C, 3 * C)), ((0, 2 * C), (2 * C, 3 * C), (3 * C, HALF)), 2),
+    (1, ((0, 4 * C, 0),), ((0, 2 * C), (2 * C, 3 * C), (3 * C, HALF)), 3),
+    (1, ((5 * C, 8 * C, 0), (4 * C, 5 * C, 3 * C)), ((0, 2 * C), (2 * C, 4 * C)), None),
+    (1, ((9 * C, 10 * C, 2 * C), (8 * C, 9 * C, 3 * C)), ((2 * C, 4 * C),), None),
+    (1, ((10 * C, 11 * C, 0),), ((0, C),), None),
+    (1, ((11 * C, 11 * C + C // 2, 0),), ((0, C // 2),), None),
+    (1, ((11 * C + C // 2, S, C),), ((C, C + C // 2),), None),
+)
+HELP = {0: (4 * C, 256), 1: (8 * C, 160), 4: (4 * C, 256), 5: (8 * C, 128)}
+EARLY_TRIOS = 2
 TOKEN_PIECES = (192, 192, 384, 384, 192, 192)
 OWN_PIECE = 1
-EARLY = 6
-ROUNDED_BUFS = 3
 
 
-def spans(widths):
+def spans_of(widths):
     result, start = [], 0
     for width in widths:
         result.append((start, start + width))
@@ -51,22 +60,11 @@ def spans(widths):
     return result
 
 
-def place_of(unit):
-    g, index = divmod(unit, GROUPS)
-    return g, ORDER[index] if g == 0 else index
-
-
-def vector_part(unit):
-    group = place_of(unit)[1]
-    return group * GROUP + HELP.get(unit, 0), (group + 1) * GROUP
-
-
 def tile_moe_pre_lin_silu_kernel(tc, xT, w, b, gate, offs, pos1, pos2, out):
     nc = tc.nc
     with ExitStack() as ctx:
         keep = ctx.enter_context(tc.tile_pool(name="keep", bufs=1))
-        rounded_ring = ctx.enter_context(tc.tile_pool(name="rounded_ring", bufs=ROUNDED_BUFS))
-        w_ring = ctx.enter_context(tc.tile_pool(name="w_ring", bufs=EARLY))
+        raw_pool = ctx.enter_context(tc.tile_pool(name="raw_pool", bufs=1))
         psum = ctx.enter_context(tc.psum_pool(name="psum", bufs=1))
 
         offs_sb = keep.tile([P, S // PER_COLUMN], U16, name="offs_sb")
@@ -75,8 +73,6 @@ def tile_moe_pre_lin_silu_kernel(tc, xT, w, b, gate, offs, pos1, pos2, out):
         bias = keep.tile([P, E], F32, name="bias")
         identity = keep.tile([P, P], F32, name="identity")
         gate_rows = keep.tile([P, P], F32, name="gate_rows")
-        gate_long = keep.tile([P, 3, LONG], F32, name="gate_long")
-        gate_short = keep.tile([P, SHORT], F32, name="gate_short")
         gate_columns = keep.tile([P, S // P], F32, name="gate_columns")
         planes = [
             [
@@ -85,23 +81,61 @@ def tile_moe_pre_lin_silu_kernel(tc, xT, w, b, gate, offs, pos1, pos2, out):
             ]
             for g in range(PASSES)
         ]
-        x_codes = keep.tile([P, PASSES * S], U32, name="x_codes", align_bytes=64)
-        x_scales = keep.tile([P, PASSES * S], U8, name="x_scales", align_bytes=64)
-        w_codes = keep.tile([P, E * W_WORDS], U32, name="w_codes", align_bytes=64)
-        w_scales = keep.tile([P, E * W_WORDS], U8, name="w_scales", align_bytes=64)
+        staging = keep.tile([P, 2 * HALF * PACK], BF16, name="staging", align_bytes=64)
+        codes = keep.tile([P, PASSES * S + E * W_WORDS], U32, name="codes", align_bytes=64)
+        scales = keep.tile([P, PASSES * S + E * W_WORDS], U8, name="scales", align_bytes=64)
 
         x_view = xT.rearrange("(g p j) t -> g j p t", g=PASSES, j=PACK)
         w_view = w.rearrange("e (g p j) n -> p (e g) (j n)", g=PASSES, j=PACK)
-        w_raw = {}
         chunks = [[], []]
-        rounded = {}
+        helped_gate = {}
+        w_raw = {}
+
+        call_column, x_column, w_column = {}, {}, {}
+        column = 0
+        for index, (g, pieces, calls, trio) in enumerate(SPANS):
+            for a, z in calls:
+                call_column[index, a] = column
+                for lo, hi, word in pieces:
+                    for slot in range(lo, hi, P):
+                        if a <= word + slot - lo < z:
+                            x_column[g, slot] = column + word + slot - lo - a
+                if trio is not None and z == HALF:
+                    for place in range(TRIO):
+                        w_column[TRIO * trio + place] = column + X_WORDS + place * W_WORDS - a
+                column += z - a
+
+        def staged(index, word, count):
+            a = (index % 2) * HALF + word
+            return staging[:, a * PACK : (a + count) * PACK]
 
         def load_plane(g, j):
             nc.sync.dma_start(planes[g][j][:, :T], x_view[g, j])
 
-        def load_w(e):
-            w_raw[e] = w_ring.tile([P, PASSES, PACK * N], F32, name="w_raw")
-            nc.sync.dma_start(w_raw[e][:], w_view[:, PASSES * e : PASSES * (e + 1), :])
+        def new_raw(first, end):
+            tile = raw_pool.tile(
+                [P, (end - first) * W_RAW], F32, name="w_raw%d" % first, offset=first % (EARLY_TRIOS * TRIO) * W_RAW * 4
+            )
+            for e in range(first, end):
+                w_raw[e] = (tile, first)
+
+        def raw(first, end):
+            tile, base = w_raw[first]
+            return tile[:, (first - base) * W_RAW : (end - base) * W_RAW]
+
+        def load_w(first, end):
+            nc.sync.dma_start(
+                raw(first, end).rearrange("p (h c) -> p h c", c=PACK * N), w_view[:, PASSES * first : PASSES * end, :]
+            )
+
+        def load_early(e):
+            new_raw(e, e + 1)
+            load_w(e, e + 1)
+
+        def load_gate(first):
+            count = max(count for lo, count in HELP.values() if lo == first)
+            helped_gate[first] = keep.tile([P, count], F32, name="gate%d" % first)
+            nc.sync.dma_start(helped_gate[first][:], gate[0:P, first : first + count])
 
         def new_chunk(g, lo, hi, buffer):
             tile = keep.tile([P, PACK, hi - lo], F32, name="gathered_" + buffer, align_bytes=64)
@@ -117,98 +151,81 @@ def tile_moe_pre_lin_silu_kernel(tc, xT, w, b, gate, offs, pos1, pos2, out):
             for j in range(PACK):
                 nc.scalar.activation(tile[:, j, :], tokens(PASSES - 1, j, lo, hi), COPY)
 
-        def round_w(e, tile, word):
-            for g in range(PASSES):
-                a = word + g * N
-                nc.gpsimd.tensor_scalar(
-                    tile[:, a * PACK : (a + N) * PACK].rearrange("p (n j) -> p n j", j=PACK),
-                    w_raw[e][:, g, :].rearrange("p (j n) -> p n j", j=PACK),
-                    1.0,
-                    0.0,
-                    MULT,
-                    ADD,
-                )
+        def round_w(first, end):
+            trio, place = divmod(first, TRIO)
+            count = end - first
+            nc.gpsimd.tensor_scalar(
+                staged(trio, X_WORDS + place * W_WORDS, count * W_WORDS).rearrange(
+                    "p (h n j) -> p h n j", n=N, j=PACK
+                ),
+                raw(first, end).rearrange("p (h j n) -> p h n j", n=N, j=PACK),
+                1.0,
+                0.0,
+                MULT,
+                ADD,
+            )
 
-        def times_gate(unit, lo, hi):
-            g, group = place_of(unit)
-            base = vector_part(unit)[0]
-            for first, end, tile in chunks[g]:
-                a, z = max(lo, first), min(hi, end)
-                if a < z:
-                    nc.vector.tensor_tensor(
-                        rounded[unit][:, (a - base) * PACK : (z - base) * PACK].rearrange(
-                            "p (c i j) -> p c j i", i=RUN, j=PACK
-                        ),
-                        tile[:, :, a - first : z - first].rearrange("p j (c i) -> p c j i", i=RUN),
-                        gate_banks[group][:, a - group * GROUP : z - group * GROUP]
-                        .rearrange("p (c i) -> p c i", i=RUN)
-                        .unsqueeze(2)
-                        .to_broadcast([P, (z - a) // RUN, PACK, RUN]),
-                        MULT,
-                    )
+        def vector_pieces(index):
+            first, count = HELP.get(index, (S, 0))
+            result = []
+            for lo, hi, word in SPANS[index][1]:
+                if lo <= first < hi:
+                    parts = ((lo, first), (first + count, hi))
+                else:
+                    parts = ((lo, hi),)
+                result.extend((a, z, word + a - lo) for a, z in parts if a < z)
+            return result
 
-        def multiply_unit(unit):
-            rounded[unit] = rounded_ring.tile([P, GROUP * PACK], BF16, name="rounded", align_bytes=64)
-            lo, hi = vector_part(unit)
-            times_gate(unit, lo, hi if unit < LAST else CHUNKS[-1][0])
-
-        def beside(unit):
-            tile = keep.tile([P, 2 * W_WORDS * PACK], BF16, name="early0", align_bytes=64)
-            if unit not in HELP:
-                e = unit + E - LAST
-                round_w(e, tile, 0)
-                return (tile, 0, W_WORDS, w_codes, w_scales, e * W_WORDS)
-            g, group = place_of(unit)
-            count = HELP[unit]
-            lo = group * GROUP
+        def help_span(index):
+            g, pieces = SPANS[index][:2]
+            lo, count = HELP[index]
+            word = [word + lo - a for a, z, word in pieces if a <= lo < z][0]
             first, end, source = [chunk for chunk in chunks[g] if chunk[0] <= lo < chunk[1]][0]
-            gates = gate_short[:] if unit == LAST else gate_long[:, group - 2, :]
             nc.gpsimd.tensor_tensor(
-                tile[:, 0 : count * PACK].rearrange("p (s j) -> p s j", j=PACK),
+                staged(index, word, count).rearrange("p (s j) -> p s j", j=PACK),
                 source[:, :, lo - first : lo - first + count].rearrange("p j s -> p s j"),
-                gates.unsqueeze(2).to_broadcast([P, count, PACK]),
+                helped_gate[lo][:, 0:count].unsqueeze(2).to_broadcast([P, count, PACK]),
                 MULT,
             )
-            return (tile, 0, count, x_codes, x_scales, g * S + lo)
 
-        def quantize(source, a, z, codes, scales, column):
-            width = max(width for width in WIDTHS if width <= z - a)
-            nc.vector.quantize_mx(
-                out=codes[:, column : column + width].bitcast(FP8X4),
-                scales=scales[:, column : column + width],
-                in_=source[:, a * PACK : (a + width) * PACK],
-            )
-            if a + width < z:
-                quantize(source, a + width, z, codes, scales, column + width)
+        def multiply_span(index):
+            g = SPANS[index][0]
+            for lo, hi, word in vector_pieces(index):
+                for group in range(lo // GROUP, (hi - 1) // GROUP + 1):
+                    for first, end, tile in chunks[g]:
+                        a, z = max(lo, first, group * GROUP), min(hi, end, (group + 1) * GROUP)
+                        if a < z:
+                            nc.vector.tensor_tensor(
+                                staged(index, word + a - lo, z - a).rearrange("p (c i j) -> p c j i", i=RUN, j=PACK),
+                                tile[:, :, a - first : z - first].rearrange("p j (c i) -> p c j i", i=RUN),
+                                gate_banks[group][:, a - group * GROUP : z - group * GROUP]
+                                .rearrange("p (c i) -> p c i", i=RUN)
+                                .unsqueeze(2)
+                                .to_broadcast([P, (z - a) // RUN, PACK, RUN]),
+                                MULT,
+                            )
 
-        def quantize_slots(unit, lo, hi):
-            base = vector_part(unit)[0]
-            quantize(rounded[unit], lo - base, hi - base, x_codes, x_scales, place_of(unit)[0] * S + lo)
-
-        def quantize_unit(unit):
-            quantize_slots(unit, *vector_part(unit))
+        def quantize_span(index):
+            for a, z in SPANS[index][2]:
+                column = call_column[index, a]
+                nc.vector.quantize_mx(
+                    out=codes[:, column : column + z - a].bitcast(FP8X4),
+                    scales=scales[:, column : column + z - a],
+                    in_=staged(index, a, z - a),
+                )
 
         def matmul_pass(g, lo, hi, sums):
-            column = lo // C * W_WORDS + g * N
+            left = w_column[lo // C] + g * N
+            right = x_column[g, lo]
             nc.tensor.matmul_mx(
                 out=sums,
-                lhsT=w_codes[:, column : column + N].bitcast(FP8X4),
-                lhsT_scale=w_scales[:, column : column + N],
-                rhs=x_codes[:, g * S + lo : g * S + hi].bitcast(FP8X4),
-                rhs_scale=x_scales[:, g * S + lo : g * S + hi],
+                lhsT=codes[:, left : left + N].bitcast(FP8X4),
+                lhsT_scale=scales[:, left : left + N],
+                rhs=codes[:, right : right + hi - lo].bitcast(FP8X4),
+                rhs_scale=scales[:, right : right + hi - lo],
                 start=(g == 0),
                 stop=(g == PASSES - 1),
             )
-
-        def matmul_group(unit):
-            g, group = place_of(unit)
-            if g == PASSES - 1:
-                bank = psum.tile([P, GROUP], F32, name="bank%d" % group)
-                for place in range(0, GROUP, C):
-                    lo = group * GROUP + place
-                    for each in range(PASSES):
-                        matmul_pass(each, lo, lo + C, bank[:, place : place + C])
-                    summed.append((lo, bank[:, place : place + C]))
 
         def activate(lo, hi, sums):
             nc.scalar.activation(y[:, lo:hi], sums, SILU, bias=bias[:, lo // C : lo // C + 1])
@@ -227,15 +244,17 @@ def tile_moe_pre_lin_silu_kernel(tc, xT, w, b, gate, offs, pos1, pos2, out):
         nc.sync.dma_start(offs_sb[:], offs)
         load_plane(0, 1)
         nc.sync.dma_start(gate_rows[0 : S // P, :], gate[0, :].rearrange("(c s) -> c s", s=P))
-        load_w(0)
+        load_early(0)
         load_plane(0, 2)
-        load_w(1)
-        load_w(2)
+        load_early(1)
+        load_early(2)
         load_plane(0, 3)
-        for e in range(3, EARLY):
-            load_w(e)
-        nc.sync.dma_start(gate_long[:], gate[0:P, :].rearrange("p (b s) -> p b s", s=GROUP)[:, 2:5, 0:LONG])
-        for j in range(PACK):
+        for e in range(3, 6):
+            load_early(e)
+        load_gate(HELP[0][0])
+        load_plane(1, 0)
+        load_gate(HELP[1][0])
+        for j in range(1, PACK):
             load_plane(1, j)
 
         by_vector = new_chunk(0, 0, VECTOR_SLOTS, "a")
@@ -247,55 +266,71 @@ def tile_moe_pre_lin_silu_kernel(tc, xT, w, b, gate, offs, pos1, pos2, out):
         turned = psum.tile([P, P], F32, name="spare0")
         nc.tensor.transpose(turned[:], gate_rows[:], identity[:])
         nc.vector.tensor_copy(gate_columns[:], turned[:, 0 : S // P])
-        gate_banks = [psum.tile([P, GROUP], F32, name="bank%d" % group) for group in range(GROUPS)]
-        for c in range(S // P):
+        gate_banks = [psum.tile([P, GROUP], F32, name="bank%d" % group) for group in range(S // GROUP)]
+        needed = sorted(
+            set(c for index in range(len(SPANS)) for lo, hi, word in vector_pieces(index) for c in range(lo // P, (hi - 1) // P + 1))
+        )
+        for c in needed:
             group, place = divmod(c * P, GROUP)
             nc.tensor.transpose(
                 gate_banks[group][:, place : place + P], gate_columns[:, c : c + 1].to_broadcast([P, P]), identity[:]
             )
 
-        gather_chunk(0)
-        early = []
-        for pair in range(EARLY // 2):
-            early.append(keep.tile([P, 2 * W_WORDS * PACK], BF16, name="early%d" % pair, align_bytes=64))
-            for place in range(2):
-                round_w(2 * pair + place, early[pair], place * W_WORDS)
-                load_w(2 * pair + place + EARLY)
-        nc.sync.dma_start(gate_short[:], gate[0:P, S - GROUP : S - GROUP + SHORT])
+        for e in range(EARLY_TRIOS * TRIO):
+            round_w(e, e + 1)
+        new_raw(6, 9)
+        new_raw(9, 12)
+        load_w(6, 9)
+        load_w(9, 12)
         nc.sync.dma_start(bias[:], b)
         nc.sync.dma_start(pos1_sb[:], pos1)
         nc.sync.dma_start(pos2_sb[:], pos2)
+        gather_chunk(0)
 
         summed = []
-        multiply_unit(0)
-        for unit in range(LAST):
-            if unit + 1 >= min(HELP):
-                helped = beside(unit + 1)
-            multiply_unit(unit + 1)
-            if unit + 1 in CHUNK_AFTER:
-                gather_chunk(CHUNK_AFTER.index(unit + 1) + 1)
-            quantize_unit(unit)
-            if unit < len(early):
-                quantize(early[unit], 0, 2 * W_WORDS, w_codes, w_scales, 2 * unit * W_WORDS)
-            if min(HELP) <= unit + 1 < LAST:
-                quantize(*helped)
-            matmul_group(unit)
+        banks = {}
+
+        def finish(index):
+            g, pieces = SPANS[index][:2]
+            quantize_span(index)
+            if g == PASSES - 1 and index < len(SPANS) - 3:
+                for first, end, word in sorted(pieces):
+                    for lo in range(first, end, C):
+                        group, place = divmod(lo, GROUP)
+                        if group not in banks:
+                            banks[group] = psum.tile([P, GROUP], F32, name="bank%d" % group)
+                        for each in range(PASSES):
+                            matmul_pass(each, lo, lo + C, banks[group][:, place : place + C])
+                        summed.append((lo, banks[group][:, place : place + C]))
+
+        def produce(index):
+            trio = SPANS[index][3]
+            if index in HELP:
+                help_span(index)
+            if trio is not None and trio >= EARLY_TRIOS:
+                round_w(TRIO * trio, TRIO * (trio + 1))
+            multiply_span(index)
+            for chunk in range(1, len(CHUNKS)):
+                if CHUNK_AFTER[chunk] == index:
+                    gather_chunk(chunk)
+
+        ends = len(SPANS) - 3
+        produce(0)
+        for index in range(ends):
+            produce(index + 1)
+            finish(index)
 
         y = keep.tile([P, S], F32, name="plane10", align_bytes=64)
-        for lo, sums in reversed(summed):
+        for lo, sums in summed:
             activate(lo, lo + C, sums)
 
-        ends = ((S - 2 * C, S - C, "spare0"), (S - C, S - C // 2, "spare1"), (S - C // 2, S, "bank%d" % (GROUPS - 1)))
-        own = vector_part(LAST)[0]
-        times_gate(LAST, CHUNKS[-1][0], S - C)
-        for index, (lo, hi, bank) in enumerate(ends):
-            if index + 1 < len(ends):
-                times_gate(LAST, *ends[index + 1][:2])
+        for index, bank in zip(range(ends, len(SPANS)), ("spare0", "spare1", "bank%d" % (S // GROUP - 1))):
+            if index + 1 < len(SPANS):
+                produce(index + 1)
+            lo, hi = SPANS[index][1][0][:2]
             sums = psum.tile([P, hi - lo], F32, name=bank)
             matmul_pass(0, lo, hi, sums[:])
-            quantize_slots(LAST, max(lo, own), hi)
-            if lo < own:
-                quantize(*helped)
+            quantize_span(index)
             matmul_pass(PASSES - 1, lo, hi, sums[:])
             activate(lo, hi, sums[:])
 
@@ -305,7 +340,7 @@ def tile_moe_pre_lin_silu_kernel(tc, xT, w, b, gate, offs, pos1, pos2, out):
         def results(places, lo, hi):
             return y[:].indirect(places[:, lo // PER_COLUMN : hi // PER_COLUMN])
 
-        pieces = spans(TOKEN_PIECES)
+        pieces = spans_of(TOKEN_PIECES)
         for index, (lo, hi) in enumerate(pieces):
             if index == OWN_PIECE:
                 nc.vector.tensor_copy(first[:, lo:hi], results(pos1_sb, lo, hi))

@@ -28,25 +28,28 @@ W_WORDS = PASSES * N
 W_RAW = PACK * W_WORDS
 GROUP = 512
 TRIO = 3
-X_WORDS = 4 * C
+H = C // 2
+X_WORDS = 4 * C + H
 HALF = X_WORDS + TRIO * W_WORDS
 
-VECTOR_SLOTS = 1472
+VECTOR_SLOTS = 1440
 SPARE = S - VECTOR_SLOTS + 2 * PER_COLUMN - T
 CHUNKS = ((0, 1408, "c"), (1408, 2176, "a"), (2176, 2688, "b"), (2688, S, "c"))
 CHUNK_AFTER = {1: 2, 2: 2, 3: 4}
+LAST = X_WORDS - C
+FULL = ((0, 2 * C), (2 * C, LAST), (LAST, HALF))
 SPANS = (
-    (0, ((0, 3 * C, 0), (4 * C, 5 * C, 3 * C)), ((0, 2 * C), (2 * C, 3 * C), (3 * C, HALF)), 0),
-    (0, ((6 * C, 10 * C, 0),), ((0, 2 * C), (2 * C, 3 * C), (3 * C, HALF)), 1),
-    (0, ((10 * C, 12 * C, 0), (3 * C, 4 * C, 2 * C), (5 * C, 6 * C, 3 * C)), ((0, 2 * C), (2 * C, 3 * C), (3 * C, HALF)), 2),
-    (1, ((0, 4 * C, 0),), ((0, 2 * C), (2 * C, 3 * C), (3 * C, HALF)), 3),
-    (1, ((5 * C, 8 * C, 0), (4 * C, 5 * C, 3 * C)), ((0, 2 * C), (2 * C, 4 * C)), None),
-    (1, ((9 * C, 10 * C, 2 * C), (8 * C, 9 * C, 3 * C)), ((2 * C, 4 * C),), None),
-    (1, ((10 * C, 11 * C, 0),), ((0, C),), None),
-    (1, ((11 * C, 11 * C + C // 2, 0),), ((0, C // 2),), None),
-    (1, ((11 * C + C // 2, S, C),), ((C, C + C // 2),), None),
+    (0, ((0, 3 * C, 0), (4 * C, 5 * C, LAST)), ((0, 2 * C), (2 * C, 3 * C), (LAST, HALF)), 0),
+    (0, ((6 * C, 8 * C, 0), (9 * C, 9 * C + H, 2 * C), (8 * C, 9 * C, LAST)), ((0, 2 * C), (2 * C, 2 * C + H), (LAST, HALF)), 1),
+    (0, ((10 * C, 12 * C, 0), (9 * C + H, 10 * C, 2 * C), (3 * C, 4 * C, 2 * C + H), (5 * C, 6 * C, LAST)), FULL, 2),
+    (1, ((0, 4 * C, 0), (5 * C, 5 * C + H, 4 * C)), FULL, 3),
+    (1, ((5 * C + H, 8 * C, C), (4 * C, 5 * C, LAST)), ((C, 3 * C), (3 * C, X_WORDS)), None),
+    (1, ((9 * C, 10 * C, LAST - C), (8 * C, 9 * C, LAST)), ((LAST - C, X_WORDS),), None),
+    (1, ((10 * C, 11 * C, 3 * C),), ((3 * C, 4 * C),), None),
+    (1, ((11 * C, 11 * C + H, 0),), ((0, H),), None),
+    (1, ((11 * C + H, S, 0),), ((0, H),), None),
 )
-HELP = {0: (4 * C, 256), 1: (8 * C, 160), 4: (4 * C, 256), 5: (8 * C, 128)}
+HELP = {0: (4 * C, 256), 1: (8 * C, 128), 4: (4 * C, 224), 5: (8 * C, 128), 6: (10 * C, 64)}
 EARLY_TRIOS = 2
 TOKEN_PIECES = (192, 192, 384, 384, 192, 192)
 OWN_PIECE = 1
@@ -282,26 +285,32 @@ def tile_moe_pre_lin_silu_kernel(tc, xT, w, b, gate, offs, pos1, pos2, out):
         new_raw(9, 12)
         load_w(6, 9)
         load_w(9, 12)
+        load_gate(HELP[6][0])
         nc.sync.dma_start(bias[:], b)
         nc.sync.dma_start(pos1_sb[:], pos1)
         nc.sync.dma_start(pos2_sb[:], pos2)
         gather_chunk(0)
 
         summed = []
-        banks = {}
+        done = set()
 
         def finish(index):
             g, pieces = SPANS[index][:2]
             quantize_span(index)
-            if g == PASSES - 1 and index < len(SPANS) - 3:
-                for first, end, word in sorted(pieces):
-                    for lo in range(first, end, C):
-                        group, place = divmod(lo, GROUP)
-                        if group not in banks:
-                            banks[group] = psum.tile([P, GROUP], F32, name="bank%d" % group)
-                        for each in range(PASSES):
-                            matmul_pass(each, lo, lo + C, banks[group][:, place : place + C])
-                        summed.append((lo, banks[group][:, place : place + C]))
+            if g == PASSES - 1:
+                done.update(slot for lo, hi, word in pieces for slot in range(lo, hi, H))
+                for group in range(len(summed) * C // GROUP, S // GROUP):
+                    if all(slot in done for slot in range(group * GROUP, (group + 1) * GROUP, H)):
+                        bank = psum.tile([P, GROUP], F32, name="bank%d" % group)
+                        for place in range(0, GROUP, C):
+                            lo = group * GROUP + place
+                            whole = all(x_column[each, lo + H] == x_column[each, lo] + H for each in range(PASSES))
+                            width = C if whole else H
+                            for part in range(0, C, width):
+                                for each in range(PASSES):
+                                    at = place + part
+                                    matmul_pass(each, lo + part, lo + part + width, bank[:, at : at + width])
+                            summed.append((lo, bank[:, place : place + C]))
 
         def produce(index):
             trio = SPANS[index][3]
@@ -316,17 +325,19 @@ def tile_moe_pre_lin_silu_kernel(tc, xT, w, b, gate, offs, pos1, pos2, out):
 
         ends = len(SPANS) - 3
         produce(0)
-        for index in range(ends):
+        for index in range(ends - 1):
             produce(index + 1)
             finish(index)
+        produce(ends + 1)
+        produce(ends)
+        finish(ends - 1)
+        produce(ends + 2)
 
         y = keep.tile([P, S], F32, name="plane10", align_bytes=64)
         for lo, sums in summed:
             activate(lo, lo + C, sums)
 
         for index, bank in zip(range(ends, len(SPANS)), ("spare0", "spare1", "bank%d" % (S // GROUP - 1))):
-            if index + 1 < len(SPANS):
-                produce(index + 1)
             lo, hi = SPANS[index][1][0][:2]
             sums = psum.tile([P, hi - lo], F32, name=bank)
             matmul_pass(0, lo, hi, sums[:])

@@ -32,7 +32,7 @@ H = C // 2
 X_WORDS = 4 * C + H
 HALF = X_WORDS + TRIO * W_WORDS
 
-VECTOR_SLOTS = 1440
+VECTOR_SLOTS = 1472
 SPARE = S - VECTOR_SLOTS + 2 * PER_COLUMN - T
 CHUNKS = ((0, 1408, "c"), (1408, 2176, "a"), (2176, 2688, "b"), (2688, S, "c"))
 CHUNK_AFTER = {1: 2, 2: 2, 3: 4}

@@ -32,10 +32,10 @@ H = C // 2
 X_WORDS = 4 * C + H
 HALF = X_WORDS + TRIO * W_WORDS
 
-VECTOR_SLOTS = 1472
+VECTOR_SLOTS = 1536
 SPARE = S - VECTOR_SLOTS + 2 * PER_COLUMN - T
-CHUNKS = ((0, 1408, "c"), (1408, 2176, "a"), (2176, 2688, "b"), (2688, S, "c"))
-CHUNK_AFTER = {1: 2, 2: 2, 3: 4}
+CHUNKS = ((0, 1408, "c"), (1408, 2176, "a"), (2176, 2688, "a"), (2688, S, "a"))
+CHUNK_AFTER = {1: 2, 2: 2, 3: 2}
 LAST = X_WORDS - C
 FULL = ((0, 2 * C), (2 * C, LAST), (LAST, HALF))
 SPANS = (
@@ -43,13 +43,13 @@ SPANS = (
     (0, ((6 * C, 8 * C, 0), (9 * C, 9 * C + H, 2 * C), (8 * C, 9 * C, LAST)), ((0, 2 * C), (2 * C, 2 * C + H), (LAST, HALF)), 1),
     (0, ((10 * C, 12 * C, 0), (9 * C + H, 10 * C, 2 * C), (3 * C, 4 * C, 2 * C + H), (5 * C, 6 * C, LAST)), FULL, 2),
     (1, ((0, 4 * C, 0), (5 * C, 5 * C + H, 4 * C)), FULL, 3),
-    (1, ((5 * C + H, 8 * C, C), (4 * C, 5 * C, LAST)), ((C, 3 * C), (3 * C, X_WORDS)), None),
+    (1, ((5 * C + H, 8 * C, C), (4 * C, 5 * C, LAST)), ((3 * C, X_WORDS), (C, 3 * C)), None),
     (1, ((9 * C, 10 * C, LAST - C), (8 * C, 9 * C, LAST)), ((LAST - C, X_WORDS),), None),
-    (1, ((10 * C, 11 * C, 3 * C),), ((3 * C, 4 * C),), None),
-    (1, ((11 * C, 11 * C + H, 0),), ((0, H),), None),
-    (1, ((11 * C + H, S, 0),), ((0, H),), None),
+    (1, ((10 * C, 11 * C, 3 * C - 80),), ((3 * C - 80, 4 * C - 80),), None),
+    (1, ((11 * C, 11 * C + H, C),), ((C, C + H),), None),
+    (1, ((11 * C + H, S, C + H),), ((C + H, 2 * C),), None),
 )
-HELP = {0: (4 * C, 256), 1: (8 * C, 128), 4: (4 * C, 224), 5: (8 * C, 128), 6: (10 * C, 64)}
+HELP = {0: (4 * C, 256), 1: (8 * C, 192), 4: (4 * C, 240), 5: (8 * C, 128), 6: (10 * C, 80)}
 EARLY_TRIOS = 2
 TOKEN_PIECES = (192, 192, 384, 384, 192, 192)
 OWN_PIECE = 1
@@ -92,6 +92,7 @@ def tile_moe_pre_lin_silu_kernel(tc, xT, w, b, gate, offs, pos1, pos2, out):
         w_view = w.rearrange("e (g p j) n -> p (e g) (j n)", g=PASSES, j=PACK)
         chunks = [[], []]
         helped_gate = {}
+        buffers = {}
         w_raw = {}
 
         call_column, x_column, w_column = {}, {}, {}
@@ -109,7 +110,7 @@ def tile_moe_pre_lin_silu_kernel(tc, xT, w, b, gate, offs, pos1, pos2, out):
                 column += z - a
 
         def staged(index, word, count):
-            a = (index % 2) * HALF + word
+            a = (index % 2 if index < len(SPANS) - 3 else 0) * HALF + word
             return staging[:, a * PACK : (a + count) * PACK]
 
         def load_plane(g, j):
@@ -141,9 +142,14 @@ def tile_moe_pre_lin_silu_kernel(tc, xT, w, b, gate, offs, pos1, pos2, out):
             nc.sync.dma_start(helped_gate[first][:], gate[0:P, first : first + count])
 
         def new_chunk(g, lo, hi, buffer):
-            tile = keep.tile([P, PACK, hi - lo], F32, name="gathered_" + buffer, align_bytes=64)
-            chunks[g].append((lo, hi, tile))
-            return tile
+            if (g, buffer) not in buffers:
+                ends = [z for a, z, name in CHUNKS if name == buffer] if g else [hi]
+                tile = keep.tile([P, PACK * (max(ends) - lo)], F32, name="gathered_" + buffer, align_bytes=64)
+                buffers[g, buffer] = (lo, tile)
+            base, tile = buffers[g, buffer]
+            view = tile[:, PACK * (lo - base) : PACK * (hi - base)].rearrange("p (j s) -> p j s", j=PACK)
+            chunks[g].append((lo, hi, view))
+            return view
 
         def tokens(g, j, lo, hi):
             return planes[g][j][:].indirect(offs_sb[:, lo // PER_COLUMN : hi // PER_COLUMN])
@@ -254,8 +260,8 @@ def tile_moe_pre_lin_silu_kernel(tc, xT, w, b, gate, offs, pos1, pos2, out):
         load_plane(0, 3)
         for e in range(3, 6):
             load_early(e)
-        load_gate(HELP[0][0])
         load_plane(1, 0)
+        load_gate(HELP[0][0])
         load_gate(HELP[1][0])
         for j in range(1, PACK):
             load_plane(1, j)
@@ -263,7 +269,9 @@ def tile_moe_pre_lin_silu_kernel(tc, xT, w, b, gate, offs, pos1, pos2, out):
         by_vector = new_chunk(0, 0, VECTOR_SLOTS, "a")
         by_scalar = new_chunk(0, VECTOR_SLOTS, S, "b")
         for j in range(PACK):
-            nc.vector.tensor_copy(by_vector[:, j, :], tokens(0, j, 0, VECTOR_SLOTS))
+            cuts = (0, VECTOR_SLOTS) if j < PACK - 1 else (0, 3 * C, VECTOR_SLOTS)
+            for lo, hi in zip(cuts, cuts[1:]):
+                nc.vector.tensor_copy(by_vector[:, j, lo:hi], tokens(0, j, lo, hi))
             nc.scalar.activation(by_scalar[:, j, :], tokens(0, j, VECTOR_SLOTS, S), COPY)
 
         turned = psum.tile([P, P], F32, name="spare0")
@@ -328,10 +336,9 @@ def tile_moe_pre_lin_silu_kernel(tc, xT, w, b, gate, offs, pos1, pos2, out):
         for index in range(ends - 1):
             produce(index + 1)
             finish(index)
-        produce(ends + 1)
         produce(ends)
+        produce(ends + 1)
         finish(ends - 1)
-        produce(ends + 2)
 
         y = keep.tile([P, S], F32, name="plane10", align_bytes=64)
         for lo, sums in summed:
@@ -342,6 +349,8 @@ def tile_moe_pre_lin_silu_kernel(tc, xT, w, b, gate, offs, pos1, pos2, out):
             sums = psum.tile([P, hi - lo], F32, name=bank)
             matmul_pass(0, lo, hi, sums[:])
             quantize_span(index)
+            if index == ends:
+                produce(ends + 2)
             matmul_pass(PASSES - 1, lo, hi, sums[:])
             activate(lo, hi, sums[:])
 

@@ -37,21 +37,21 @@ SPARE = S - VECTOR_SLOTS + 2 * PER_COLUMN - T
 CHUNKS = ((0, 1408, "c"), (1408, 2176, "a"), (2176, 2688, "a"), (2688, S, "a"))
 CHUNK_AFTER = {1: 2, 2: 2, 3: 2}
 LAST = X_WORDS - C
-FULL = ((0, 2 * C), (2 * C, LAST), (LAST, HALF))
+FULL = ((2 * C, LAST), (LAST, HALF), (0, 2 * C))
 SPANS = (
-    (0, ((0, 3 * C, 0), (4 * C, 5 * C, LAST)), ((0, 2 * C), (2 * C, 3 * C), (LAST, HALF)), 0),
-    (0, ((6 * C, 8 * C, 0), (9 * C, 9 * C + H, 2 * C), (8 * C, 9 * C, LAST)), ((0, 2 * C), (2 * C, 2 * C + H), (LAST, HALF)), 1),
-    (0, ((10 * C, 12 * C, 0), (9 * C + H, 10 * C, 2 * C), (3 * C, 4 * C, 2 * C + H), (5 * C, 6 * C, LAST)), FULL, 2),
-    (1, ((0, 4 * C, 0), (5 * C, 5 * C + H, 4 * C)), FULL, 3),
-    (1, ((5 * C + H, 8 * C, C), (4 * C, 5 * C, LAST)), ((3 * C, X_WORDS), (C, 3 * C)), None),
+    (0, ((0, 3 * C, 0), (4 * C, 5 * C, LAST)), ((2 * C, 3 * C), (LAST, HALF), (0, 2 * C)), 0),
+    (0, ((6 * C, 8 * C, 0), (9 * C, 9 * C + H, 2 * C), (8 * C, 9 * C, LAST)), ((2 * C, 2 * C + H), (LAST, HALF), (0, 2 * C)), 1),
+    (0, ((9 * C + H, 10 * C, 2 * C), (3 * C, 4 * C, 2 * C + H), (10 * C, 12 * C, 0), (5 * C, 6 * C, LAST)), FULL, 2),
+    (1, ((2 * C, 4 * C, 2 * C), (0, 2 * C, 0), (5 * C, 5 * C + H, 4 * C)), FULL, 3),
+    (1, ((5 * C + H, 6 * C, 3 * C), (6 * C, 8 * C, C), (4 * C, 5 * C, LAST)), ((3 * C, X_WORDS), (C, 3 * C)), None),
     (1, ((9 * C, 10 * C, LAST - C), (8 * C, 9 * C, LAST)), ((LAST - C, X_WORDS),), None),
-    (1, ((10 * C, 11 * C, 3 * C - 80),), ((3 * C - 80, 4 * C - 80),), None),
+    (1, ((10 * C, 11 * C, 3 * C),), ((3 * C, 4 * C),), None),
     (1, ((11 * C, 11 * C + H, C),), ((C, C + H),), None),
     (1, ((11 * C + H, S, C + H),), ((C + H, 2 * C),), None),
 )
-HELP = {0: (4 * C, 256), 1: (8 * C, 192), 4: (4 * C, 240), 5: (8 * C, 128), 6: (10 * C, 80)}
+HELP = {0: (4 * C, 256), 1: (8 * C, 224), 4: (4 * C, 256), 5: (8 * C, 128), 6: (10 * C, 96)}
 EARLY_TRIOS = 2
-TOKEN_PIECES = (192, 192, 384, 384, 192, 192)
+TOKEN_PIECES = (192, 256, 384, 320, 192, 192)
 OWN_PIECE = 1
 
 

@@ -49,7 +49,7 @@ SPANS = (
     (1, ((11 * C, 11 * C + H, C),), ((C, C + H),), None),
     (1, ((11 * C + H, S, C + H),), ((C + H, 2 * C),), None),
 )
-HELP = {0: (4 * C, 256), 1: (8 * C, 224), 4: (4 * C, 256), 5: (8 * C, 128), 6: (10 * C, 96)}
+HELP = {0: (4 * C, 256), 1: (8 * C, 160), 4: (4 * C, 256), 5: (8 * C, 128), 6: (10 * C, 96)}
 EARLY_TRIOS = 2
 TOKEN_PIECES = (192, 256, 384, 320, 192, 192)
 OWN_PIECE = 1

@@ -32,7 +32,7 @@ H = C // 2
 X_WORDS = 4 * C + H
 HALF = X_WORDS + TRIO * W_WORDS
 
-VECTOR_SLOTS = 1536
+VECTOR_SLOTS = 1504
 SPARE = S - VECTOR_SLOTS + 2 * PER_COLUMN - T
 CHUNKS = ((0, 1408, "c"), (1408, 2176, "a"), (2176, 2688, "a"), (2688, S, "a"))
 CHUNK_AFTER = {1: 2, 2: 2, 3: 2}
@@ -45,11 +45,11 @@ SPANS = (
     (1, ((2 * C, 4 * C, 2 * C), (0, 2 * C, 0), (5 * C, 5 * C + H, 4 * C)), FULL, 3),
     (1, ((5 * C + H, 6 * C, 3 * C), (6 * C, 8 * C, C), (4 * C, 5 * C, LAST)), ((3 * C, X_WORDS), (C, 3 * C)), None),
     (1, ((9 * C, 10 * C, LAST - C), (8 * C, 9 * C, LAST)), ((LAST - C, X_WORDS),), None),
-    (1, ((10 * C, 11 * C, 3 * C),), ((3 * C, 4 * C),), None),
-    (1, ((11 * C, 11 * C + H, C),), ((C, C + H),), None),
-    (1, ((11 * C + H, S, C + H),), ((C + H, 2 * C),), None),
+    (1, ((10 * C, 11 * C, C),), ((C, 2 * C),), None),
+    (1, ((11 * C, 11 * C + H, 2 * C),), ((2 * C, 2 * C + H),), None),
+    (1, ((11 * C + H, S, 2 * C + H),), ((2 * C + H, 3 * C),), None),
 )
-HELP = {0: (4 * C, 256), 1: (8 * C, 160), 4: (4 * C, 256), 5: (8 * C, 128), 6: (10 * C, 96)}
+HELP = {0: (4 * C, 256), 1: (8 * C, 176), 4: (4 * C, 256), 5: (8 * C, 128), 6: (10 * C, 96)}
 EARLY_TRIOS = 2
 TOKEN_PIECES = (192, 256, 384, 320, 192, 192)
 OWN_PIECE = 1
@@ -336,9 +336,9 @@ def tile_moe_pre_lin_silu_kernel(tc, xT, w, b, gate, offs, pos1, pos2, out):
         for index in range(ends - 1):
             produce(index + 1)
             finish(index)
+        finish(ends - 1)
         produce(ends)
         produce(ends + 1)
-        finish(ends - 1)
 
         y = keep.tile([P, S], F32, name="plane10", align_bytes=64)
         for lo, sums in summed:

@@ -27,47 +27,51 @@ RUN = 2
 W_WORDS = PASSES * N
 W_RAW = PACK * W_WORDS
 GROUP = 512
-TRIO = 3
+CALL = 1024
 H = C // 2
-X_WORDS = 4 * C + H
-HALF = X_WORDS + TRIO * W_WORDS
 
-VECTOR_SLOTS = 1504
-SPARE = S - VECTOR_SLOTS + 2 * PER_COLUMN - T
-CHUNKS = ((0, 1408, "c"), (1408, 2176, "a"), (2176, 2688, "a"), (2688, S, "a"))
-CHUNK_AFTER = {1: 2, 2: 2, 3: 2}
-LAST = X_WORDS - C
-FULL = ((2 * C, LAST), (LAST, HALF), (0, 2 * C))
-SPANS = (
-    (0, ((0, 3 * C, 0), (4 * C, 5 * C, LAST)), ((2 * C, 3 * C), (LAST, HALF), (0, 2 * C)), 0),
-    (0, ((6 * C, 8 * C, 0), (9 * C, 9 * C + H, 2 * C), (8 * C, 9 * C, LAST)), ((2 * C, 2 * C + H), (LAST, HALF), (0, 2 * C)), 1),
-    (0, ((9 * C + H, 10 * C, 2 * C), (3 * C, 4 * C, 2 * C + H), (10 * C, 12 * C, 0), (5 * C, 6 * C, LAST)), FULL, 2),
-    (1, ((2 * C, 4 * C, 2 * C), (0, 2 * C, 0), (5 * C, 5 * C + H, 4 * C)), FULL, 3),
-    (1, ((5 * C + H, 6 * C, 3 * C), (6 * C, 8 * C, C), (4 * C, 5 * C, LAST)), ((3 * C, X_WORDS), (C, 3 * C)), None),
-    (1, ((9 * C, 10 * C, LAST - C), (8 * C, 9 * C, LAST)), ((LAST - C, X_WORDS),), None),
-    (1, ((10 * C, 11 * C, C),), ((C, 2 * C),), None),
-    (1, ((11 * C, 11 * C + H, 2 * C),), ((2 * C, 2 * C + H),), None),
-    (1, ((11 * C + H, S, 2 * C + H),), ((2 * C + H, 3 * C),), None),
-)
-HELP = {0: (4 * C, 256), 1: (8 * C, 176), 4: (4 * C, 256), 5: (8 * C, 128), 6: (10 * C, 96)}
-EARLY_TRIOS = 2
+EARLY = 7
+SINGLES = 5
+SCALAR_SLOTS = 1536
+SPARE = max(SCALAR_SLOTS, S - SCALAR_SLOTS) + 2 * PER_COLUMN - T
+HELP_FIRST = 832
+HELP_THIRD = 128
+HELP_LAST = 96
+FIRST_CHUNK = 1152
+SECOND_END = 8 * C
+CHUNKS = ((0, FIRST_CHUNK), (FIRST_CHUNK, SECOND_END), (SECOND_END, 10 * C + H), (10 * C + H, S))
 TOKEN_PIECES = (192, 256, 384, 320, 192, 192)
 OWN_PIECE = 1
 
+EARLY_WORDS = EARLY * W_WORDS
+STAGED = EARLY_WORDS + S
+LOW = EARLY_WORDS + CALL
+THIRD = LOW + CALL
 
-def spans_of(widths):
-    result, start = [], 0
-    for width in widths:
-        result.append((start, start + width))
-        start += width
-    return result
+
+def word_of(g, slot):
+    if g == 0:
+        return LOW + slot if slot < 2 * CALL else EARLY_WORDS + slot - 2 * CALL
+    if slot < SECOND_END:
+        return slot
+    if slot < 10 * C:
+        return THIRD + slot - SECOND_END
+    if slot < 11 * C:
+        return THIRD + slot - 10 * C
+    return slot - 11 * C
+
+
+def weight_word(e):
+    if e >= EARLY:
+        return LOW + (e - EARLY) * W_WORDS
+    return (e - SINGLES) % EARLY * W_WORDS
 
 
 def tile_moe_pre_lin_silu_kernel(tc, xT, w, b, gate, offs, pos1, pos2, out):
     nc = tc.nc
     with ExitStack() as ctx:
         keep = ctx.enter_context(tc.tile_pool(name="keep", bufs=1))
-        raw_pool = ctx.enter_context(tc.tile_pool(name="raw_pool", bufs=1))
+        shared = ctx.enter_context(tc.tile_pool(name="shared", bufs=1))
         psum = ctx.enter_context(tc.psum_pool(name="psum", bufs=1))
 
         offs_sb = keep.tile([P, S // PER_COLUMN], U16, name="offs_sb")
@@ -77,153 +81,109 @@ def tile_moe_pre_lin_silu_kernel(tc, xT, w, b, gate, offs, pos1, pos2, out):
         identity = keep.tile([P, P], F32, name="identity")
         gate_rows = keep.tile([P, P], F32, name="gate_rows")
         gate_columns = keep.tile([P, S // P], F32, name="gate_columns")
-        planes = [
-            [
-                keep.tile([P, T + (SPARE if g == 0 else 0)], F32, name="plane%d%d" % (g, j), align_bytes=64)
-                for j in range(PACK)
-            ]
-            for g in range(PASSES)
-        ]
-        staging = keep.tile([P, 2 * HALF * PACK], BF16, name="staging", align_bytes=64)
+        staging = keep.tile([P, STAGED * PACK], BF16, name="staging", align_bytes=64)
         codes = keep.tile([P, PASSES * S + E * W_WORDS], U32, name="codes", align_bytes=64)
         scales = keep.tile([P, PASSES * S + E * W_WORDS], U8, name="scales", align_bytes=64)
 
+        wide = T + SPARE
+        second_planes = PACK * wide
+        gathered_at = second_planes + PACK * T
+        raw_at = gathered_at + PACK * S
+
+        def placed(name, first, width):
+            return shared.tile([P, width], F32, name=name, offset=4 * first)
+
+        planes = [
+            [placed("plane0%d" % j, j * wide, wide) for j in range(PACK)],
+            [placed("plane1%d" % j, second_planes + j * T, T) for j in range(PACK)],
+        ]
         x_view = xT.rearrange("(g p j) t -> g j p t", g=PASSES, j=PACK)
         w_view = w.rearrange("e (g p j) n -> p (e g) (j n)", g=PASSES, j=PACK)
         chunks = [[], []]
         helped_gate = {}
-        buffers = {}
-        w_raw = {}
+        raw = {}
+        x_column, w_column = {}, {}
+        used = [0]
 
-        call_column, x_column, w_column = {}, {}, {}
-        column = 0
-        for index, (g, pieces, calls, trio) in enumerate(SPANS):
-            for a, z in calls:
-                call_column[index, a] = column
-                for lo, hi, word in pieces:
-                    for slot in range(lo, hi, P):
-                        if a <= word + slot - lo < z:
-                            x_column[g, slot] = column + word + slot - lo - a
-                if trio is not None and z == HALF:
-                    for place in range(TRIO):
-                        w_column[TRIO * trio + place] = column + X_WORDS + place * W_WORDS - a
-                column += z - a
-
-        def staged(index, word, count):
-            a = (index % 2 if index < len(SPANS) - 3 else 0) * HALF + word
-            return staging[:, a * PACK : (a + count) * PACK]
+        def staged(word, count):
+            return staging[:, word * PACK : (word + count) * PACK]
 
         def load_plane(g, j):
             nc.sync.dma_start(planes[g][j][:, :T], x_view[g, j])
 
-        def new_raw(first, end):
-            tile = raw_pool.tile(
-                [P, (end - first) * W_RAW], F32, name="w_raw%d" % first, offset=first % (EARLY_TRIOS * TRIO) * W_RAW * 4
-            )
-            for e in range(first, end):
-                w_raw[e] = (tile, first)
-
-        def raw(first, end):
-            tile, base = w_raw[first]
-            return tile[:, (first - base) * W_RAW : (end - base) * W_RAW]
-
         def load_w(first, end):
+            place = first % EARLY
+            raw[first] = placed("raw%d" % first, raw_at + place * W_RAW, (end - first) * W_RAW)
             nc.sync.dma_start(
-                raw(first, end).rearrange("p (h c) -> p h c", c=PACK * N), w_view[:, PASSES * first : PASSES * end, :]
+                raw[first][:].rearrange("p (h c) -> p h c", c=PACK * N), w_view[:, PASSES * first : PASSES * end, :]
             )
 
-        def load_early(e):
-            new_raw(e, e + 1)
-            load_w(e, e + 1)
-
-        def load_gate(first):
-            count = max(count for lo, count in HELP.values() if lo == first)
+        def load_gate(first, count):
             helped_gate[first] = keep.tile([P, count], F32, name="gate%d" % first)
             nc.sync.dma_start(helped_gate[first][:], gate[0:P, first : first + count])
 
-        def new_chunk(g, lo, hi, buffer):
-            if (g, buffer) not in buffers:
-                ends = [z for a, z, name in CHUNKS if name == buffer] if g else [hi]
-                tile = keep.tile([P, PACK * (max(ends) - lo)], F32, name="gathered_" + buffer, align_bytes=64)
-                buffers[g, buffer] = (lo, tile)
-            base, tile = buffers[g, buffer]
-            view = tile[:, PACK * (lo - base) : PACK * (hi - base)].rearrange("p (j s) -> p j s", j=PACK)
-            chunks[g].append((lo, hi, view))
-            return view
+        def planes_of(tile, first, lo, hi):
+            return tile[:, PACK * (lo - first) : PACK * (hi - first)].rearrange("p (j s) -> p j s", j=PACK)
 
         def tokens(g, j, lo, hi):
             return planes[g][j][:].indirect(offs_sb[:, lo // PER_COLUMN : hi // PER_COLUMN])
 
-        def gather_chunk(index):
-            lo, hi, buffer = CHUNKS[index]
-            tile = new_chunk(PASSES - 1, lo, hi, buffer)
+        def gather_chunk(tile, first, lo, hi):
+            view = planes_of(tile, first, lo, hi)
+            chunks[1].append((lo, hi, view))
             for j in range(PACK):
-                nc.scalar.activation(tile[:, j, :], tokens(PASSES - 1, j, lo, hi), COPY)
+                nc.scalar.activation(view[:, j, :], tokens(1, j, lo, hi), COPY)
 
         def round_w(first, end):
-            trio, place = divmod(first, TRIO)
-            count = end - first
             nc.gpsimd.tensor_scalar(
-                staged(trio, X_WORDS + place * W_WORDS, count * W_WORDS).rearrange(
-                    "p (h n j) -> p h n j", n=N, j=PACK
-                ),
-                raw(first, end).rearrange("p (h j n) -> p h n j", n=N, j=PACK),
+                staged(weight_word(first), (end - first) * W_WORDS).rearrange("p (h n j) -> p h n j", n=N, j=PACK),
+                raw[first][:].rearrange("p (h j n) -> p h n j", n=N, j=PACK),
                 1.0,
                 0.0,
                 MULT,
                 ADD,
             )
 
-        def vector_pieces(index):
-            first, count = HELP.get(index, (S, 0))
-            result = []
-            for lo, hi, word in SPANS[index][1]:
-                if lo <= first < hi:
-                    parts = ((lo, first), (first + count, hi))
-                else:
-                    parts = ((lo, hi),)
-                result.extend((a, z, word + a - lo) for a, z in parts if a < z)
-            return result
-
-        def help_span(index):
-            g, pieces = SPANS[index][:2]
-            lo, count = HELP[index]
-            word = [word + lo - a for a, z, word in pieces if a <= lo < z][0]
+        def help_multiply(g, lo, count):
             first, end, source = [chunk for chunk in chunks[g] if chunk[0] <= lo < chunk[1]][0]
             nc.gpsimd.tensor_tensor(
-                staged(index, word, count).rearrange("p (s j) -> p s j", j=PACK),
+                staged(word_of(g, lo), count).rearrange("p (s j) -> p s j", j=PACK),
                 source[:, :, lo - first : lo - first + count].rearrange("p j s -> p s j"),
-                helped_gate[lo][:, 0:count].unsqueeze(2).to_broadcast([P, count, PACK]),
+                helped_gate[lo][:].unsqueeze(2).to_broadcast([P, count, PACK]),
                 MULT,
             )
 
-        def multiply_span(index):
-            g = SPANS[index][0]
-            for lo, hi, word in vector_pieces(index):
-                for group in range(lo // GROUP, (hi - 1) // GROUP + 1):
-                    for first, end, tile in chunks[g]:
-                        a, z = max(lo, first, group * GROUP), min(hi, end, (group + 1) * GROUP)
-                        if a < z:
-                            nc.vector.tensor_tensor(
-                                staged(index, word + a - lo, z - a).rearrange("p (c i j) -> p c j i", i=RUN, j=PACK),
-                                tile[:, :, a - first : z - first].rearrange("p j (c i) -> p c j i", i=RUN),
-                                gate_banks[group][:, a - group * GROUP : z - group * GROUP]
-                                .rearrange("p (c i) -> p c i", i=RUN)
-                                .unsqueeze(2)
-                                .to_broadcast([P, (z - a) // RUN, PACK, RUN]),
-                                MULT,
-                            )
+        def multiply(g, lo, hi):
+            for group in range(lo // GROUP, (hi - 1) // GROUP + 1):
+                for first, end, tile in chunks[g]:
+                    a, z = max(lo, first, group * GROUP), min(hi, end, (group + 1) * GROUP)
+                    if a < z:
+                        nc.vector.tensor_tensor(
+                            staged(word_of(g, a), z - a).rearrange("p (c i j) -> p c j i", i=RUN, j=PACK),
+                            tile[:, :, a - first : z - first].rearrange("p j (c i) -> p c j i", i=RUN),
+                            gate_banks[group][:, a - group * GROUP : z - group * GROUP]
+                            .rearrange("p (c i) -> p c i", i=RUN)
+                            .unsqueeze(2)
+                            .to_broadcast([P, (z - a) // RUN, PACK, RUN]),
+                            MULT,
+                        )
 
-        def quantize_span(index):
-            for a, z in SPANS[index][2]:
-                column = call_column[index, a]
-                nc.vector.quantize_mx(
-                    out=codes[:, column : column + z - a].bitcast(FP8X4),
-                    scales=scales[:, column : column + z - a],
-                    in_=staged(index, a, z - a),
-                )
+        def quantize(g, slots, experts, a, z):
+            column = used[0]
+            used[0] = column + z - a
+            for slot in range(slots[0], slots[1], H):
+                if a <= word_of(g, slot) < z:
+                    x_column[g, slot] = column + word_of(g, slot) - a
+            for e in experts:
+                if a <= weight_word(e) < z:
+                    w_column[e] = column + weight_word(e) - a
+            nc.vector.quantize_mx(
+                out=codes[:, column : column + z - a].bitcast(FP8X4),
+                scales=scales[:, column : column + z - a],
+                in_=staged(a, z - a),
+            )
 
-        def matmul_pass(g, lo, hi, sums):
+        def matmul_pass(g, lo, hi, sums, start, stop):
             left = w_column[lo // C] + g * N
             right = x_column[g, lo]
             nc.tensor.matmul_mx(
@@ -232,8 +192,8 @@ def tile_moe_pre_lin_silu_kernel(tc, xT, w, b, gate, offs, pos1, pos2, out):
                 lhsT_scale=scales[:, left : left + N],
                 rhs=codes[:, right : right + hi - lo].bitcast(FP8X4),
                 rhs_scale=scales[:, right : right + hi - lo],
-                start=(g == 0),
-                stop=(g == PASSES - 1),
+                start=start,
+                stop=stop,
             )
 
         def activate(lo, hi, sums):
@@ -251,122 +211,125 @@ def tile_moe_pre_lin_silu_kernel(tc, xT, w, b, gate, offs, pos1, pos2, out):
 
         load_plane(0, 0)
         nc.sync.dma_start(offs_sb[:], offs)
+        load_w(0, 1)
         load_plane(0, 1)
         nc.sync.dma_start(gate_rows[0 : S // P, :], gate[0, :].rearrange("(c s) -> c s", s=P))
-        load_early(0)
+        load_w(1, 2)
+        load_w(2, 3)
         load_plane(0, 2)
-        load_early(1)
-        load_early(2)
+        load_w(3, 4)
         load_plane(0, 3)
-        for e in range(3, 6):
-            load_early(e)
-        load_plane(1, 0)
-        load_gate(HELP[0][0])
-        load_gate(HELP[1][0])
-        for j in range(1, PACK):
-            load_plane(1, j)
-
-        by_vector = new_chunk(0, 0, VECTOR_SLOTS, "a")
-        by_scalar = new_chunk(0, VECTOR_SLOTS, S, "b")
+        load_w(4, 5)
+        load_gate(0, HELP_FIRST)
         for j in range(PACK):
-            cuts = (0, VECTOR_SLOTS) if j < PACK - 1 else (0, 3 * C, VECTOR_SLOTS)
+            load_plane(1, j)
+        load_w(SINGLES, EARLY)
+
+        by_scalar = planes_of(placed("by_scalar", gathered_at, PACK * SCALAR_SLOTS), 0, 0, SCALAR_SLOTS)
+        by_vector = planes_of(
+            placed("by_vector", gathered_at + PACK * SCALAR_SLOTS, PACK * (S - SCALAR_SLOTS)),
+            SCALAR_SLOTS,
+            SCALAR_SLOTS,
+            S,
+        )
+        chunks[0].extend(((0, SCALAR_SLOTS, by_scalar), (SCALAR_SLOTS, S, by_vector)))
+        for j in range(PACK):
+            cuts = (SCALAR_SLOTS, S) if j < PACK - 1 else (SCALAR_SLOTS, 2 * CALL, S)
             for lo, hi in zip(cuts, cuts[1:]):
-                nc.vector.tensor_copy(by_vector[:, j, lo:hi], tokens(0, j, lo, hi))
-            nc.scalar.activation(by_scalar[:, j, :], tokens(0, j, VECTOR_SLOTS, S), COPY)
+                nc.vector.tensor_copy(by_vector[:, j, lo - SCALAR_SLOTS : hi - SCALAR_SLOTS], tokens(0, j, lo, hi))
+            cuts = (0, SCALAR_SLOTS) if j < PACK - 1 else (0, HELP_FIRST, SCALAR_SLOTS)
+            for lo, hi in zip(cuts, cuts[1:]):
+                nc.scalar.activation(by_scalar[:, j, lo:hi], tokens(0, j, lo, hi), COPY)
 
         turned = psum.tile([P, P], F32, name="spare0")
         nc.tensor.transpose(turned[:], gate_rows[:], identity[:])
         nc.vector.tensor_copy(gate_columns[:], turned[:, 0 : S // P])
         gate_banks = [psum.tile([P, GROUP], F32, name="bank%d" % group) for group in range(S // GROUP)]
-        needed = sorted(
-            set(c for index in range(len(SPANS)) for lo, hi, word in vector_pieces(index) for c in range(lo // P, (hi - 1) // P + 1))
-        )
-        for c in needed:
+        for c in range(S // P):
             group, place = divmod(c * P, GROUP)
             nc.tensor.transpose(
                 gate_banks[group][:, place : place + P], gate_columns[:, c : c + 1].to_broadcast([P, P]), identity[:]
             )
 
-        for e in range(EARLY_TRIOS * TRIO):
+        for e in range(SINGLES):
             round_w(e, e + 1)
-        new_raw(6, 9)
-        new_raw(9, 12)
-        load_w(6, 9)
-        load_w(9, 12)
-        load_gate(HELP[6][0])
+        help_multiply(0, 0, HELP_FIRST)
+        round_w(SINGLES, EARLY)
+        load_w(EARLY, E)
+        load_gate(SECOND_END, HELP_THIRD)
+        load_gate(10 * C, HELP_LAST)
         nc.sync.dma_start(bias[:], b)
         nc.sync.dma_start(pos1_sb[:], pos1)
         nc.sync.dma_start(pos2_sb[:], pos2)
-        gather_chunk(0)
+        gather_chunk(placed("first_chunk", 0, PACK * FIRST_CHUNK), 0, *CHUNKS[0])
+        multiply(0, SCALAR_SLOTS, 2 * CALL)
+        multiply(0, HELP_FIRST, SCALAR_SLOTS)
+        multiply(0, 2 * CALL, S)
+        early = range(EARLY)
+        for a, z in ((0, CALL), (CALL, CALL + C), (CALL + C, EARLY_WORDS), (LOW, THIRD), (THIRD, STAGED), (EARLY_WORDS, LOW)):
+            quantize(0, (0, S), early, a, z)
+        later = placed("later_chunks", raw_at - PACK * (S - FIRST_CHUNK), PACK * (S - FIRST_CHUNK))
+        for lo, hi in CHUNKS[1:]:
+            gather_chunk(later, FIRST_CHUNK, lo, hi)
 
-        summed = []
-        done = set()
+        round_w(EARLY, E)
+        multiply(1, 0, SECOND_END)
+        banks = [psum.tile([P, GROUP], F32, name="bank%d" % group) for group in range(SECOND_END // GROUP)]
+        pair = psum.tile([P, GROUP], F32, name="spare0")
+        tenth = psum.tile([P, C], F32, name="spare1")
+        homes = [bank[:, place : place + C] for bank in banks + [pair] for place in (0, C)] + [tenth[:]]
+        for e in early:
+            matmul_pass(0, e * C, (e + 1) * C, homes[e], e % 2 == 0, False)
+        for a, z in ((LOW, THIRD), (0, CALL), (THIRD, THIRD + C), (CALL, 2 * CALL)):
+            quantize(1, (0, SECOND_END), range(EARLY, E), a, z)
+        for e in range(EARLY, E - 1):
+            matmul_pass(0, e * C, (e + 1) * C, homes[e], e % 2 == 0, False)
+        for e in range(SECOND_END // C):
+            matmul_pass(1, e * C, (e + 1) * C, homes[e], False, e % 2 == 1)
+        summed = [(e * C, (e + 1) * C, homes[e]) for e in range(SECOND_END // C)]
 
-        def finish(index):
-            g, pieces = SPANS[index][:2]
-            quantize_span(index)
-            if g == PASSES - 1:
-                done.update(slot for lo, hi, word in pieces for slot in range(lo, hi, H))
-                for group in range(len(summed) * C // GROUP, S // GROUP):
-                    if all(slot in done for slot in range(group * GROUP, (group + 1) * GROUP, H)):
-                        bank = psum.tile([P, GROUP], F32, name="bank%d" % group)
-                        for place in range(0, GROUP, C):
-                            lo = group * GROUP + place
-                            whole = all(x_column[each, lo + H] == x_column[each, lo] + H for each in range(PASSES))
-                            width = C if whole else H
-                            for part in range(0, C, width):
-                                for each in range(PASSES):
-                                    at = place + part
-                                    matmul_pass(each, lo + part, lo + part + width, bank[:, at : at + width])
-                            summed.append((lo, bank[:, place : place + C]))
+        help_multiply(1, SECOND_END, HELP_THIRD)
+        multiply(1, SECOND_END + HELP_THIRD, 9 * C)
+        multiply(1, 9 * C, 10 * C)
+        for place in (0, C):
+            quantize(1, (SECOND_END, 10 * C), (), THIRD + place, THIRD + place + C)
+            matmul_pass(1, SECOND_END + place, SECOND_END + place + C, pair[:, place : place + C], False, place == C)
+        summed.extend((SECOND_END + place, SECOND_END + place + C, pair[:, place : place + C]) for place in (0, C))
 
-        def produce(index):
-            trio = SPANS[index][3]
-            if index in HELP:
-                help_span(index)
-            if trio is not None and trio >= EARLY_TRIOS:
-                round_w(TRIO * trio, TRIO * (trio + 1))
-            multiply_span(index)
-            for chunk in range(1, len(CHUNKS)):
-                if CHUNK_AFTER[chunk] == index:
-                    gather_chunk(chunk)
+        help_multiply(1, 10 * C, HELP_LAST)
+        multiply(1, 10 * C + HELP_LAST, 11 * C)
+        multiply(1, 11 * C, 11 * C + H)
+        y = placed("y", second_planes + 2 * T, S)
+        for lo, hi, sums in summed:
+            activate(lo, hi, sums)
+        halves = [psum.tile([P, H], F32, name="bank4")]
+        matmul_pass(0, 11 * C, 11 * C + H, halves[0][:], True, False)
+        quantize(1, (10 * C, 11 * C), (), THIRD, THIRD + C)
+        matmul_pass(1, 10 * C, 11 * C, tenth[:], False, True)
+        activate(10 * C, 11 * C, tenth[:])
+        multiply(1, 11 * C + H, S)
+        halves.append(psum.tile([P, H], F32, name="bank5"))
+        matmul_pass(0, 11 * C + H, S, halves[1][:], True, False)
+        for index in range(2):
+            lo = 11 * C + index * H
+            quantize(1, (lo, lo + H), (), index * H, (index + 1) * H)
+            matmul_pass(1, lo, lo + H, halves[index][:], False, True)
+            activate(lo, lo + H, halves[index][:])
 
-        ends = len(SPANS) - 3
-        produce(0)
-        for index in range(ends - 1):
-            produce(index + 1)
-            finish(index)
-        finish(ends - 1)
-        produce(ends)
-        produce(ends + 1)
-
-        y = keep.tile([P, S], F32, name="plane10", align_bytes=64)
-        for lo, sums in summed:
-            activate(lo, lo + C, sums)
-
-        for index, bank in zip(range(ends, len(SPANS)), ("spare0", "spare1", "bank%d" % (S // GROUP - 1))):
-            lo, hi = SPANS[index][1][0][:2]
-            sums = psum.tile([P, hi - lo], F32, name=bank)
-            matmul_pass(0, lo, hi, sums[:])
-            quantize_span(index)
-            if index == ends:
-                produce(ends + 2)
-            matmul_pass(PASSES - 1, lo, hi, sums[:])
-            activate(lo, hi, sums[:])
-
-        first = keep.tile([P, T], F32, name="plane00", align_bytes=64)
-        total = keep.tile([P, T], F32, name="plane01", align_bytes=64)
+        first = placed("first", second_planes, T)
+        total = placed("total", second_planes + T, T)
 
         def results(places, lo, hi):
             return y[:].indirect(places[:, lo // PER_COLUMN : hi // PER_COLUMN])
 
-        pieces = spans_of(TOKEN_PIECES)
+        ends = [sum(TOKEN_PIECES[: index + 1]) for index in range(len(TOKEN_PIECES))]
+        pieces = list(zip([0] + ends, ends))
         for index, (lo, hi) in enumerate(pieces):
             if index == OWN_PIECE:
                 nc.vector.tensor_copy(first[:, lo:hi], results(pos1_sb, lo, hi))
             else:
                 nc.scalar.activation(first[:, lo:hi], results(pos1_sb, lo, hi), COPY)
-        second = keep.tile([P, TOKEN_PIECES[-1]], F32, name="plane02", align_bytes=64)
+        second = placed("second", 0, TOKEN_PIECES[-1])
         nc.scalar.activation(second[:], results(pos2_sb, *pieces[-1]), COPY)
         stored = 0
         for index, (lo, hi) in enumerate(pieces):

@@ -54,17 +54,17 @@ def word_of(g, slot):
         return LOW + slot if slot < 2 * CALL else EARLY_WORDS + slot - 2 * CALL
     if slot < SECOND_END:
         return slot
-    if slot < 10 * C:
-        return THIRD + slot - SECOND_END
     if slot < 11 * C:
-        return THIRD + slot - 10 * C
+        return CALL + (slot - SECOND_END) % GROUP
     return slot - 11 * C
 
 
 def weight_word(e):
     if e >= EARLY:
         return LOW + (e - EARLY) * W_WORDS
-    return (e - SINGLES) % EARLY * W_WORDS
+    if e >= SINGLES:
+        return CALL + (e - SINGLES - 1) * W_WORDS
+    return e * W_WORDS if (e + 1) * W_WORDS < CALL else (e + EARLY - SINGLES) * W_WORDS
 
 
 def tile_moe_pre_lin_silu_kernel(tc, xT, w, b, gate, offs, pos1, pos2, out):
@@ -83,7 +83,7 @@ def tile_moe_pre_lin_silu_kernel(tc, xT, w, b, gate, offs, pos1, pos2, out):
         gate_columns = keep.tile([P, S // P], F32, name="gate_columns")
         staging = keep.tile([P, STAGED * PACK], BF16, name="staging", align_bytes=64)
         codes = keep.tile([P, PASSES * S + E * W_WORDS], U32, name="codes", align_bytes=64)
-        scales = keep.tile([P, PASSES * S + E * W_WORDS], U8, name="scales", align_bytes=64)
+        scales = keep.tile([P, 4 * CALL + C], U8, name="scales", align_bytes=64)
 
         wide = T + SPARE
         second_planes = PACK * wide
@@ -168,30 +168,34 @@ def tile_moe_pre_lin_silu_kernel(tc, xT, w, b, gate, offs, pos1, pos2, out):
                             MULT,
                         )
 
-        def quantize(g, slots, experts, a, z):
+        def quantize(g, slots, experts, a, z, row, scale_column):
             column = used[0]
             used[0] = column + z - a
             for slot in range(slots[0], slots[1], H):
-                if a <= word_of(g, slot) < z:
-                    x_column[g, slot] = column + word_of(g, slot) - a
+                shift = word_of(g, slot) - a
+                if 0 <= shift < z - a:
+                    x_column[g, slot] = (column + shift, row, scale_column + shift)
             for e in experts:
-                if a <= weight_word(e) < z:
-                    w_column[e] = column + weight_word(e) - a
+                shift = weight_word(e) - a
+                if 0 <= shift < z - a:
+                    w_column[e] = (column + shift, scale_column + shift)
             nc.vector.quantize_mx(
                 out=codes[:, column : column + z - a].bitcast(FP8X4),
-                scales=scales[:, column : column + z - a],
+                scales=scales[row:, scale_column : scale_column + z - a],
                 in_=staged(a, z - a),
             )
 
         def matmul_pass(g, lo, hi, sums, start, stop):
-            left = w_column[lo // C] + g * N
-            right = x_column[g, lo]
+            left, left_scale = [column + g * N for column in w_column[lo // C]]
+            right, row, right_scale = x_column[g, lo]
+            if (g, lo + H) in x_column and hi - lo == C:
+                assert x_column[g, lo + H] == (right + H, row, right_scale + H)
             nc.tensor.matmul_mx(
                 out=sums,
                 lhsT=codes[:, left : left + N].bitcast(FP8X4),
-                lhsT_scale=scales[:, left : left + N],
+                lhsT_scale=scales[:, left_scale : left_scale + N],
                 rhs=codes[:, right : right + hi - lo].bitcast(FP8X4),
-                rhs_scale=scales[:, right : right + hi - lo],
+                rhs_scale=scales[row:, right_scale : right_scale + hi - lo],
                 start=start,
                 stop=stop,
             )
@@ -266,8 +270,17 @@ def tile_moe_pre_lin_silu_kernel(tc, xT, w, b, gate, offs, pos1, pos2, out):
         multiply(0, HELP_FIRST, SCALAR_SLOTS)
         multiply(0, 2 * CALL, S)
         early = range(EARLY)
-        for a, z in ((0, CALL), (CALL, CALL + C), (CALL + C, EARLY_WORDS), (LOW, THIRD), (THIRD, STAGED), (EARLY_WORDS, LOW)):
-            quantize(0, (0, S), early, a, z)
+        for a, count, row, scale_column in (
+            (0, CALL, 0, 0),
+            (CALL, CALL, 0, CALL),
+            (LOW, GROUP, 4, 0),
+            (LOW + GROUP, GROUP, 4, CALL),
+            (THIRD + GROUP, GROUP, 4, GROUP),
+            (2 * CALL + GROUP, C, 4, CALL + GROUP),
+            (THIRD, GROUP, 8, 0),
+            (2 * CALL, GROUP, 8, CALL),
+        ):
+            quantize(0, (0, S), early, a, a + count, row, scale_column)
         later = placed("later_chunks", raw_at - PACK * (S - FIRST_CHUNK), PACK * (S - FIRST_CHUNK))
         for lo, hi in CHUNKS[1:]:
             gather_chunk(later, FIRST_CHUNK, lo, hi)
@@ -280,8 +293,11 @@ def tile_moe_pre_lin_silu_kernel(tc, xT, w, b, gate, offs, pos1, pos2, out):
         homes = [bank[:, place : place + C] for bank in banks + [pair] for place in (0, C)] + [tenth[:]]
         for e in early:
             matmul_pass(0, e * C, (e + 1) * C, homes[e], e % 2 == 0, False)
-        for a, z in ((LOW, THIRD), (0, CALL), (THIRD, THIRD + C), (CALL, 2 * CALL)):
-            quantize(1, (0, SECOND_END), range(EARLY, E), a, z)
+        quantize(1, (0, 0), range(EARLY, E), LOW, THIRD, 0, 2 * CALL)
+        quantize(1, (0, 0), range(EARLY, E), THIRD, THIRD + C, 0, 3 * CALL)
+        for index in range(SECOND_END // GROUP):
+            a = index * GROUP
+            quantize(1, (0, SECOND_END), (), a, a + GROUP, 4 + 4 * (index // 2), 2 * CALL + a % CALL)
         for e in range(EARLY, E - 1):
             matmul_pass(0, e * C, (e + 1) * C, homes[e], e % 2 == 0, False)
         for e in range(SECOND_END // C):
@@ -292,7 +308,7 @@ def tile_moe_pre_lin_silu_kernel(tc, xT, w, b, gate, offs, pos1, pos2, out):
         multiply(1, SECOND_END + HELP_THIRD, 9 * C)
         multiply(1, 9 * C, 10 * C)
         for place in (0, C):
-            quantize(1, (SECOND_END, 10 * C), (), THIRD + place, THIRD + place + C)
+            quantize(1, (SECOND_END, 10 * C), (), CALL + place, CALL + place + C, 0, 3 * CALL + C + place)
             matmul_pass(1, SECOND_END + place, SECOND_END + place + C, pair[:, place : place + C], False, place == C)
         summed.extend((SECOND_END + place, SECOND_END + place + C, pair[:, place : place + C]) for place in (0, C))
 
@@ -304,7 +320,7 @@ def tile_moe_pre_lin_silu_kernel(tc, xT, w, b, gate, offs, pos1, pos2, out):
             activate(lo, hi, sums)
         halves = [psum.tile([P, H], F32, name="bank4")]
         matmul_pass(0, 11 * C, 11 * C + H, halves[0][:], True, False)
-        quantize(1, (10 * C, 11 * C), (), THIRD, THIRD + C)
+        quantize(1, (10 * C, 11 * C), (), CALL, CALL + C, 0, 3 * CALL + 3 * C)
         matmul_pass(1, 10 * C, 11 * C, tenth[:], False, True)
         activate(10 * C, 11 * C, tenth[:])
         multiply(1, 11 * C + H, S)
@@ -312,7 +328,7 @@ def tile_moe_pre_lin_silu_kernel(tc, xT, w, b, gate, offs, pos1, pos2, out):
         matmul_pass(0, 11 * C + H, S, halves[1][:], True, False)
         for index in range(2):
             lo = 11 * C + index * H
-            quantize(1, (lo, lo + H), (), index * H, (index + 1) * H)
+            quantize(1, (lo, lo + H), (), index * H, (index + 1) * H, 0, 4 * CALL + index * H)
             matmul_pass(1, lo, lo + H, halves[index][:], False, True)
             activate(lo, lo + H, halves[index][:])
 

@@ -24,6 +24,7 @@ PACK = 4
 PASSES = K // (P * PACK)
 PER_COLUMN = 16
 RUN = 2
+LINE = 4
 W_WORDS = PASSES * N
 W_RAW = PACK * W_WORDS
 GROUP = 512
@@ -147,9 +148,12 @@ def tile_moe_pre_lin_silu_kernel(tc, xT, w, b, gate, offs, pos1, pos2, out):
         def help_multiply(g, lo, count):
             first, end, source = [chunk for chunk in chunks[g] if chunk[0] <= lo < chunk[1]][0]
             nc.gpsimd.tensor_tensor(
-                staged(word_of(g, lo), count).rearrange("p (s j) -> p s j", j=PACK),
-                source[:, :, lo - first : lo - first + count].rearrange("p j s -> p s j"),
-                helped_gate[lo][:].unsqueeze(2).to_broadcast([P, count, PACK]),
+                staged(word_of(g, lo), count).rearrange("p (c i j) -> p c j i", i=LINE, j=PACK),
+                source[:, :, lo - first : lo - first + count].rearrange("p j (c i) -> p c j i", i=LINE),
+                helped_gate[lo][:]
+                .rearrange("p (c i) -> p c i", i=LINE)
+                .unsqueeze(2)
+                .to_broadcast([P, count // LINE, PACK, LINE]),
                 MULT,
             )
 

@@ -33,14 +33,15 @@ H = C // 2
 
 EARLY = 7
 SINGLES = 5
-SCALAR_SLOTS = 1536
+SCALAR_SLOTS = 1472
 SPARE = max(SCALAR_SLOTS, S - SCALAR_SLOTS) + 2 * PER_COLUMN - T
-HELP_FIRST = 832
+HELP_FIRST = 896
+HELP_SECOND = 160
 HELP_THIRD = 128
 HELP_LAST = 96
-FIRST_CHUNK = 1152
+FIRST_CHUNK = 1216
 SECOND_END = 8 * C
-CHUNKS = ((0, FIRST_CHUNK), (FIRST_CHUNK, SECOND_END), (SECOND_END, 10 * C + H), (10 * C + H, S))
+CHUNKS = ((0, FIRST_CHUNK), (FIRST_CHUNK, 6 * C + H), (6 * C + H, SECOND_END), (SECOND_END, 10 * C + H), (10 * C + H, S))
 TOKEN_PIECES = (192, 256, 384, 320, 192, 192)
 OWN_PIECE = 1
 
@@ -53,10 +54,12 @@ THIRD = LOW + CALL
 def word_of(g, slot):
     if g == 0:
         return LOW + slot if slot < 2 * CALL else EARLY_WORDS + slot - 2 * CALL
+    if slot < C:
+        return THIRD + C + slot
     if slot < SECOND_END:
-        return slot
+        return slot - C
     if slot < 11 * C:
-        return CALL + (slot - SECOND_END) % GROUP
+        return 3 * C + (slot - SECOND_END) % GROUP
     return slot - 11 * C
 
 
@@ -84,7 +87,7 @@ def tile_moe_pre_lin_silu_kernel(tc, xT, w, b, gate, offs, pos1, pos2, out):
         gate_columns = keep.tile([P, S // P], F32, name="gate_columns")
         staging = keep.tile([P, STAGED * PACK], BF16, name="staging", align_bytes=64)
         codes = keep.tile([P, PASSES * S + E * W_WORDS], U32, name="codes", align_bytes=64)
-        scales = keep.tile([P, 4 * CALL + C], U8, name="scales", align_bytes=64)
+        scales = keep.tile([P, 4 * CALL + GROUP], U8, name="scales", align_bytes=64)
 
         wide = T + SPARE
         second_planes = PACK * wide
@@ -100,6 +103,7 @@ def tile_moe_pre_lin_silu_kernel(tc, xT, w, b, gate, offs, pos1, pos2, out):
         ]
         x_view = xT.rearrange("(g p j) t -> g j p t", g=PASSES, j=PACK)
         w_view = w.rearrange("e (g p j) n -> p (e g) (j n)", g=PASSES, j=PACK)
+        w_rows = w.rearrange("e (g p j) n -> j p (e g) n", g=PASSES, j=PACK)
         chunks = [[], []]
         helped_gate = {}
         raw = {}
@@ -117,6 +121,22 @@ def tile_moe_pre_lin_silu_kernel(tc, xT, w, b, gate, offs, pos1, pos2, out):
             raw[first] = placed("raw%d" % first, raw_at + place * W_RAW, (end - first) * W_RAW)
             nc.sync.dma_start(
                 raw[first][:].rearrange("p (h c) -> p h c", c=PACK * N), w_view[:, PASSES * first : PASSES * end, :]
+            )
+
+        def load_w_by_rows(first, end):
+            raw[first] = placed("raw%d" % first, raw_at + first % EARLY * W_RAW, (end - first) * W_RAW)
+            rows = raw[first][:].rearrange("p (j h n) -> p j h n", j=PACK, n=N)
+            for j in range(PACK):
+                nc.sync.dma_start(rows[:, j], w_rows[j, :, PASSES * first : PASSES * end, :])
+
+        def round_w_by_lines(first, end):
+            nc.gpsimd.tensor_scalar(
+                staged(weight_word(first), (end - first) * W_WORDS).rearrange("p (c i j) -> p c j i", i=LINE, j=PACK),
+                raw[first][:].rearrange("p (j c i) -> p c j i", i=LINE, j=PACK),
+                1.0,
+                0.0,
+                MULT,
+                ADD,
             )
 
         def load_gate(first, count):
@@ -150,7 +170,7 @@ def tile_moe_pre_lin_silu_kernel(tc, xT, w, b, gate, offs, pos1, pos2, out):
             nc.gpsimd.tensor_tensor(
                 staged(word_of(g, lo), count).rearrange("p (c i j) -> p c j i", i=LINE, j=PACK),
                 source[:, :, lo - first : lo - first + count].rearrange("p j (c i) -> p c j i", i=LINE),
-                helped_gate[lo][:]
+                helped_gate[lo][:, :count]
                 .rearrange("p (c i) -> p c i", i=LINE)
                 .unsqueeze(2)
                 .to_broadcast([P, count // LINE, PACK, LINE]),
@@ -231,7 +251,7 @@ def tile_moe_pre_lin_silu_kernel(tc, xT, w, b, gate, offs, pos1, pos2, out):
         load_gate(0, HELP_FIRST)
         for j in range(PACK):
             load_plane(1, j)
-        load_w(SINGLES, EARLY)
+        load_w_by_rows(SINGLES, EARLY)
 
         by_scalar = planes_of(placed("by_scalar", gathered_at, PACK * SCALAR_SLOTS), 0, 0, SCALAR_SLOTS)
         by_vector = planes_of(
@@ -262,8 +282,8 @@ def tile_moe_pre_lin_silu_kernel(tc, xT, w, b, gate, offs, pos1, pos2, out):
         for e in range(SINGLES):
             round_w(e, e + 1)
         help_multiply(0, 0, HELP_FIRST)
-        round_w(SINGLES, EARLY)
-        load_w(EARLY, E)
+        round_w_by_lines(SINGLES, EARLY)
+        load_w_by_rows(EARLY, E)
         load_gate(SECOND_END, HELP_THIRD)
         load_gate(10 * C, HELP_LAST)
         nc.sync.dma_start(bias[:], b)
@@ -289,8 +309,10 @@ def tile_moe_pre_lin_silu_kernel(tc, xT, w, b, gate, offs, pos1, pos2, out):
         for lo, hi in CHUNKS[1:]:
             gather_chunk(later, FIRST_CHUNK, lo, hi)
 
-        round_w(EARLY, E)
-        multiply(1, 0, SECOND_END)
+        help_multiply(1, 0, HELP_SECOND)
+        round_w_by_lines(EARLY, E)
+        multiply(1, HELP_SECOND, C)
+        multiply(1, C, SECOND_END)
         banks = [psum.tile([P, GROUP], F32, name="bank%d" % group) for group in range(SECOND_END // GROUP)]
         pair = psum.tile([P, GROUP], F32, name="spare0")
         tenth = psum.tile([P, C], F32, name="spare1")
@@ -298,10 +320,14 @@ def tile_moe_pre_lin_silu_kernel(tc, xT, w, b, gate, offs, pos1, pos2, out):
         for e in early:
             matmul_pass(0, e * C, (e + 1) * C, homes[e], e % 2 == 0, False)
         quantize(1, (0, 0), range(EARLY, E), LOW, THIRD, 0, 2 * CALL)
-        quantize(1, (0, 0), range(EARLY, E), THIRD, THIRD + C, 0, 3 * CALL)
-        for index in range(SECOND_END // GROUP):
-            a = index * GROUP
-            quantize(1, (0, SECOND_END), (), a, a + GROUP, 4 + 4 * (index // 2), 2 * CALL + a % CALL)
+        quantize(1, (0, C), range(EARLY, E), THIRD, THIRD + GROUP, 0, 3 * CALL)
+        for a, count, row, scale_column in (
+            (0, C, 4, 2 * CALL),
+            (C, GROUP, 4, 3 * CALL),
+            (3 * C, GROUP, 8, 2 * CALL),
+            (5 * C, GROUP, 8, 3 * CALL),
+        ):
+            quantize(1, (C, SECOND_END), (), a, a + count, row, scale_column)
         for e in range(EARLY, E - 1):
             matmul_pass(0, e * C, (e + 1) * C, homes[e], e % 2 == 0, False)
         for e in range(SECOND_END // C):
@@ -312,7 +338,7 @@ def tile_moe_pre_lin_silu_kernel(tc, xT, w, b, gate, offs, pos1, pos2, out):
         multiply(1, SECOND_END + HELP_THIRD, 9 * C)
         multiply(1, 9 * C, 10 * C)
         for place in (0, C):
-            quantize(1, (SECOND_END, 10 * C), (), CALL + place, CALL + place + C, 0, 3 * CALL + C + place)
+            quantize(1, (SECOND_END, 10 * C), (), 3 * C + place, 4 * C + place, 0, 3 * CALL + GROUP + place)
             matmul_pass(1, SECOND_END + place, SECOND_END + place + C, pair[:, place : place + C], False, place == C)
         summed.extend((SECOND_END + place, SECOND_END + place + C, pair[:, place : place + C]) for place in (0, C))
 
@@ -324,7 +350,7 @@ def tile_moe_pre_lin_silu_kernel(tc, xT, w, b, gate, offs, pos1, pos2, out):
             activate(lo, hi, sums)
         halves = [psum.tile([P, H], F32, name="bank4")]
         matmul_pass(0, 11 * C, 11 * C + H, halves[0][:], True, False)
-        quantize(1, (10 * C, 11 * C), (), CALL, CALL + C, 0, 3 * CALL + 3 * C)
+        quantize(1, (10 * C, 11 * C), (), 3 * C, 4 * C, 0, 4 * CALL)
         matmul_pass(1, 10 * C, 11 * C, tenth[:], False, True)
         activate(10 * C, 11 * C, tenth[:])
         multiply(1, 11 * C + H, S)
@@ -332,7 +358,7 @@ def tile_moe_pre_lin_silu_kernel(tc, xT, w, b, gate, offs, pos1, pos2, out):
         matmul_pass(0, 11 * C + H, S, halves[1][:], True, False)
         for index in range(2):
             lo = 11 * C + index * H
-            quantize(1, (lo, lo + H), (), index * H, (index + 1) * H, 0, 4 * CALL + index * H)
+            quantize(1, (lo, lo + H), (), index * H, (index + 1) * H, 0, 4 * CALL + C + index * H)
             matmul_pass(1, lo, lo + H, halves[index][:], False, True)
             activate(lo, lo + H, halves[index][:])
 

@@ -103,7 +103,6 @@ def tile_moe_pre_lin_silu_kernel(tc, xT, w, b, gate, offs, pos1, pos2, out):
         ]
         x_view = xT.rearrange("(g p j) t -> g j p t", g=PASSES, j=PACK)
         w_view = w.rearrange("e (g p j) n -> p (e g) (j n)", g=PASSES, j=PACK)
-        w_rows = w.rearrange("e (g p j) n -> j p (e g) n", g=PASSES, j=PACK)
         chunks = [[], []]
         helped_gate = {}
         raw = {}
@@ -123,22 +122,6 @@ def tile_moe_pre_lin_silu_kernel(tc, xT, w, b, gate, offs, pos1, pos2, out):
                 raw[first][:].rearrange("p (h c) -> p h c", c=PACK * N), w_view[:, PASSES * first : PASSES * end, :]
             )
 
-        def load_w_by_rows(first, end):
-            raw[first] = placed("raw%d" % first, raw_at + first % EARLY * W_RAW, (end - first) * W_RAW)
-            rows = raw[first][:].rearrange("p (j h n) -> p j h n", j=PACK, n=N)
-            for j in range(PACK):
-                nc.sync.dma_start(rows[:, j], w_rows[j, :, PASSES * first : PASSES * end, :])
-
-        def round_w_by_lines(first, end):
-            nc.gpsimd.tensor_scalar(
-                staged(weight_word(first), (end - first) * W_WORDS).rearrange("p (c i j) -> p c j i", i=LINE, j=PACK),
-                raw[first][:].rearrange("p (j c i) -> p c j i", i=LINE, j=PACK),
-                1.0,
-                0.0,
-                MULT,
-                ADD,
-            )
-
         def load_gate(first, count):
             helped_gate[first] = keep.tile([P, count], F32, name="gate%d" % first)
             nc.sync.dma_start(helped_gate[first][:], gate[0:P, first : first + count])
@@ -156,13 +139,11 @@ def tile_moe_pre_lin_silu_kernel(tc, xT, w, b, gate, offs, pos1, pos2, out):
                 nc.scalar.activation(view[:, j, :], tokens(1, j, lo, hi), COPY)
 
         def round_w(first, end):
-            nc.gpsimd.tensor_scalar(
-                staged(weight_word(first), (end - first) * W_WORDS).rearrange("p (h n j) -> p h n j", n=N, j=PACK),
-                raw[first][:].rearrange("p (h j n) -> p h n j", n=N, j=PACK),
-                1.0,
-                0.0,
-                MULT,
-                ADD,
+            nc.gpsimd.tensor_copy(
+                staged(weight_word(first), (end - first) * W_WORDS).rearrange(
+                    "p (h c i j) -> p h c j i", c=N // LINE, i=LINE, j=PACK
+                ),
+                raw[first][:].rearrange("p (h j c i) -> p h c j i", c=N // LINE, i=LINE, j=PACK),
             )
 
         def help_multiply(g, lo, count):
@@ -251,7 +232,7 @@ def tile_moe_pre_lin_silu_kernel(tc, xT, w, b, gate, offs, pos1, pos2, out):
         load_gate(0, HELP_FIRST)
         for j in range(PACK):
             load_plane(1, j)
-        load_w_by_rows(SINGLES, EARLY)
+        load_w(SINGLES, EARLY)
 
         by_scalar = planes_of(placed("by_scalar", gathered_at, PACK * SCALAR_SLOTS), 0, 0, SCALAR_SLOTS)
         by_vector = planes_of(
@@ -282,8 +263,8 @@ def tile_moe_pre_lin_silu_kernel(tc, xT, w, b, gate, offs, pos1, pos2, out):
         for e in range(SINGLES):
             round_w(e, e + 1)
         help_multiply(0, 0, HELP_FIRST)
-        round_w_by_lines(SINGLES, EARLY)
-        load_w_by_rows(EARLY, E)
+        round_w(SINGLES, EARLY)
+        load_w(EARLY, E)
         load_gate(SECOND_END, HELP_THIRD)
         load_gate(10 * C, HELP_LAST)
         nc.sync.dma_start(bias[:], b)
@@ -310,7 +291,7 @@ def tile_moe_pre_lin_silu_kernel(tc, xT, w, b, gate, offs, pos1, pos2, out):
             gather_chunk(later, FIRST_CHUNK, lo, hi)
 
         help_multiply(1, 0, HELP_SECOND)
-        round_w_by_lines(EARLY, E)
+        round_w(EARLY, E)
         multiply(1, HELP_SECOND, C)
         multiply(1, C, SECOND_END)
         banks = [psum.tile([P, GROUP], F32, name="bank%d" % group) for group in range(SECOND_END // GROUP)]

@@ -38,7 +38,7 @@ SPARE = max(SCALAR_SLOTS, S - SCALAR_SLOTS) + 2 * PER_COLUMN - T
 HELP_FIRST = 896
 HELP_SECOND = 160
 HELP_THIRD = 128
-HELP_LAST = 96
+THIRD_FROM = 9 * C - HELP_THIRD // 2
 FIRST_CHUNK = 1216
 SECOND_END = 8 * C
 CHUNKS = ((0, FIRST_CHUNK), (FIRST_CHUNK, 6 * C + H), (6 * C + H, SECOND_END), (SECOND_END, 10 * C + H), (10 * C + H, S))
@@ -58,9 +58,11 @@ def word_of(g, slot):
         return THIRD + C + slot
     if slot < SECOND_END:
         return slot - C
-    if slot < 11 * C:
-        return 3 * C + (slot - SECOND_END) % GROUP
-    return slot - 11 * C
+    if slot < 10 * C:
+        return 3 * C + slot - SECOND_END
+    if slot < S - H:
+        return 3 * C + H + slot - 10 * C
+    return 3 * C + slot - (S - H)
 
 
 def weight_word(e):
@@ -116,7 +118,7 @@ def tile_moe_pre_lin_silu_kernel(tc, xT, w, b, gate, offs, pos1, pos2, out):
             nc.sync.dma_start(planes[g][j][:, :T], x_view[g, j])
 
         def load_w(first, end):
-            place = first % EARLY
+            place = (first - SINGLES) % EARLY if first < EARLY else EARLY - SINGLES
             raw[first] = placed("raw%d" % first, raw_at + place * W_RAW, (end - first) * W_RAW)
             nc.sync.dma_start(
                 raw[first][:].rearrange("p (h c) -> p h c", c=PACK * N), w_view[:, PASSES * first : PASSES * end, :]
@@ -230,9 +232,10 @@ def tile_moe_pre_lin_silu_kernel(tc, xT, w, b, gate, offs, pos1, pos2, out):
         load_plane(0, 3)
         load_w(4, 5)
         load_gate(0, HELP_FIRST)
-        for j in range(PACK):
+        for j in range(PACK - 1):
             load_plane(1, j)
         load_w(SINGLES, EARLY)
+        load_plane(1, PACK - 1)
 
         by_scalar = planes_of(placed("by_scalar", gathered_at, PACK * SCALAR_SLOTS), 0, 0, SCALAR_SLOTS)
         by_vector = planes_of(
@@ -265,8 +268,8 @@ def tile_moe_pre_lin_silu_kernel(tc, xT, w, b, gate, offs, pos1, pos2, out):
         help_multiply(0, 0, HELP_FIRST)
         round_w(SINGLES, EARLY)
         load_w(EARLY, E)
-        load_gate(SECOND_END, HELP_THIRD)
-        load_gate(10 * C, HELP_LAST)
+        load_gate(THIRD_FROM, HELP_THIRD)
+        load_gate(S - H, H)
         nc.sync.dma_start(bias[:], b)
         nc.sync.dma_start(pos1_sb[:], pos1)
         nc.sync.dma_start(pos2_sb[:], pos2)
@@ -286,7 +289,9 @@ def tile_moe_pre_lin_silu_kernel(tc, xT, w, b, gate, offs, pos1, pos2, out):
             (2 * CALL, GROUP, 8, CALL),
         ):
             quantize(0, (0, S), early, a, a + count, row, scale_column)
-        later = placed("later_chunks", raw_at - PACK * (S - FIRST_CHUNK), PACK * (S - FIRST_CHUNK))
+        later = placed(
+            "later_chunks", raw_at + (EARLY - SINGLES) * W_RAW - PACK * (S - FIRST_CHUNK), PACK * (S - FIRST_CHUNK)
+        )
         for lo, hi in CHUNKS[1:]:
             gather_chunk(later, FIRST_CHUNK, lo, hi)
 
@@ -315,33 +320,28 @@ def tile_moe_pre_lin_silu_kernel(tc, xT, w, b, gate, offs, pos1, pos2, out):
             matmul_pass(1, e * C, (e + 1) * C, homes[e], False, e % 2 == 1)
         summed = [(e * C, (e + 1) * C, homes[e]) for e in range(SECOND_END // C)]
 
-        help_multiply(1, SECOND_END, HELP_THIRD)
-        multiply(1, SECOND_END + HELP_THIRD, 9 * C)
-        multiply(1, 9 * C, 10 * C)
+        help_multiply(1, THIRD_FROM, HELP_THIRD)
+        multiply(1, SECOND_END, THIRD_FROM)
+        multiply(1, THIRD_FROM + HELP_THIRD, 10 * C)
         for place in (0, C):
             quantize(1, (SECOND_END, 10 * C), (), 3 * C + place, 4 * C + place, 0, 3 * CALL + GROUP + place)
             matmul_pass(1, SECOND_END + place, SECOND_END + place + C, pair[:, place : place + C], False, place == C)
         summed.extend((SECOND_END + place, SECOND_END + place + C, pair[:, place : place + C]) for place in (0, C))
 
-        help_multiply(1, 10 * C, HELP_LAST)
-        multiply(1, 10 * C + HELP_LAST, 11 * C)
-        multiply(1, 11 * C, 11 * C + H)
+        help_multiply(1, S - H, H)
+        multiply(1, 10 * C, 11 * C)
+        multiply(1, 11 * C, S - H)
         y = placed("y", second_planes + 2 * T, S)
         for lo, hi, sums in summed:
             activate(lo, hi, sums)
-        halves = [psum.tile([P, H], F32, name="bank4")]
-        matmul_pass(0, 11 * C, 11 * C + H, halves[0][:], True, False)
-        quantize(1, (10 * C, 11 * C), (), 3 * C, 4 * C, 0, 4 * CALL)
-        matmul_pass(1, 10 * C, 11 * C, tenth[:], False, True)
-        activate(10 * C, 11 * C, tenth[:])
-        multiply(1, 11 * C + H, S)
-        halves.append(psum.tile([P, H], F32, name="bank5"))
-        matmul_pass(0, 11 * C + H, S, halves[1][:], True, False)
+        halves = [psum.tile([P, H], F32, name="bank%d" % group) for group in (4, 5)]
         for index in range(2):
-            lo = 11 * C + index * H
-            quantize(1, (lo, lo + H), (), index * H, (index + 1) * H, 0, 4 * CALL + C + index * H)
-            matmul_pass(1, lo, lo + H, halves[index][:], False, True)
-            activate(lo, lo + H, halves[index][:])
+            matmul_pass(0, 11 * C + index * H, 11 * C + (index + 1) * H, halves[index][:], True, False)
+        for lo, hi, sums in ((10 * C, 11 * C, tenth), (11 * C, S - H, halves[0]), (S - H, S, halves[1])):
+            a = word_of(1, lo)
+            quantize(1, (lo, hi), (), a, a + hi - lo, 0, 4 * CALL + lo - 10 * C)
+            matmul_pass(1, lo, hi, sums[:], False, True)
+            activate(lo, hi, sums[:])
 
         first = placed("first", second_planes, T)
         total = placed("total", second_planes + T, T)

@@ -41,28 +41,35 @@ HELP_THIRD = 128
 THIRD_FROM = 9 * C - HELP_THIRD // 2
 FIRST_CHUNK = 1216
 SECOND_END = 8 * C
-CHUNKS = ((0, FIRST_CHUNK), (FIRST_CHUNK, 6 * C + H), (6 * C + H, SECOND_END), (SECOND_END, 10 * C + H), (10 * C + H, S))
+CHUNKS = (
+    (0, FIRST_CHUNK),
+    (FIRST_CHUNK, 6 * C + H),
+    (6 * C + H, SECOND_END),
+    (SECOND_END, 10 * C + H),
+    (10 * C + H, S),
+)
 TOKEN_PIECES = (192, 256, 384, 320, 192, 192)
 OWN_PIECE = 1
 
 EARLY_WORDS = EARLY * W_WORDS
 STAGED = EARLY_WORDS + S
 LOW = EARLY_WORDS + CALL
-THIRD = LOW + CALL
+MIDDLE = LOW + CALL
+END_WORD = 3 * C
 
 
 def word_of(g, slot):
     if g == 0:
         return LOW + slot if slot < 2 * CALL else EARLY_WORDS + slot - 2 * CALL
     if slot < C:
-        return THIRD + C + slot
+        return MIDDLE + C + slot
     if slot < SECOND_END:
         return slot - C
     if slot < 10 * C:
-        return 3 * C + slot - SECOND_END
+        return END_WORD + slot - SECOND_END
     if slot < S - H:
-        return 3 * C + H + slot - 10 * C
-    return 3 * C + slot - (S - H)
+        return END_WORD + H + slot - 10 * C
+    return END_WORD + slot - (S - H)
 
 
 def weight_word(e):
@@ -96,8 +103,8 @@ def tile_moe_pre_lin_silu_kernel(tc, xT, w, b, gate, offs, pos1, pos2, out):
         gathered_at = second_planes + PACK * T
         raw_at = gathered_at + PACK * S
 
-        def placed(name, first, width):
-            return shared.tile([P, width], F32, name=name, offset=4 * first)
+        def placed(name, column, width):
+            return shared.tile([P, width], F32, name=name, offset=4 * column)
 
         planes = [
             [placed("plane0%d" % j, j * wide, wide) for j in range(PACK)],
@@ -109,7 +116,7 @@ def tile_moe_pre_lin_silu_kernel(tc, xT, w, b, gate, offs, pos1, pos2, out):
         helped_gate = {}
         raw = {}
         x_column, w_column = {}, {}
-        used = [0]
+        next_column = [0]
 
         def staged(word, count):
             return staging[:, word * PACK : (word + count) * PACK]
@@ -117,42 +124,42 @@ def tile_moe_pre_lin_silu_kernel(tc, xT, w, b, gate, offs, pos1, pos2, out):
         def load_plane(g, j):
             nc.sync.dma_start(planes[g][j][:, :T], x_view[g, j])
 
-        def load_w(first, end):
-            place = (first - SINGLES) % EARLY if first < EARLY else EARLY - SINGLES
-            raw[first] = placed("raw%d" % first, raw_at + place * W_RAW, (end - first) * W_RAW)
+        def load_w(e, end):
+            place = (e - SINGLES) % EARLY if e < EARLY else EARLY - SINGLES
+            raw[e] = placed("raw%d" % e, raw_at + place * W_RAW, (end - e) * W_RAW)
             nc.sync.dma_start(
-                raw[first][:].rearrange("p (h c) -> p h c", c=PACK * N), w_view[:, PASSES * first : PASSES * end, :]
+                raw[e][:].rearrange("p (h c) -> p h c", c=PACK * N), w_view[:, PASSES * e : PASSES * end, :]
             )
 
-        def load_gate(first, count):
-            helped_gate[first] = keep.tile([P, count], F32, name="gate%d" % first)
-            nc.sync.dma_start(helped_gate[first][:], gate[0:P, first : first + count])
+        def load_gate(lo, count):
+            helped_gate[lo] = keep.tile([P, count], F32, name="gate%d" % lo)
+            nc.sync.dma_start(helped_gate[lo][:], gate[0:P, lo : lo + count])
 
-        def planes_of(tile, first, lo, hi):
-            return tile[:, PACK * (lo - first) : PACK * (hi - first)].rearrange("p (j s) -> p j s", j=PACK)
+        def by_plane(tile, base, lo, hi):
+            return tile[:, PACK * (lo - base) : PACK * (hi - base)].rearrange("p (j s) -> p j s", j=PACK)
 
         def tokens(g, j, lo, hi):
             return planes[g][j][:].indirect(offs_sb[:, lo // PER_COLUMN : hi // PER_COLUMN])
 
-        def gather_chunk(tile, first, lo, hi):
-            view = planes_of(tile, first, lo, hi)
+        def gather_chunk(tile, base, lo, hi):
+            view = by_plane(tile, base, lo, hi)
             chunks[1].append((lo, hi, view))
             for j in range(PACK):
                 nc.scalar.activation(view[:, j, :], tokens(1, j, lo, hi), COPY)
 
-        def round_w(first, end):
+        def round_w(e, end):
             nc.gpsimd.tensor_copy(
-                staged(weight_word(first), (end - first) * W_WORDS).rearrange(
+                staged(weight_word(e), (end - e) * W_WORDS).rearrange(
                     "p (h c i j) -> p h c j i", c=N // LINE, i=LINE, j=PACK
                 ),
-                raw[first][:].rearrange("p (h j c i) -> p h c j i", c=N // LINE, i=LINE, j=PACK),
+                raw[e][:].rearrange("p (h j c i) -> p h c j i", c=N // LINE, i=LINE, j=PACK),
             )
 
         def help_multiply(g, lo, count):
-            first, end, source = [chunk for chunk in chunks[g] if chunk[0] <= lo < chunk[1]][0]
+            base, end, source = [chunk for chunk in chunks[g] if chunk[0] <= lo < chunk[1]][0]
             nc.gpsimd.tensor_tensor(
                 staged(word_of(g, lo), count).rearrange("p (c i j) -> p c j i", i=LINE, j=PACK),
-                source[:, :, lo - first : lo - first + count].rearrange("p j (c i) -> p c j i", i=LINE),
+                source[:, :, lo - base : lo - base + count].rearrange("p j (c i) -> p c j i", i=LINE),
                 helped_gate[lo][:, :count]
                 .rearrange("p (c i) -> p c i", i=LINE)
                 .unsqueeze(2)
@@ -162,12 +169,12 @@ def tile_moe_pre_lin_silu_kernel(tc, xT, w, b, gate, offs, pos1, pos2, out):
 
         def multiply(g, lo, hi):
             for group in range(lo // GROUP, (hi - 1) // GROUP + 1):
-                for first, end, tile in chunks[g]:
-                    a, z = max(lo, first, group * GROUP), min(hi, end, (group + 1) * GROUP)
+                for base, end, source in chunks[g]:
+                    a, z = max(lo, base, group * GROUP), min(hi, end, (group + 1) * GROUP)
                     if a < z:
                         nc.vector.tensor_tensor(
                             staged(word_of(g, a), z - a).rearrange("p (c i j) -> p c j i", i=RUN, j=PACK),
-                            tile[:, :, a - first : z - first].rearrange("p j (c i) -> p c j i", i=RUN),
+                            source[:, :, a - base : z - base].rearrange("p j (c i) -> p c j i", i=RUN),
                             gate_banks[group][:, a - group * GROUP : z - group * GROUP]
                             .rearrange("p (c i) -> p c i", i=RUN)
                             .unsqueeze(2)
@@ -175,28 +182,26 @@ def tile_moe_pre_lin_silu_kernel(tc, xT, w, b, gate, offs, pos1, pos2, out):
                             MULT,
                         )
 
-        def quantize(g, slots, experts, a, z, row, scale_column):
-            column = used[0]
-            used[0] = column + z - a
+        def quantize(g, slots, experts, word, count, row, scale_column):
+            column = next_column[0]
+            next_column[0] = column + count
             for slot in range(slots[0], slots[1], H):
-                shift = word_of(g, slot) - a
-                if 0 <= shift < z - a:
+                shift = word_of(g, slot) - word
+                if 0 <= shift < count:
                     x_column[g, slot] = (column + shift, row, scale_column + shift)
             for e in experts:
-                shift = weight_word(e) - a
-                if 0 <= shift < z - a:
+                shift = weight_word(e) - word
+                if 0 <= shift < count:
                     w_column[e] = (column + shift, scale_column + shift)
             nc.vector.quantize_mx(
-                out=codes[:, column : column + z - a].bitcast(FP8X4),
-                scales=scales[row:, scale_column : scale_column + z - a],
-                in_=staged(a, z - a),
+                out=codes[:, column : column + count].bitcast(FP8X4),
+                scales=scales[row:, scale_column : scale_column + count],
+                in_=staged(word, count),
             )
 
         def matmul_pass(g, lo, hi, sums, start, stop):
             left, left_scale = [column + g * N for column in w_column[lo // C]]
             right, row, right_scale = x_column[g, lo]
-            if (g, lo + H) in x_column and hi - lo == C:
-                assert x_column[g, lo + H] == (right + H, row, right_scale + H)
             nc.tensor.matmul_mx(
                 out=sums,
                 lhsT=codes[:, left : left + N].bitcast(FP8X4),
@@ -237,12 +242,10 @@ def tile_moe_pre_lin_silu_kernel(tc, xT, w, b, gate, offs, pos1, pos2, out):
         load_w(SINGLES, EARLY)
         load_plane(1, PACK - 1)
 
-        by_scalar = planes_of(placed("by_scalar", gathered_at, PACK * SCALAR_SLOTS), 0, 0, SCALAR_SLOTS)
-        by_vector = planes_of(
-            placed("by_vector", gathered_at + PACK * SCALAR_SLOTS, PACK * (S - SCALAR_SLOTS)),
-            SCALAR_SLOTS,
-            SCALAR_SLOTS,
-            S,
+        vector_slots = S - SCALAR_SLOTS
+        by_scalar = by_plane(placed("by_scalar", gathered_at, PACK * SCALAR_SLOTS), 0, 0, SCALAR_SLOTS)
+        by_vector = by_plane(
+            placed("by_vector", gathered_at + PACK * SCALAR_SLOTS, PACK * vector_slots), SCALAR_SLOTS, SCALAR_SLOTS, S
         )
         chunks[0].extend(((0, SCALAR_SLOTS, by_scalar), (SCALAR_SLOTS, S, by_vector)))
         for j in range(PACK):
@@ -257,7 +260,7 @@ def tile_moe_pre_lin_silu_kernel(tc, xT, w, b, gate, offs, pos1, pos2, out):
         nc.tensor.transpose(turned[:], gate_rows[:], identity[:])
         nc.vector.tensor_copy(gate_columns[:], turned[:, 0 : S // P])
         gate_banks = [psum.tile([P, GROUP], F32, name="bank%d" % group) for group in range(S // GROUP)]
-        for c in range(S // P):
+        for c in range(HELP_SECOND // P, S // P):
             group, place = divmod(c * P, GROUP)
             nc.tensor.transpose(
                 gate_banks[group][:, place : place + P], gate_columns[:, c : c + 1].to_broadcast([P, P]), identity[:]
@@ -277,21 +280,21 @@ def tile_moe_pre_lin_silu_kernel(tc, xT, w, b, gate, offs, pos1, pos2, out):
         multiply(0, SCALAR_SLOTS, 2 * CALL)
         multiply(0, HELP_FIRST, SCALAR_SLOTS)
         multiply(0, 2 * CALL, S)
-        early = range(EARLY)
-        for a, count, row, scale_column in (
+
+        for word, count, row, scale_column in (
             (0, CALL, 0, 0),
             (CALL, CALL, 0, CALL),
             (LOW, GROUP, 4, 0),
             (LOW + GROUP, GROUP, 4, CALL),
-            (THIRD + GROUP, GROUP, 4, GROUP),
+            (MIDDLE + GROUP, GROUP, 4, GROUP),
             (2 * CALL + GROUP, C, 4, CALL + GROUP),
-            (THIRD, GROUP, 8, 0),
+            (MIDDLE, GROUP, 8, 0),
             (2 * CALL, GROUP, 8, CALL),
         ):
-            quantize(0, (0, S), early, a, a + count, row, scale_column)
-        later = placed(
-            "later_chunks", raw_at + (EARLY - SINGLES) * W_RAW - PACK * (S - FIRST_CHUNK), PACK * (S - FIRST_CHUNK)
-        )
+            quantize(0, (0, S), range(EARLY), word, count, row, scale_column)
+
+        later_width = PACK * (S - FIRST_CHUNK)
+        later = placed("later_chunks", raw_at + (EARLY - SINGLES) * W_RAW - later_width, later_width)
         for lo, hi in CHUNKS[1:]:
             gather_chunk(later, FIRST_CHUNK, lo, hi)
 
@@ -300,46 +303,45 @@ def tile_moe_pre_lin_silu_kernel(tc, xT, w, b, gate, offs, pos1, pos2, out):
         multiply(1, HELP_SECOND, C)
         multiply(1, C, SECOND_END)
         banks = [psum.tile([P, GROUP], F32, name="bank%d" % group) for group in range(SECOND_END // GROUP)]
-        pair = psum.tile([P, GROUP], F32, name="spare0")
+        banks.append(psum.tile([P, GROUP], F32, name="spare0"))
         tenth = psum.tile([P, C], F32, name="spare1")
-        homes = [bank[:, place : place + C] for bank in banks + [pair] for place in (0, C)] + [tenth[:]]
-        for e in early:
+        homes = [bank[:, place : place + C] for bank in banks for place in (0, C)] + [tenth[:]]
+        for e in range(EARLY):
             matmul_pass(0, e * C, (e + 1) * C, homes[e], e % 2 == 0, False)
-        quantize(1, (0, 0), range(EARLY, E), LOW, THIRD, 0, 2 * CALL)
-        quantize(1, (0, C), range(EARLY, E), THIRD, THIRD + GROUP, 0, 3 * CALL)
-        for a, count, row, scale_column in (
+
+        quantize(1, (0, C), range(EARLY, E), LOW, CALL, 0, 2 * CALL)
+        quantize(1, (0, C), range(EARLY, E), MIDDLE, GROUP, 0, 3 * CALL)
+        for word, count, row, scale_column in (
             (0, C, 4, 2 * CALL),
             (C, GROUP, 4, 3 * CALL),
-            (3 * C, GROUP, 8, 2 * CALL),
-            (5 * C, GROUP, 8, 3 * CALL),
+            (END_WORD, GROUP, 8, 2 * CALL),
+            (END_WORD + GROUP, GROUP, 8, 3 * CALL),
         ):
-            quantize(1, (C, SECOND_END), (), a, a + count, row, scale_column)
+            quantize(1, (C, SECOND_END), (), word, count, row, scale_column)
         for e in range(EARLY, E - 1):
             matmul_pass(0, e * C, (e + 1) * C, homes[e], e % 2 == 0, False)
         for e in range(SECOND_END // C):
             matmul_pass(1, e * C, (e + 1) * C, homes[e], False, e % 2 == 1)
-        summed = [(e * C, (e + 1) * C, homes[e]) for e in range(SECOND_END // C)]
 
         help_multiply(1, THIRD_FROM, HELP_THIRD)
         multiply(1, SECOND_END, THIRD_FROM)
         multiply(1, THIRD_FROM + HELP_THIRD, 10 * C)
-        for place in (0, C):
-            quantize(1, (SECOND_END, 10 * C), (), 3 * C + place, 4 * C + place, 0, 3 * CALL + GROUP + place)
-            matmul_pass(1, SECOND_END + place, SECOND_END + place + C, pair[:, place : place + C], False, place == C)
-        summed.extend((SECOND_END + place, SECOND_END + place + C, pair[:, place : place + C]) for place in (0, C))
+        for e in (8, 9):
+            lo = e * C
+            quantize(1, (lo, lo + C), (), word_of(1, lo), C, 0, 3 * CALL + GROUP + lo - SECOND_END)
+            matmul_pass(1, lo, lo + C, homes[e], False, e % 2 == 1)
 
         help_multiply(1, S - H, H)
         multiply(1, 10 * C, 11 * C)
         multiply(1, 11 * C, S - H)
         y = placed("y", second_planes + 2 * T, S)
-        for lo, hi, sums in summed:
-            activate(lo, hi, sums)
+        for e in range(10):
+            activate(e * C, (e + 1) * C, homes[e])
         halves = [psum.tile([P, H], F32, name="bank%d" % group) for group in (4, 5)]
         for index in range(2):
             matmul_pass(0, 11 * C + index * H, 11 * C + (index + 1) * H, halves[index][:], True, False)
         for lo, hi, sums in ((10 * C, 11 * C, tenth), (11 * C, S - H, halves[0]), (S - H, S, halves[1])):
-            a = word_of(1, lo)
-            quantize(1, (lo, hi), (), a, a + hi - lo, 0, 4 * CALL + lo - 10 * C)
+            quantize(1, (lo, hi), (), word_of(1, lo), hi - lo, 0, 4 * CALL + lo - 10 * C)
             matmul_pass(1, lo, hi, sums[:], False, True)
             activate(lo, hi, sums[:])
 

from contextlib import ExitStack

import concourse.mybir as mybir
from concourse.masks import make_identity

K, T, E, C, N = 1024, 1536, 12, 256, 128
S = E * C
FLOPS = 2 * K * N * S
BYTES = 4 * (K * T + E * K * N + N * E + S + N * T) + 2 * 128 * (S + 2 * T) // 16

F32 = mybir.dt.float32
BF16 = mybir.dt.bfloat16
U32 = mybir.dt.uint32
U16 = mybir.dt.uint16
U8 = mybir.dt.uint8
FP8X4 = mybir.dt.float8_e4m3fn_x4
MULT = mybir.AluOpType.mult
ADD = mybir.AluOpType.add
COPY = mybir.ActivationFunctionType.Copy
SILU = mybir.ActivationFunctionType.Silu

P = 128
PACK = 4
PASSES = K // (P * PACK)
PER_COLUMN = 16
RUN = 2
LINE = 4
W_WORDS = PASSES * N
W_RAW = PACK * W_WORDS
GROUP = 512
CALL = 1024
H = C // 2

EARLY = 7
SINGLES = 5
SCALAR_SLOTS = 1472
SPARE = max(SCALAR_SLOTS, S - SCALAR_SLOTS) + 2 * PER_COLUMN - T
HELP_FIRST = 896
HELP_SECOND = 160
HELP_THIRD = 128
THIRD_FROM = 9 * C - HELP_THIRD // 2
FIRST_CHUNK = 1216
SECOND_END = 8 * C
CHUNKS = (
    (0, FIRST_CHUNK),
    (FIRST_CHUNK, 6 * C + H),
    (6 * C + H, SECOND_END),
    (SECOND_END, 10 * C + H),
    (10 * C + H, S),
)
TOKEN_PIECES = (192, 256, 384, 320, 192, 192)
OWN_PIECE = 1

EARLY_WORDS = EARLY * W_WORDS
STAGED = EARLY_WORDS + S
LOW = EARLY_WORDS + CALL
MIDDLE = LOW + CALL
END_WORD = 3 * C


def word_of(g, slot):
    if g == 0:
        return LOW + slot if slot < 2 * CALL else EARLY_WORDS + slot - 2 * CALL
    if slot < C:
        return MIDDLE + C + slot
    if slot < SECOND_END:
        return slot - C
    if slot < 10 * C:
        return END_WORD + slot - SECOND_END
    if slot < S - H:
        return END_WORD + H + slot - 10 * C
    return END_WORD + slot - (S - H)


def weight_word(e):
    if e >= EARLY:
        return LOW + (e - EARLY) * W_WORDS
    if e >= SINGLES:
        return CALL + (e - SINGLES - 1) * W_WORDS
    return e * W_WORDS if (e + 1) * W_WORDS < CALL else (e + EARLY - SINGLES) * W_WORDS


def tile_moe_pre_lin_silu_kernel(tc, xT, w, b, gate, offs, pos1, pos2, out):
    nc = tc.nc
    with ExitStack() as ctx:
        keep = ctx.enter_context(tc.tile_pool(name="keep", bufs=1))
        shared = ctx.enter_context(tc.tile_pool(name="shared", bufs=1))
        psum = ctx.enter_context(tc.psum_pool(name="psum", bufs=1))

        offs_sb = keep.tile([P, S // PER_COLUMN], U16, name="offs_sb")
        pos1_sb = keep.tile([P, T // PER_COLUMN], U16, name="pos1_sb")
        pos2_sb = keep.tile([P, T // PER_COLUMN], U16, name="pos2_sb")
        bias = keep.tile([P, E], F32, name="bias")
        identity = keep.tile([P, P], F32, name="identity")
        gate_rows = keep.tile([P, P], F32, name="gate_rows")
        gate_columns = keep.tile([P, S // P], F32, name="gate_columns")
        staging = keep.tile([P, STAGED * PACK], BF16, name="staging", align_bytes=64)
        codes = keep.tile([P, PASSES * S + E * W_WORDS], U32, name="codes", align_bytes=64)
        scales = keep.tile([P, 4 * CALL + GROUP], U8, name="scales", align_bytes=64)

        wide = T + SPARE
        second_planes = PACK * wide
        gathered_at = second_planes + PACK * T
        raw_at = gathered_at + PACK * S

        def placed(name, column, width):
            return shared.tile([P, width], F32, name=name, offset=4 * column)

        planes = [
            [placed("plane0%d" % j, j * wide, wide) for j in range(PACK)],
            [placed("plane1%d" % j, second_planes + j * T, T) for j in range(PACK)],
        ]
        x_view = xT.rearrange("(g p j) t -> g j p t", g=PASSES, j=PACK)
        w_view = w.rearrange("e (g p j) n -> p (e g) (j n)", g=PASSES, j=PACK)
        chunks = [[], []]
        helped_gate = {}
        raw = {}
        x_column, w_column = {}, {}
        next_column = [0]

        def staged(word, count):
            return staging[:, word * PACK : (word + count) * PACK]

        def load_plane(g, j):
            nc.sync.dma_start(planes[g][j][:, :T], x_view[g, j])

        def load_w(e, end):
            place = (e - SINGLES) % EARLY if e < EARLY else EARLY - SINGLES
            raw[e] = placed("raw%d" % e, raw_at + place * W_RAW, (end - e) * W_RAW)
            nc.sync.dma_start(
                raw[e][:].rearrange("p (h c) -> p h c", c=PACK * N), w_view[:, PASSES * e : PASSES * end, :]
            )

        def load_gate(lo, count):
            helped_gate[lo] = keep.tile([P, count], F32, name="gate%d" % lo)
            nc.sync.dma_start(helped_gate[lo][:], gate[0:P, lo : lo + count])

        def by_plane(tile, base, lo, hi):
            return tile[:, PACK * (lo - base) : PACK * (hi - base)].rearrange("p (j s) -> p j s", j=PACK)

        def tokens(g, j, lo, hi):
            return planes[g][j][:].indirect(offs_sb[:, lo // PER_COLUMN : hi // PER_COLUMN])

        def gather_chunk(tile, base, lo, hi):
            view = by_plane(tile, base, lo, hi)
            chunks[1].append((lo, hi, view))
            for j in range(PACK):
                nc.scalar.activation(view[:, j, :], tokens(1, j, lo, hi), COPY)

        def round_w(e, end):
            nc.gpsimd.tensor_copy(
                staged(weight_word(e), (end - e) * W_WORDS).rearrange(
                    "p (h c i j) -> p h c j i", c=N // LINE, i=LINE, j=PACK
                ),
                raw[e][:].rearrange("p (h j c i) -> p h c j i", c=N // LINE, i=LINE, j=PACK),
            )

        def help_multiply(g, lo, count):
            base, end, source = [chunk for chunk in chunks[g] if chunk[0] <= lo < chunk[1]][0]
            nc.gpsimd.tensor_tensor(
                staged(word_of(g, lo), count).rearrange("p (c i j) -> p c j i", i=LINE, j=PACK),
                source[:, :, lo - base : lo - base + count].rearrange("p j (c i) -> p c j i", i=LINE),
                helped_gate[lo][:, :count]
                .rearrange("p (c i) -> p c i", i=LINE)
                .unsqueeze(2)
                .to_broadcast([P, count // LINE, PACK, LINE]),
                MULT,
            )

        def multiply(g, lo, hi):
            for group in range(lo // GROUP, (hi - 1) // GROUP + 1):
                for base, end, source in chunks[g]:
                    a, z = max(lo, base, group * GROUP), min(hi, end, (group + 1) * GROUP)
                    if a < z:
                        nc.vector.tensor_tensor(
                            staged(word_of(g, a), z - a).rearrange("p (c i j) -> p c j i", i=RUN, j=PACK),
                            source[:, :, a - base : z - base].rearrange("p j (c i) -> p c j i", i=RUN),
                            gate_banks[group][:, a - group * GROUP : z - group * GROUP]
                            .rearrange("p (c i) -> p c i", i=RUN)
                            .unsqueeze(2)
                            .to_broadcast([P, (z - a) // RUN, PACK, RUN]),
                            MULT,
                        )

        def quantize(g, slots, experts, word, count, row, scale_column):
            column = next_column[0]
            next_column[0] = column + count
            for slot in range(slots[0], slots[1], H):
                shift = word_of(g, slot) - word
                if 0 <= shift < count:
                    x_column[g, slot] = (column + shift, row, scale_column + shift)
            for e in experts:
                shift = weight_word(e) - word
                if 0 <= shift < count:
                    w_column[e] = (column + shift, scale_column + shift)
            nc.vector.quantize_mx(
                out=codes[:, column : column + count].bitcast(FP8X4),
                scales=scales[row:, scale_column : scale_column + count],
                in_=staged(word, count),
            )

        def matmul_pass(g, lo, hi, sums, start, stop):
            left, left_scale = [column + g * N for column in w_column[lo // C]]
            right, row, right_scale = x_column[g, lo]
            nc.tensor.matmul_mx(
                out=sums,
                lhsT=codes[:, left : left + N].bitcast(FP8X4),
                lhsT_scale=scales[:, left_scale : left_scale + N],
                rhs=codes[:, right : right + hi - lo].bitcast(FP8X4),
                rhs_scale=scales[row:, right_scale : right_scale + hi - lo],
                start=start,
                stop=stop,
            )

        def activate(lo, hi, sums):
            nc.scalar.activation(y[:, lo:hi], sums, SILU, bias=bias[:, lo // C : lo // C + 1])

        warm_in = keep.tile([P, 1], F32, name="warm_in")
        warm_out = keep.tile([P, 1], F32, name="warm_out")
        nc.gpsimd.memset(warm_in[:], 0.0)
        nc.scalar.activation(warm_out[:], warm_in[:], SILU)

        nc.gpsimd.memset(gate_rows[:], 0.0)
        make_identity(nc, identity[:])
        for j in range(PACK):
            nc.vector.memset(planes[0][j][:, T:], 0.0)

        load_plane(0, 0)
        nc.sync.dma_start(offs_sb[:], offs)
        load_w(0, 1)
        load_plane(0, 1)
        nc.sync.dma_start(gate_rows[0 : S // P, :], gate[0, :].rearrange("(c s) -> c s", s=P))
        load_w(1, 2)
        load_w(2, 3)
        load_plane(0, 2)
        load_w(3, 4)
        load_plane(0, 3)
        load_w(4, 5)
        load_gate(0, HELP_FIRST)
        for j in range(PACK - 1):
            load_plane(1, j)
        load_w(SINGLES, EARLY)
        load_plane(1, PACK - 1)

        vector_slots = S - SCALAR_SLOTS
        by_scalar = by_plane(placed("by_scalar", gathered_at, PACK * SCALAR_SLOTS), 0, 0, SCALAR_SLOTS)
        by_vector = by_plane(
            placed("by_vector", gathered_at + PACK * SCALAR_SLOTS, PACK * vector_slots), SCALAR_SLOTS, SCALAR_SLOTS, S
        )
        chunks[0].extend(((0, SCALAR_SLOTS, by_scalar), (SCALAR_SLOTS, S, by_vector)))
        for j in range(PACK):
            cuts = (SCALAR_SLOTS, S) if j < PACK - 1 else (SCALAR_SLOTS, 2 * CALL, S)
            for lo, hi in zip(cuts, cuts[1:]):
                nc.vector.tensor_copy(by_vector[:, j, lo - SCALAR_SLOTS : hi - SCALAR_SLOTS], tokens(0, j, lo, hi))
            cuts = (0, SCALAR_SLOTS) if j < PACK - 1 else (0, HELP_FIRST, SCALAR_SLOTS)
            for lo, hi in zip(cuts, cuts[1:]):
                nc.scalar.activation(by_scalar[:, j, lo:hi], tokens(0, j, lo, hi), COPY)

        turned = psum.tile([P, P], F32, name="spare0")
        nc.tensor.transpose(turned[:], gate_rows[:], identity[:])
        nc.vector.tensor_copy(gate_columns[:], turned[:, 0 : S // P])
        gate_banks = [psum.tile([P, GROUP], F32, name="bank%d" % group) for group in range(S // GROUP)]
        for c in range(HELP_SECOND // P, S // P):
            group, place = divmod(c * P, GROUP)
            nc.tensor.transpose(
                gate_banks[group][:, place : place + P], gate_columns[:, c : c + 1].to_broadcast([P, P]), identity[:]
            )

        for e in range(SINGLES):
            round_w(e, e + 1)
        help_multiply(0, 0, HELP_FIRST)
        round_w(SINGLES, EARLY)
        load_w(EARLY, E)
        load_gate(THIRD_FROM, HELP_THIRD)
        load_gate(S - H, H)
        nc.sync.dma_start(bias[:], b)
        nc.sync.dma_start(pos1_sb[:], pos1)
        nc.sync.dma_start(pos2_sb[:], pos2)
        gather_chunk(placed("first_chunk", 0, PACK * FIRST_CHUNK), 0, *CHUNKS[0])
        multiply(0, SCALAR_SLOTS, 2 * CALL)
        multiply(0, HELP_FIRST, SCALAR_SLOTS)
        multiply(0, 2 * CALL, S)

        for word, count, row, scale_column in (
            (0, CALL, 0, 0),
            (CALL, CALL, 0, CALL),
            (LOW, GROUP, 4, 0),
            (LOW + GROUP, GROUP, 4, CALL),
            (MIDDLE + GROUP, GROUP, 4, GROUP),
            (2 * CALL + GROUP, C, 4, CALL + GROUP),
            (MIDDLE, GROUP, 8, 0),
            (2 * CALL, GROUP, 8, CALL),
        ):
            quantize(0, (0, S), range(EARLY), word, count, row, scale_column)

        later_width = PACK * (S - FIRST_CHUNK)
        later = placed("later_chunks", raw_at + (EARLY - SINGLES) * W_RAW - later_width, later_width)
        for lo, hi in CHUNKS[1:]:
            gather_chunk(later, FIRST_CHUNK, lo, hi)

        help_multiply(1, 0, HELP_SECOND)
        round_w(EARLY, E)
        multiply(1, HELP_SECOND, C)
        multiply(1, C, SECOND_END)
        banks = [psum.tile([P, GROUP], F32, name="bank%d" % group) for group in range(SECOND_END // GROUP)]
        banks.append(psum.tile([P, GROUP], F32, name="spare0"))
        tenth = psum.tile([P, C], F32, name="spare1")
        homes = [bank[:, place : place + C] for bank in banks for place in (0, C)] + [tenth[:]]
        for e in range(EARLY):
            matmul_pass(0, e * C, (e + 1) * C, homes[e], e % 2 == 0, False)

        quantize(1, (0, C), range(EARLY, E), LOW, CALL, 0, 2 * CALL)
        quantize(1, (0, C), range(EARLY, E), MIDDLE, GROUP, 0, 3 * CALL)
        for word, count, row, scale_column in (
            (0, C, 4, 2 * CALL),
            (C, GROUP, 4, 3 * CALL),
            (END_WORD, GROUP, 8, 2 * CALL),
            (END_WORD + GROUP, GROUP, 8, 3 * CALL),
        ):
            quantize(1, (C, SECOND_END), (), word, count, row, scale_column)
        for e in range(EARLY, E - 1):
            matmul_pass(0, e * C, (e + 1) * C, homes[e], e % 2 == 0, False)
        for e in range(SECOND_END // C):
            matmul_pass(1, e * C, (e + 1) * C, homes[e], False, e % 2 == 1)

        help_multiply(1, THIRD_FROM, HELP_THIRD)
        multiply(1, SECOND_END, THIRD_FROM)
        multiply(1, THIRD_FROM + HELP_THIRD, 10 * C)
        for e in (8, 9):
            lo = e * C
            quantize(1, (lo, lo + C), (), word_of(1, lo), C, 0, 3 * CALL + GROUP + lo - SECOND_END)
            matmul_pass(1, lo, lo + C, homes[e], False, e % 2 == 1)

        help_multiply(1, S - H, H)
        multiply(1, 10 * C, 11 * C)
        multiply(1, 11 * C, S - H)
        y = placed("y", second_planes + 2 * T, S)
        for e in range(10):
            activate(e * C, (e + 1) * C, homes[e])
        halves = [psum.tile([P, H], F32, name="bank%d" % group) for group in (4, 5)]
        for index in range(2):
            matmul_pass(0, 11 * C + index * H, 11 * C + (index + 1) * H, halves[index][:], True, False)
        for lo, hi, sums in ((10 * C, 11 * C, tenth), (11 * C, S - H, halves[0]), (S - H, S, halves[1])):
            quantize(1, (lo, hi), (), word_of(1, lo), hi - lo, 0, 4 * CALL + lo - 10 * C)
            matmul_pass(1, lo, hi, sums[:], False, True)
            activate(lo, hi, sums[:])

        first = placed("first", second_planes, T)
        total = placed("total", second_planes + T, T)

        def results(places, lo, hi):
            return y[:].indirect(places[:, lo // PER_COLUMN : hi // PER_COLUMN])

        ends = [sum(TOKEN_PIECES[: index + 1]) for index in range(len(TOKEN_PIECES))]
        pieces = list(zip([0] + ends, ends))
        for index, (lo, hi) in enumerate(pieces):
            if index == OWN_PIECE:
                nc.vector.tensor_copy(first[:, lo:hi], results(pos1_sb, lo, hi))
            else:
                nc.scalar.activation(first[:, lo:hi], results(pos1_sb, lo, hi), COPY)
        second = placed("second", 0, TOKEN_PIECES[-1])
        nc.scalar.activation(second[:], results(pos2_sb, *pieces[-1]), COPY)
        stored = 0
        for index, (lo, hi) in enumerate(pieces):
            other = second[:] if hi == T else results(pos2_sb, lo, hi)
            nc.vector.tensor_tensor(total[:, lo:hi], other, first[:, lo:hi], ADD)
            if index >= OWN_PIECE:
                nc.sync.dma_start(out[:, stored:hi], total[:, stored:hi])
                stored = hi
